import numpy as np, ml_dtypes
CORES = [16,18,20,22]
N = 4
BF = ml_dtypes.bfloat16
def gentries(a):
    return np.ascontiguousarray(a.reshape(8, 16, -1).transpose(0, 2, 1)).reshape(8, -1)
def gtable(e):
    e = np.asarray(e); return np.ascontiguousarray(e.reshape(8, -1, 16).transpose(0, 2, 1)).reshape(128, -1).astype(np.int32)
V, B, K, PH, CAP, R, ZP, M = 1024, 256, 16, 4, 48, 6, 2048, 512
NC, TH = N * CAP, 2047
def parts(rng):
    c = rng.integers(0, 256, (N, 8, 16, V)); low = rng.random((N, 8, 1, V)) < 0.125; c = np.where(low, rng.integers(0, 41, c.shape), c)
    z = rng.integers(0, 256, (N, 8, 16, ZP)); hi = np.argsort(rng.random((N, 8, ZP)), axis=-1)[..., :ZP // 4]
    mark = np.zeros((N, 8, ZP), bool); np.put_along_axis(mark, hi, True, 2); z = np.where(mark[:, :, None], rng.integers(200, 256, z.shape), z)
    e = rng.integers(0, ZP, (N, 8, K, V)); far = np.take_along_axis(hi, rng.integers(0, ZP // 4, (N, 8, K * V)), 2).reshape(N, 8, K, V)
    e = np.where(low & (rng.random((N, 8, 1, V)) < 0.5), far, e)
    p = np.argsort(rng.random((8, K, N * V)), axis=-1)
    share = rng.choice(np.array([0.3, 0.5, 0.75, 1.0]), (N, 8, 1, 1))
    j = np.where(rng.random((N, 8, 1, M)) < share, rng.integers(0, 256, (N, 8, 16, M)), rng.integers(0, 7, (N, 8, 16, M)))
    x = np.clip(c + rng.integers(-6, 7, c.shape), 0, 255)
    return c, z, e, p, j, x
def order(a):
    s = a.shape[:-2]; return np.ascontiguousarray(np.swapaxes(a.reshape(s + (K, PH, B)), -3, -2)).reshape(s + (K * V,))
def small(a):
    return np.ascontiguousarray(a.reshape(N, 128, -1)).astype(np.float32).astype(BF)
def pack(c, z, e, p, j, x):
    n = order(np.ascontiguousarray(p.reshape(8, K, N, V).transpose(2, 0, 1, 3)))
    return {"cen": small(c), "pl": small(z), "ent": order(e).astype(np.int32), "nb": np.stack([gtable(a) for a in n]), "jmp": small(j), "wk": small(x)}
def even(c, j):
    c[:, :, 0] = c[:, :, 0] ^ (np.add.reduce(c, axis=2) & 1); j[..., 0::2] = 0
def steer(rng, c, p, x, cnt, face, last=None):
    x[..., :B] = c[..., :B]
    for g in range(8):
        al = c[:, g].transpose(1, 0, 2).reshape(16, N * V); P = np.full(N * V, -1); pos = {}
        for q in range(N):
            i = rng.permutation(B); at = 0
            if last is not None and last[g, q] >= 0:
                m = int(np.add.reduce(cnt[g, q, :int(last[g, q]) + 1])) - 1; i[i == B - 1] = i[m]; i[m] = B - 1
            for o in range(N):
                n = int(cnt[g, q, o]); pos[q, o] = q * V + i[at:at + n]; at += n
            s = pos[q, q]
            if len(s): P[s] = np.roll(s, 1) if len(s) > 1 else q * V + (s - q * V + 1) % V
        for o in range(N):
            left = rng.permutation(np.setdiff1d(np.arange(o * V, (o + 1) * V), P)); at = 0
            for q in range(N):
                if q != o:
                    s = pos[q, o]; P[s] = left[at:at + len(s)]; at += len(s)
        go = np.nonzero(P >= 0)[0]; r = go // V
        x[r, g, :, go - r * V] = al[:, P[go]].T
        P[P < 0] = rng.permutation(np.setdiff1d(np.arange(N * V), P)); p[g, face[g]] = P
def plant(P, at, val):
    i = int(np.argmax(P == val)); P[i] = P[at]; P[at] = val
def setup_inputs(rng):
    return pack(*parts(rng))
def setup_inputs_corners(rng):
    c, z, e, p, j, x = parts(rng); even(c, j); cnt = np.zeros((8, N, N), np.int64); many = B // 2
    face = rng.integers(0, K, 8); face[0] = K - 1; face[7] = 0
    for g in range(8):
        room = [V] * N
        for q in range(N):
            left = B
            for h in [1] + [int(a) for a in rng.permutation(N) if a != 1]:
                o = (q + h) % N; n = int(rng.choice(np.array([0, 1, CAP - 1, CAP, CAP + 1, many])))
                if q == 0 and h == 1: n = (CAP, CAP + 1, many, CAP - 1, 1, 0, CAP, CAP)[g]
                n = min(n, left, room[o]); cnt[g, q, o] = n; left -= n; room[o] -= n
    steer(rng, c, p, x, cnt, face)
    for g in (1, 5): p[g, (face[g] + 1) % K] = np.arange(N * V)
    m = rng.random((N, 4, 1, V)) < 0.5
    e[:, ::2] = np.where(m, rng.choice(np.array([0, NC - 1, NC, R * NC - 1, R * NC, ZP - 1]), (N, 4, K, V)), e[:, ::2])
    return pack(c, z, e, p, j, x)
def setup_inputs_crowd(rng):
    c, z, e, p, j, x = parts(rng); even(c, j); cnt = np.zeros((8, N, N), np.int64); face = rng.integers(0, K, 8); last = np.full((8, N), -1)
    for g in range(8):
        for q in range(N):
            n = int(rng.choice(np.array([B, B - 1, B // 2, 0])))
            if q == 0: n = B
            if q == 1: n = B - 1 if g == 0 else B
            if q == 2 and g % 2 == 1: n = min(n, B // 2)
            cnt[g, q, (q + g) % N] = n
        if g % 2 == 1:
            n = int(rng.choice(np.array([1, CAP]))); o = (g + 2) % N
            if g == 7: n = CAP
            cnt[g, 0, g % N] -= n; cnt[g, 0, o] += n; last[g, 0] = o
    steer(rng, c, p, x, cnt, face, last)
    return pack(c, z, e, p, j, x)
def setup_inputs_ties(rng):
    c, z, e, p, j, x = parts(rng)
    c = rng.integers(0, 9, c.shape); z = rng.integers(0, 9, z.shape); j = rng.integers(0, 9, j.shape); x = rng.integers(0, 9, x.shape)
    c[:, ::2, :, 1::2] = c[:, ::2, :, 0::2]
    z[:, 3] = rng.integers(128, 136, z[:, 3].shape); z[:, 5] = rng.integers(248, 256, z[:, 5].shape)
    e = np.where(rng.random((N, 8, 1, V)) < 0.6, rng.integers(0, ZP, (N, 8, 1, V)), rng.integers(0, ZP, (N, 8, K, V)))
    i = np.concatenate([np.array([0, B - 1]), 1 + rng.permutation(B - 2)[:6]])
    c[..., i] = 8; x[..., i] = 2; j[..., 0] = 0; z[..., ZP - 2:] = 8; z[:, :, 15, ZP - 2] = 7
    e[:, :, :K // 2, i] = ZP - 1; e[:, :, K // 2:, i] = ZP - 2
    return pack(c, z, e, p, j, x)
def setup_inputs_spread(rng):
    c, z, e, p, j, x = parts(rng)
    c, z, j, x = [(np.exp2(8 * rng.random((N, 8, 1, n))) * rng.random((N, 8, 16, n))).astype(np.int64) for n in (V, ZP, M, V)]
    e = np.minimum((ZP * rng.random(e.shape) ** 3).astype(np.int64), ZP - 1)
    return pack(c, z, e, p, j, x)
def setup_inputs_ends(rng):
    p = np.argsort(rng.random((8, K, N * V)), axis=-1)
    c, z, j, x = [255 * (rng.random((N, 8, 16, n)) < rng.choice(np.array([0.0, 0.1, 0.5, 0.9, 1.0]), (N, 8, 1, n))).astype(np.int64) for n in (V, ZP, M, V)]
    e = (ZP - 1) * rng.integers(0, 2, (N, 8, K, V))
    z[..., 0] = 255; z[..., ZP - 1] = 0; j[..., 65280 & (M - 1)] = 0
    for a, b in ((0, 1), (V - 1, V - 2)):
        c[..., a] = 0; c[..., b] = 255; x[..., a] = 255; e[..., a] = ZP - 1
    for a in (2, B - 3):
        c[..., a] = 0; x[..., a] = 255
    for g in range(8):
        for k in range(K):
            for a in range(N):
                o = ((a + 1) % N) * V; near = (g + k) % 2 == 0
                plant(p[g, k], a * V, o + (1 if near else 0)); plant(p[g, k], a * V + V - 1, o + (V - 2 if near else V - 1))
                plant(p[g, k], a * V + 2, o + 2); plant(p[g, k], a * V + B - 3, o + B - 3)
    u = rng.random((N, 1, V)); nz = np.where(u < 0.5, 8, np.where(u < 0.95, 7, 0))
    c[:, 6] = np.where(np.arange(16)[None, :, None] < nz, 0, 255); z[:, 6] = 255; x[:, 6] = 255; j[:, 6] = 0; e[:, 6] = ZP - 1
    return pack(c, z, e, p, j, x)
def check_inputs(d):
    bad = []
    for k, hi in (("cen", 255), ("pl", 255), ("jmp", 255), ("wk", 255), ("ent", ZP - 1), ("nb", N * V - 1)):
        v = np.asarray(d[k]).astype(np.float32)
        if not np.all((v >= 0) & (v <= hi) & (v == np.floor(v))): bad.append("range of " + k)
    a = np.stack([gentries(q) for q in d["nb"]]).reshape(N, 8, PH, K, B).transpose(1, 3, 0, 2, 4).reshape(8, K, N * V)
    if np.any(np.sort(a, axis=-1) != np.arange(N * V)): bad.append("neighbours k of all boxes all different")
    return bad
def reference(cen, pl, ent, nb, jmp, wk):
    C, Z, D, X = [a.astype(np.float32).astype(np.int32).reshape(N, 8, 16, -1) for a in (cen, pl, jmp, wk)]
    E = ent.astype(np.int32).reshape(N, 8, PH, K, B); F = np.ones((N, 8, PH, K, B), np.int32)
    L = np.stack([gentries(a) for a in nb]).reshape(N, 8, PH, K, B); A = [0] * N
    w = (2 * np.arange(16, dtype=np.int32) + 1)[None, None, :, None]
    for t in range(R):
        b = t % PH; lo, hi = b * B, b * B + B
        x = X[..., lo:hi]; ix = np.add.reduce(w * x, axis=2) & (M - 1)
        y = np.abs(x - np.take_along_axis(D, ix[:, :, None, :], 3))
        al = np.ascontiguousarray(C.transpose(1, 2, 0, 3)).reshape(8, 16, N * V)
        outs = []
        for q in range(N):
            c = C[q, :, :, lo:hi].astype(np.int32); yq = y[q]; n = L[q, :, b]
            v = np.take_along_axis(al, n.reshape(8, 1, K * B), 2).reshape(8, 16, K, B)
            d = np.add.reduce(np.abs(v - yq[:, :, None, :]), axis=1)
            k = np.argmin(d, axis=1); own = np.add.reduce(np.abs(c - yq), axis=1)
            go = np.min(d, axis=1) + (A[q] & 63) < own
            s = np.take_along_axis(Z[q], E[q, :, b].reshape(8, 1, K * B), 2).reshape(8, 16, K, B)
            h = np.add.reduce(np.abs(s - c[:, :, None, :]), axis=1)
            P = np.add.accumulate(F[q, :, b] * np.maximum(TH - h, 0), axis=1)
            u = np.add.reduce(yq, axis=1) & 63
            ok = 64 * P > (u * P[:, K - 1])[:, None, :]
            first = np.argmax(ok, axis=1)
            z = np.take_along_axis(s, first[:, None, None, :], 2)[:, :, 0]
            z = np.where(np.any(ok, axis=1)[:, None, :], z, c)
            new = np.where(go[:, None, :], z, yq)
            X[q, :, :, lo:hi] = new; C[q, :, :, lo:hi] = c + np.clip(new - c, -1, 1)
            A[q] = int(np.count_nonzero(go))
            outs.append((go, np.take_along_axis(n, k[:, None, :], 1)[:, 0], k))
        land = np.zeros((N, 8, 16, NC), np.int32)
        for q in range(N):
            go, to, k = outs[q]
            for o in range(N):
                hit = go & (to // V == o); at = np.add.accumulate(hit.astype(np.int64), axis=1) - 1
                g, i = np.nonzero(hit & (at < CAP)); s = q * CAP + at[g, i]
                land[o][g, :, s] = y[q][g, :, i]
                v = to[g, i] - o * V; bl = v // B; row = k[g, i] ^ 1
                E[o][g, bl, row, v - bl * B] = NC * t + s
                F[o][g, bl, row, v - bl * B] += 1
        Z[..., NC * t:NC * t + NC] = land
    return {"yc": C.reshape(N, 128, V).astype(np.float32).astype(BF), "yx": X.reshape(N, 128, V).astype(np.float32).astype(BF), "yz": Z.reshape(N, 128, ZP).astype(np.float32).astype(BF),
            "ye": E.reshape(N, 8, K * V).astype(np.float32), "yn": F.reshape(N, 8, K * V).astype(np.float32).astype(BF)}

@@ -1,0 +1,695 @@
+import numpy as np
+from concourse.bass import DstId, RemoteDMATransfer
+from concourse.mybir import AluOpType as ALU, ActivationFunctionType as ACT
+
+N, V, B, K, CAP, R, ZP, M = 4, 1024, 256, 16, 48, 6, 2048, 512
+NC = N * CAP
+WW = K * V + NC
+XW_ = 592
+MAGIC = 3221225472.0
+CFG = {"nj": [0, 0, 1, 0, 1, 1], "cut": [0, 64, 128, 256], "pool": 7, "look": 1.0,
+       "lead": {'L': 41.3, 'N0': 2.5, 'N1': -1.3, 'N2': 2.6, 'N3': 1.1, 'N4': 3.8, 'N5': 1.7, 'T0': 3.2, 'T1': 15.4, 'T2': 2.0,
+                'T3': 1.9, 'T4': 21.2, 'T5': 0.4, 'A0': -4.7, 'A1': 20.6, 'A2': -4.3, 'A3': -4.6, 'A4': -7.0, 'A5': 0.6,
+                'P0': -3.6, 'P1': -0.1, 'P2': -2.1, 'P3': -1.8, 'P4': -4.7, 'P5': -1.5, 'Q0': 16.0, 'Q1': 45.2, 'Q2': 6.8,
+                'Q3': -7.8, 'Q4': -6.0, 'Q5': 2.2, 'W0': -10.7, 'W1': 1.7, 'W2': 8.0, 'W3': -2.2, 'W4': 11.3},
+       "f": 1.25, "g": 1.56, "s": 3.8, "pe": 0.42, "dma": 1800.0, "rem": 2000.0, "row": 40.0, "bw": 20.0,
+       "wake": 70.0, "fix": 50.0}
+
+f32, bf, i32, u16 = "float32", "bfloat16", "int32", "uint16"
+SCRATCH = {}
+for _n, _w, _d in [
+    ("W", WW, bf), ("WF", WW, f32), ("CT", N * V, bf), ("PL", ZP, bf), ("JM", M, bf), ("XS", V, bf), ("Y", R * B, bf),
+    ("YF", B, f32), ("AN", 17 * B, bf), ("MN", 17 * B, bf), ("AP0", 18 * B, bf), ("AP1", 18 * B, bf), ("MP", 16 * B, bf),
+    ("NBI", V, i32), ("NBU", V, u16), ("TC", V, f32), ("KO2", V, bf), ("A8", B, bf), ("NBF", B, f32),
+    ("EI", V, i32), ("EF", V, f32), ("EH", V, bf), ("EL", V, bf), ("EU", B, u16), ("NN", B, bf),
+    ("XB0", XW_, f32), ("XB1", XW_, f32), ("XB2", XW_, f32), ("XB3", XW_, f32), ("XB4", XW_, f32), ("XB5", XW_, f32),
+    ("PI", 4, i32), ("PJ", 4, i32), ("COL", 16, f32), ("REP", 4, u16), ("X143", 144, f32), ("XG", 128, f32), ("J16", B, f32),
+    ("DM", 144, bf), ("DA", 144, bf), ("DE", 144, bf), ("DW", 144, bf), ("DC", 144, bf), ("DP", 144, bf), ("DN", 144, bf),
+    ("D1", 144, bf), ("ID", 128, bf), ("IDM", 128, bf), ("IDF", 128, f32), ("IDFM", 128, f32), ("ID8", 128, bf),
+    ("ID10", 128, bf), ("ID64", 128, bf), ("ONE", 128, bf), ("BO", 128, bf), ("BOM", 128, bf), ("BOF", 128, f32),
+    ("BOS", 128, f32), ("B64", 128, f32), ("TRI", 128, f32), ("LB", 128, bf), ("LM", 128, bf),
+    ("DIAG", B, f32), ("SEG", NC, f32), ("KO1", B, bf), ("K1", B, bf), ("OC", 64, f32), ("C16", 16, f32),
+    ("IB", 16, bf), ("I17", 16, f32), ("DUM", 16, f32), ("NDI", 64, f32), ("NDC", 64, bf), ("THR", 64, f32),
+    ("TPI", NC, f32), ("PB", NC, f32), ("PW", NC, bf), ("BI", 8, f32), ("BC", 8, f32),
+    ("HI", 48, i32), ("HU", 48, u16), ("DF", 768, bf), ("UF", B, bf), ("U", B, f32),
+    ("ACC", 64, f32), ("A32", 32, f32), ("KEY", 16, f32), ("TH", 16, f32), ("GO", 16, bf), ("BP", 16, f32),
+    ("KG", 16, i32), ("CODE", 16, i32), ("L1", 16, i32), ("L1U", 16, u16), ("H", 64, bf), ("S", 64, bf),
+    ("VV", 64, f32), ("Q", 64, f32), ("QA", 32, f32), ("QB", 16, f32), ("QC", 16, f32), ("PY", 16, u16),
+    ("X", B, f32), ("AG", 1, bf), ("AM", 1, f32),
+    ("G", B, f32), ("UT", B, f32), ("NO", B, bf), ("IX", 16, f32), ("IXU", 16, u16), ("CM", B, bf), ("CN", B, bf),
+    ("HX", NC, f32), ("MM", NC, f32), ("MS", NC, f32), ("MU0", 12, u16), ("MU1", 12, u16), ("TW", NC, bf),
+]:
+    SCRATCH[_n] = ("sbuf", [128, _w], _d)
+BANKS = ("K0", "KB1", "HB", "YB", "CB", "TB", "M1", "M2")
+for _n in BANKS:
+    SCRATCH[_n] = ("psum", [128, 512], f32)
+SEMAPHORES = ["qv", "qa", "qp", "qg"] + ["d%d" % i for i in range(90)] + ["ax%d" % t for t in range(R)] + \
+    ["ac%d" % t for t in range(R)] + ["lx%d" % t for t in range(R)] + ["lc%d" % t for t in range(R)] + \
+    ["af%d" % t for t in range(R - 1)] + ["lf%d" % t for t in range(R - 1)]
+
+
+def arrange(ops):
+    n = len(ops)
+    last, readers, pred = {}, {}, []
+    for i, (q, fn, rd, wr, own, c) in enumerate(ops):
+        need = set()
+        for t in rd:
+            if t in last:
+                need.add(last[t])
+            if t in BANKS:
+                need.update(x for x in readers.get(t, []) if ops[x][0] != q)
+        for t in wr:
+            if t in last:
+                need.add(last[t])
+            need.update(readers.get(t, []))
+        if fn is None:
+            need.add(i - 1)
+        pred.append(sorted(need))
+        for t in rd:
+            readers.setdefault(t, []).append(i)
+        for t in wr:
+            last[t] = i
+            readers[t] = []
+    succ = [[] for _ in range(n)]
+    for i in range(n):
+        for j in pred[i]:
+            succ[j].append(i)
+    hold = [o[5][0] for o in ops]
+    wake = CFG["wake"]
+    level = [0.0] * n
+    for i in range(n - 1, -1, -1):
+        level[i] = sum(ops[i][5][:3]) + max([level[j] + wake for j in succ[i]] + [0.0])
+    level = [level[i] + 1000.0 * ops[i][5][3] for i in range(n)]
+    left = [len(x) for x in pred]
+    est = [0.0] * n
+    ready = {q: [] for q in "vapsgx"}
+    free = {q: 0.0 for q in "vapsgx"}
+    engines = 0.0
+    for i in range(n):
+        if not left[i]:
+            ready[ops[i][0]].append(i)
+    order = []
+    while len(order) < n:
+        pick = None
+        for q, lst in ready.items():
+            if not lst:
+                continue
+            t0 = max(free[q], min(est[i] for i in lst))
+            c = max((i for i in lst if est[i] <= t0), key=lambda i: level[i])
+            soon = [i for i in lst if t0 < est[i] < t0 + hold[c] and
+                    level[i] - level[c] > CFG["look"] * hold[c] and est[i] - t0 < t0 + hold[c] - est[i]]
+            if soon:
+                c = max(soon, key=lambda i: level[i])
+            st = max(t0, est[c])
+            if pick is None or st < pick[0]:
+                pick = (st, q, c)
+        st, q, c = pick
+        ready[q].remove(c)
+        order.append(c)
+        free[q] = st + hold[c]
+        if ops[c][5][2]:
+            engines = max(engines, st + ops[c][5][1]) + ops[c][5][2]
+            end = engines
+        else:
+            end = st + max(hold[c], ops[c][5][1])
+        for j in succ[c]:
+            est[j] = max(est[j], end + (0.0 if (q == "p" and ops[j][0] == "p") or ops[j][1] is None else wake))
+            left[j] -= 1
+            if not left[j]:
+                ready[ops[j][0]].append(j)
+    return [ops[i] for i in order]
+
+
+def build(g, T, ops):
+    queues = {"v": g.vector, "a": g.scalar, "p": g.tensor, "s": g.sync, "g": g}
+    last, readers = {}, {}
+    known = {q: {} for q in "vapsgx"}
+    clock, waits, used = {}, [], set()
+    seq = {q: 0 for q in queues}
+    totals = {}
+    for n, (q, fn, rd, wr, own, cost) in enumerate(ops):
+        if own is None:
+            seq[q] += 1
+            tok = ("q" + q, seq[q])
+        else:
+            tok = own
+            totals[own[0]] = max(totals.get(own[0], 0), own[1])
+        need = []
+        for t in rd:
+            if t in last:
+                need.append(last[t])
+            if t in BANKS:
+                need.extend(x for x in readers.get(t, []) if x[0] != "q" + q)
+        for t in wr:
+            if t in last:
+                need.append(last[t])
+            need.extend(readers.get(t, []))
+        mine = []
+        if fn is not None:
+            kn = known[q]
+            for (s, c) in sorted(set(need), key=lambda x: -x[1]):
+                if (q == "p" and s == "qp") or kn.get(s, 0) >= c:
+                    continue
+                mine.append((s, c))
+                used.add((s, c))
+                kn[s] = c
+                for s2, c2 in clock.get((s, c), {}).items():
+                    if kn.get(s2, 0) < c2:
+                        kn[s2] = c2
+            clock[tok] = dict(kn)
+        waits.append((tok, mine))
+        for t in rd:
+            readers.setdefault(t, []).append(tok)
+        for t in wr:
+            last[t] = tok
+            readers[t] = []
+    count = {}
+    for s in ("qv", "qa", "qp", "qg"):
+        for k, x in enumerate(sorted(c for (s2, c) in used if s2 == s)):
+            count[(s, x)] = k + 1
+    for n, (q, fn, rd, wr, own, cost) in enumerate(ops):
+        if fn is None:
+            continue
+        tok, mine = waits[n]
+        for w in mine:
+            queues[q].wait_ge(T.sem[w[0]], count.get(w, w[1]))
+        for f in fn:
+            ins = f()
+            if own is not None and own[0][0] == "d":
+                ins.then_inc(T.sem[own[0]], 16)
+        if own is None and tok in count:
+            ins.then_inc(T.sem[tok[0]], 1)
+    for s, c in totals.items():
+        g.sync.wait_ge(T.sem[s], c)
+
+
+def rank_program(g, core, T, topo):
+    me = T.rank_of(core)
+    if me is None:
+        return
+    kinds = {f32: "f4", i32: "i4", bf: "i2", u16: "u2"}
+    shapes = [(n, "f8" if w == "psum" else kinds[d], tuple(sh)) for n, (w, sh, d) in SCRATCH.items()]
+    shapes += [(n, "i2", tuple(T[n].shape)) for n in ("cen", "pl", "jmp", "wk", "yc", "yx", "yz", "yn")]
+    shapes += [(n, "i4", tuple(T[n].shape)) for n in ("ent", "nb", "ye")]
+    sizes = calls(g, core, me, np.recarray((1,), shapes)[0], T, topo, False)
+    ops = calls(g, core, me, T, T, topo, True)
+    build(g, T, arrange([o[:5] + (z[5],) for o, z in zip(ops, sizes)]))
+
+
+def calls(g, core, me, T, G, topo, real):
+    ops = []
+    nd = [0]
+    v, a, p = g.vector, g.scalar, g.tensor
+    NJ, C = CFG["nj"], CFG
+    part_of = [""]
+
+    def op(q, fn, rd, wr, own=None, cost=None):
+        ops.append((q, fn, list(rd), list(wr), own, (cost or (0.0, 0.0, 0.0)) +
+                    (C["lead"].get(part_of[0], 0.0) + C["lead"].get(part_of[0] + q, 0.0),)))
+
+    def join(n):
+        some = ops[-n:]
+        del ops[-n:]
+        op(some[0][0], [f for o in some for f in o[1]], some[0][2], some[0][3], None, (C["fix"] * 2 + 250.0 * C["f"], 0.0, 0.0))
+
+    def ind(win, off):
+        return win.indirect(off) if real else (win, off)
+
+    def work(out, ins, two=False):
+        if real:
+            return None
+        if isinstance(out, tuple):
+            c = C["s"] * 16 * out[1].shape[1]
+        elif isinstance(ins[0], tuple):
+            c = C["g"] * out.shape[1]
+        else:
+            c = ins[0].shape[1] * (0.5 if all(x.itemsize == 2 for x in [out] + ins) else 1.0)
+            if two and all(x.itemsize < 8 for x in ins):
+                c = 2 * c
+        return (C["fix"] + max(20.0, c) * 0.83 * C["f"], 0.0, 0.0)
+
+    def moved(rows, nbytes, engines):
+        return (rows * C["row"] + nbytes / C["bw"]) / engines
+
+    def dma(q, pairs, rd, wr):
+        s = "d%d" % nd[0]
+        nd[0] += 1
+        e = g.sync if q == "s" else g.scalar
+        cost = None if real else (60.0 * len(pairs), C["dma"],
+                                  sum(moved(max(o.shape[0], i.shape[0], 16), o.nbytes, 16) for o, i in pairs))
+        op(q, [lambda o=o, i=i: e.dma_start(o, i) for o, i in pairs], rd, wr, (s, 16 * len(pairs)), cost)
+
+    def ts(out, in0, s1, s2, o0, o1, rd, wr):
+        if s2 is None:
+            op("v", [lambda: v.tensor_scalar(out, in0, s1, None, o0)], rd, wr, None, work(out, [in0]))
+        else:
+            op("v", [lambda: v.tensor_scalar(out, in0, s1, s2, o0, o1)], rd, wr, None, work(out, [in0]))
+
+    def tt(out, in0, in1, o, rd, wr):
+        op("v", [lambda: v.tensor_tensor(out, in0, in1, o)], rd, wr, None, work(out, [in0, in1], True))
+
+    def cp(out, in_, rd, wr):
+        op("v", [lambda: v.tensor_copy(out, in_)], rd, wr, None, work(out, [in_]))
+
+    def fill(ap, x, wr):
+        op("v", [lambda: v.memset(ap, x)], [], wr, None, work(ap, [ap]))
+
+    def scan(out, d0, d1, rd, wr):
+        op("v", [lambda: v.tensor_tensor_scan(out, d0, d1, 0.0, ALU.mult, ALU.add)], rd, wr, None, work(out, [d0, d1]))
+
+    def act(out, in_, func, rd, wr, bias=0.0, scale=1.0, acc=None):
+        cost = None if real else work(out, [in_, T.COL])
+        if func == ACT.Copy:
+            op("a", [lambda: a.activation(out, in_, func)], rd, wr, None, cost)
+        elif acc is not None:
+            op("a", [lambda: a.activation(out, in_, func, bias=bias, scale=scale, accum_out=acc)], rd, wr, None, cost)
+        else:
+            op("a", [lambda: a.activation(out, in_, func, bias=bias, scale=scale)], rd, wr, None, cost)
+
+    def mm(out, terms, bank, first=True, final=True):
+        fns, rd = [], []
+        for n, (l, r, x) in enumerate(terms):
+            st, sp = first and n == 0, final and n == len(terms) - 1
+            fns.append(lambda l=l, r=r, st=st, sp=sp: p.matmul(out, l, r, st, sp))
+            rd += x
+        cost = None if real else (sum(max(64, out.shape[1]) * (4 if l.itemsize == 4 else 1) for l, r, x in terms)
+                                  * C["pe"] * C["f"], 0.0, 0.0)
+        op("p", fns, sorted(set(rd)), [bank], None, cost)
+
+    def pool(fn, w, rd, wr):
+        op("g", [fn], rd, wr, None, (150.0 + 2 * w * 0.83 * C["f"], 0.0, 0.0))
+
+    def iota(name, lo, hi, pat, base=0, cm=0, integer=False, tag=None):
+        if integer:
+            pool(lambda: g.iota(T[name][:, lo:hi], pat, base, cm), hi - lo, [], [tag or name])
+        else:
+            pool(lambda: g.iota(T[name][:, lo:hi], pat, base, cm, allow_small_or_imprecise_dtypes=True), hi - lo, [], [tag or name])
+
+    def sel(name, r):
+        return T[name][:, 15 - r:143 - r]
+
+    peers = [(me + d) % N for d in (1, 2, 3)]
+    ids = {q: DstId(rid=topo.addr(G.cores[q])[0], pnc=topo.addr(G.cores[q])[1]) for q in peers}
+    eng = [e for e in topo.engines(core, G.cores[peers[0]])
+           if all(e in topo.engines(core, G.cores[q]) for q in peers)]
+    full = sum(1 << e for e in eng)
+    part = len(eng) // 4
+    own0 = me * V
+    n1 = CAP * (N - 1 - me)
+    CTALL = ["CTo0", "CTo1", "CTo2", "CTo3", "CTr"]
+    WALL = ["W0", "W1", "W2", "W3"]
+
+    def send_c(lo, w, t, rd):
+        ap = T.CT[:, own0 + lo:own0 + lo + w]
+        op("g", [lambda: g.remote_dma_fused([RemoteDMATransfer(
+            dst_ids=[ids[q] for q in peers], dma_engine_mask=full, remote_sem=G.sem["ac%d" % t], srcs=[ap], dsts=[ap, ap, ap])],
+            local_sem=G.sem["lc%d" % t])], rd, [], ("lc%d" % t, len(eng)), (500.0, C["rem"], moved(384, 768 * w, len(eng))))
+        op("x", None, [], ["CTr"], ("ac%d" % t, 3 * len(eng)))
+
+    def send_x(t):
+        xb = T["XB%d" % t]
+
+        def trs():
+            return [RemoteDMATransfer(dst_ids=[ids[q]], dma_engine_mask=sum(1 << e for e in eng[d * part:(d + 1) * part]),
+                                      remote_sem=G.sem["ax%d" % t], src=xb[:, NC + CAP * d:NC + CAP * (d + 1)],
+                                      dst=xb[:, CAP * (2 - d):CAP * (3 - d)]) for d, q in enumerate(peers)]
+        op("g", [lambda: g.remote_dma_fused(trs(), local_sem=G.sem["lx%d" % t])], ["XB%d" % t], [], ("lx%d" % t, 3 * part),
+           (500.0, C["rem"], moved(128, 128 * 192, part)))
+        op("x", None, [], ["XL%d" % t], ("ax%d" % t, 3 * part))
+
+    def send_free(t):
+        op("g", [lambda: g.remote_dma_fused([RemoteDMATransfer(dst_ids=[ids[q]], dma_engine_mask=1 << eng[3 * part + d],
+                                                               remote_sem=G.sem["af%d" % t]) for d, q in enumerate(peers)],
+                                            local_sem=G.sem["lf%d" % t])],
+           ["AN%d" % j for j in range(8)], [], ("lf%d" % t, 3), (500.0, C["rem"], 0.0))
+        op("x", None, [], ["FR"], ("af%d" % t, 3))
+
+    def col(j):
+        return T.COL[:, j:j + 1]
+
+    def blk(name, b):
+        return T[name][:, b * B:(b + 1) * B]
+
+    def cown(t):
+        b = t % 4
+        return T.CT[:, own0 + b * B:own0 + (b + 1) * B]
+
+    def dmat(name, w, rd=()):
+        ts(T[name][:, :], T.X143[:, :], col(2), w, ALU.is_equal, ALU.mult, ["X143", "c2"] + list(rd), [name])
+
+    def scaled(name, src, w):
+        act(T[name][:, :], T[src][:, :], ACT.Identity, [src], [name], scale=w)
+
+    def y_list(xlo, n, rd, bank):
+        c = n // 16
+        mm(T[bank][:, 0:c], [(sel("DW", r), T.XS[:, xlo + r:xlo + n:16], ["DW"] + rd) for r in range(16)], bank)
+        cp(T.HI[:, 0:c], T[bank][:, 0:c], [bank], ["HI"])
+        ts(T.HI[:, 0:c], T.HI[:, 0:c], M - 1, None, ALU.bitwise_and, None, ["HI"], ["HI"])
+        cp(T.HU[:, 0:c], T.HI[:, 0:c], ["HI"], ["HU"])
+        tt(T.DF[:, 0:n], ind(T.JM[:, :], T.HU[:, 0:c]), T.XS[:, xlo:xlo + n], ALU.subtract, ["JM", "HU"] + rd, ["DF"])
+
+    def y_abs(n, ylo, wr):
+        act(T.Y[:, ylo:ylo + n], T.DF[:, 0:n], ACT.Abs, ["DF"], wr)
+
+    def nb_lists(b):
+        nbi, tg = blk("NBI", b), "NBI%d" % b
+        cp(blk("NBU", b), nbi, [tg], ["NBU%d" % b])
+        ts(blk("KO2", b), nbi, 1.0 / 1024, 193.0 - 511.5 / 1024, ALU.mult, ALU.add, [tg], ["KO2%d" % b])
+        ts(T.A8[:, :], nbi, 1.0 / 256, 192.0 - 127.5 / 256, ALU.mult, ALU.add, [tg], ["A8"])
+        cp(T.NBF[:, :], nbi, [tg], ["NBF"])
+        mm(T.M1[:, 0:B], [(T.IDF[:, :], T.NBF[:, :], ["IDF", "NBF"]), (T.ID8[:, :], T.A8[:, :], ["ID8", "A8"]),
+                          (T.ID10[:, :], blk("KO2", b), ["ID10", "KO2%d" % b]), (T.ID[:, :], T.K1[:, :], ["ID", "K1"])], "M1")
+        act(blk("TC", b), T.M1[:, 0:B], ACT.Identity, ["M1"], ["TC%d" % b], bias=256.0 * (16384 * 193 - 3840 * 192), scale=256.0)
+
+    def ent_split(lo, hi, tag, bank):
+        cp(T.EF[:, lo:hi], T.EI[:, lo:hi], ["EI" + tag], ["EF" + tag])
+        act(T.EH[:, lo:hi], T.EF[:, lo:hi], ACT.Copy, ["EF" + tag], ["EH" + tag])
+        mm(T[bank][:, 0:hi - lo], [(T.IDF[:, :], T.EF[:, lo:hi], ["IDF", "EF" + tag]),
+                                   (T.IDM[:, :], T.EH[:, lo:hi], ["IDM", "EH" + tag])], bank)
+        act(T.EL[:, lo:hi], T[bank][:, 0:hi - lo], ACT.Copy, [bank], ["EL" + tag])
+
+    def ent_place(b0, b1, tags):
+        pairs = []
+        for b in range(b0, b1):
+            w = slice(b * K * B, (b + 1) * K * B)
+            pairs += [(T.W[0::16, w], blk("EH", b)), (T.W[1::16, w], blk("EL", b))]
+        dma("s", pairs, ["EH" + x for x in tags] + ["EL" + x for x in tags],
+            ["W%d" % b for b in range(b0, b1)] + ["Wf%d" % x for x in range(4 * b0, 4 * b1)])
+
+    def e_lists(t):
+        b = t % 4
+        for lo, hi in zip(C["cut"][:-1], C["cut"][1:]):
+            mm(T.M2[:, 0:hi - lo], [(sel("DE", r), T.W[:, b * K * B + 16 * lo + r:b * K * B + 16 * hi:16], ["DE", "W%d" % b])
+                                    for r in range(16)], "M2")
+            cp(T.EU[:, lo:hi], T.M2[:, 0:hi - lo], ["M2"], ["EU%d" % j for j in range(lo // 32, hi // 32)])
+
+    def n_tile(t):
+        b = t % 4
+        dma("s", [(T.NN[:, :], T.W[2::16, b * K * B:(b + 1) * K * B])], ["W%d" % b], ["NN"])
+
+    def ucalc(t):
+        mm(T.M1[:, 0:B], [(T.BO[:, :], blk("Y", t), ["BO", "Y%d" % t])], "M1")
+        act(T.UF[:, :], T.M1[:, 0:B], ACT.Identity, ["M1"], ["UF"], bias=192.0 - 31.5 / 64, scale=1.0 / 64)
+        mm(T.M1[:, B:2 * B], [(T.BO[:, :], blk("Y", t), ["BO", "Y%d" % t]), (T.ID64[:, :], T.UF[:, :], ["ID64", "UF"])], "M1")
+        act(T.U[:, :], T.M1[:, B:2 * B], ACT.Identity, ["M1"], ["U"], bias=64.0 * 192)
+
+    def yrep(t):
+        for h in (0, 1):
+            mm(blk("YB", h), [(T.ID[:, :], blk("Y", t), ["ID", "Y%d" % t])], "YB")
+
+    def crep(t):
+        for h in (0, 1):
+            mm(blk("CB", h), [(T.ID[:, :], cown(t), ["ID", "CTo%d" % (t % 4)])], "CB")
+
+    def tiles_n(t):
+        dma("s", [(T.AN[:, 0:B], cown(t))], ["CTo%d" % (t % 4)], ["ANo"])
+
+    def tiles_p(t):
+        ap = "AP%d" % (t % 2)
+        dma("s", [(blk(ap, 16), cown(t)), (blk(ap, 17), blk("Y", t))], ["CTo%d" % (t % 4), "Y%d" % t], [ap + "x"])
+
+    def bounds(t):
+        act(blk("TB", 0), cown(t), ACT.Identity, ["CTo%d" % (t % 4)], ["TB"], bias=1.0)
+        act(T.CM[:, :], cown(t), ACT.Identity, ["CTo%d" % (t % 4)], ["CM"], bias=-1.0)
+
+    def payload(t):
+        act(T.PW[:, :], T.PB[:, :], ACT.Identity, ["PB", "BC", "c14"], ["PW"], bias=T.BC[:, t:t + 1], scale=col(14))
+
+    def template(t):
+        act(T["XB%d" % t][:, 144:336], T.TPI[:, :], ACT.Identity, ["TPI", "c7"], ["XB%d" % t], bias=-127.5, scale=col(7))
+        act(T.YF[:, :], blk("Y", t), ACT.Identity, ["Y%d" % t], ["YF"], bias=-127.5)
+
+    def acount():
+        mm(T.M1[:, 0:16], [(T.ONE[:, :], T.GO[:, :], ["ONE", "GO"])], "M1")
+        act(T.QB[:, :], T.M1[:, 0:16], ACT.Identity, ["M1"], ["QB", "AF"], bias=1572864.0, scale=2048.0, acc=col(8))
+        act(T.AG[:, :], col(8), ACT.Identity, ["AF"], ["AG"], bias=-31.5 / 64, scale=1.0 / 131072)
+        act(T.AM[:, :], T.AG[:, :], ACT.Identity, ["AF", "AG"], ["AM"], bias=col(8), scale=-131072.0)
+
+    def arrive(t):
+        xb, tg, mu = T["XB%d" % t], ["XB%d" % t, "XL%d" % t], "MU%d" % (t % 2)
+        ts(T.HX[:, :], xb[:, 0:NC], MAGIC, MAGIC, ALU.add, ALU.subtract, tg, ["HX"])
+        mm(T.M2[:, 0:NC], [(T.BOS[:, :], T.HX[:, :], ["BOS", "HX"])], "M2")
+        tt(T.MM[:, :], T.M2[:, 0:NC], T.DIAG[:, 0:NC], ALU.mult, ["M2", "DIAG"], ["MM"])
+        scan(T.MS[:, :], T.SEG[:, :], T.MM[:, :], ["SEG", "MM"], ["MS"])
+        cp(T[mu][:, :], T.MS[:, 15:NC:16], ["MS"], [mu])
+        mm(T.M2[:, NC:2 * NC], [(T.IDF[:, :], xb[:, 0:NC], ["IDF"] + tg), (T.IDFM[:, :], T.HX[:, :], ["IDFM", "HX"])], "M2")
+        if n1:
+            act(T.PL[:, NC * t + NC - n1:NC * t + NC], T.M2[:, NC:NC + n1], ACT.Identity, ["M2"], ["PL"], bias=127.5)
+        act(T.PL[:, NC * t:NC * t + NC - n1], T.M2[:, NC + n1:2 * NC], ACT.Identity, ["M2"], ["PL"], bias=127.5)
+        join(2 if n1 else 1)
+
+    def arrive_w(t):
+        mu = "MU%d" % (t % 2)
+        if t < 4:
+            cp(ind(T.W[:, :], T[mu][:, :]), T.PW[:, :], [mu, "PW"], WALL)
+        else:
+            ts(T.TW[:, :], ind(T.W[:, :], T[mu][:, :]), col(5), col(5), ALU.mult, ALU.add, [mu, "c5"] + WALL, ["TW"])
+            tt(ind(T.W[:, :], T[mu][:, :]), T.TW[:, :], T.PW[:, :], ALU.add, [mu, "PW", "TW"], WALL)
+
+    def arrive_wf(t):
+        mu = "MU%d" % (t % 2)
+        ts(ind(T.WF[:, :], T[mu][:, :]), T.PB[:, :], 1.0, float(NC * t), ALU.mult, ALU.add, [mu, "PB"], ["WF"])
+
+    def gp(t, j):
+        ap = "AP%d" % (t % 2)
+        act(T[ap][:, 2 * B * j:2 * B * (j + 1)], ind(T.PL[:, :], T.EU[:, 32 * j:32 * j + 32]), ACT.Copy,
+            ["PL", "EU%d" % j], ["%s_%d" % (ap, j)])
+
+    def mp(t, j):
+        ap, ct = "AP%d" % (t % 2), "CTo%d" % (t % 4)
+        tg, ks, sl = "%s_%d" % (ap, j), (2 * j, 2 * j + 1), slice(2 * B * j, 2 * B * (j + 1))
+        terms = [(T.BOM[:, :], cown(t), ["BOM", ct])] if j == 0 else []
+        if j < 8 - NJ[t]:
+            terms += [(sel("DN", k), blk(ap, k), ["DN", tg]) for k in ks]
+            mm(T.HB[:, 0:B], terms, "HB", j == 0, False)
+            tt(T.MP[:, sl], T[ap][:, sl], T.CB[:, :], ALU.max, [tg, "CB"], ["MP%d" % j])
+            mm(T.HB[:, 0:B], [(sel("DP", k), blk("MP", k), ["DP", "MP%d" % j]) for k in ks], "HB", False, j == 7)
+        else:
+            bank = "M1"
+            for h in (0, 1):
+                mm(blk(bank, h), [(T.IDM[:, :], cown(t), ["IDM", ct]), (T.ID[:, :], blk(ap, ks[h]), ["ID", tg])], bank)
+            act(T.MP[:, sl], T[bank][:, :], ACT.Abs, [bank], ["MP%d" % j])
+            terms += [(sel("D1", k), cown(t), ["D1", ct]) for k in ks]
+            mm(T.HB[:, 0:B], terms, "HB", j == 0, False)
+            mm(T.HB[:, 0:B], [(sel("D1", k), blk("MP", k), ["D1", "MP%d" % j]) for k in ks], "HB", False, j == 7)
+
+    part_of[0] = "L"
+    dma("s", [(T.CT[:, own0:own0 + V], T.cen[:, :])], [], CTALL[:4])
+    part_of[0] = ""
+    dma("s", [(blk("XS", 0), T.wk[:, 0:B])], [], ["XS0"])
+    dma("s", [(T.JM[:, :], T.jmp[:, :])], [], ["JM"])
+    dma("s", [(blk("NBI", 0), T.nb[:, 0:B])], [], ["NBI0"])
+    dma("s", [(blk("EI", 0), T.ent[:, 0:K * B])], [], ["EIa"])
+    iota("PI", 0, 4, [[0, 4]], 0, 1, True)
+    iota("X143", 0, 144, [[1, 144]])
+    iota("XG", 0, 128, [[1, 8], [0, 16]])
+    iota("KO1", 0, B, [[8, B]], -192)
+    send_c(0, V, 5, CTALL[:4])
+    dma("s", [(T.PL[:, :], T.pl[:, :])], ["CTr"], ["PL"])
+    dma("s", [(blk("EI", b), T.ent[:, b * K * B:(b + 1) * K * B]) for b in (1, 2, 3)], ["CTr"], ["EIb", "EIc"])
+    dma("s", [(T.XS[:, B:V], T.wk[:, B:V])], ["CTr"], ["XS1", "XS2", "XS3"])
+    dma("s", [(T.NBI[:, B:V], T.nb[:, B:V])], ["CTr"], ["NBI1", "NBI2", "NBI3"])
+    iota("K1", 0, B, [[512, 8], [-256, 2], [0, 16]], 256)
+    iota("J16", 0, B, [[0, 16], [1, 16]])
+    iota("C16", 0, 16, [[16, 16]])
+    iota("OC", 0, 16 * (N - me), [[1, N - me], [0, 16]], me + 1)
+    if me:
+        iota("OC", 16 * (N - me), 64, [[1, me], [0, 16]], 1)
+    join(2 if me else 1)
+    iota("NDI", 0, 64, [[CAP, 4], [-16, 16]], 63)
+    iota("TPI", 0, NC, [[0, 4], [256, CAP]], 256 * (K * V + CAP * me))
+    if n1:
+        iota("PB", 0, n1, [[1, n1]], NC - n1)
+    iota("PB", n1, NC, [[1, NC - n1]], 0)
+    join(2 if n1 else 1)
+    iota("BI", 0, 8, [[NC, 8]])
+    ts(T.PJ[:, :], T.PI[:, :], 15, None, ALU.bitwise_and, None, ["PI"], ["PJ"])
+    cp(col(1), T.PI[:, 0:1], ["PI"], ["c1"])
+    cp(col(0), T.PJ[:, 0:1], ["PJ"], ["c0"])
+    ts(col(2), col(1), col(0), 15.0, ALU.subtract, ALU.add, ["c0", "c1"], ["c2"])
+    ts(col(3), col(0), 2.0, 1.0, ALU.mult, ALU.add, ["c0"], ["c3"])
+    ts(col(4), col(0), 2.0, None, ALU.is_lt, None, ["c0"], ["c4"])
+    ts(col(7), col(0), 0.0, None, ALU.is_equal, None, ["c0"], ["c7"])
+    dmat("DW", col(3), ["c3"])
+    ts(T.IDF[:, :], T.X143[:, 0:128], col(1), None, ALU.is_equal, None, ["X143", "c1"], ["IDF"])
+    dmat("D1", 1.0)
+    ts(col(6), col(2), -15.0, 0.0625, ALU.add, ALU.mult, ["c2"], ["c6"])
+    ts(T.BOF[:, :], T.XG[:, :], col(6), None, ALU.is_equal, None, ["XG", "c6"], ["BOF"])
+    for nm, src, w in [("ID", "IDF", 1.0), ("IDM", "IDF", -1.0), ("DA", "D1", -2048.0), ("DM", "D1", 4096.0),
+                       ("BOM", "BOF", -1.0), ("B64", "BOF", 64.0), ("ID8", "IDF", 3840.0), ("ID10", "IDF", -16384.0),
+                       ("DN", "D1", -1.0), ("DP", "D1", 2.0)]:
+        scaled(nm, src, w)
+    act(T.DE[:, :], T.D1[:, :], ACT.Identity, ["D1", "c4"], ["DE"], scale=col(4))
+    pool(lambda: g.affine_select(T.LB[:, :], T.BOM[:, :], [[-1, 128]], ALU.is_ge, 0.0, 0, 1), 128, ["BOM"], ["LB"])
+    pool(lambda: g.affine_select(T.LM[:, :], T.LB[:, :], [[-1, 128]], ALU.not_equal, -256.0, 0, 1), 128, ["LB"], ["LM"])
+    pool(lambda: g.affine_select(T.TRI[:, :], T.B64[:, :], [[1, 128]], ALU.is_ge, 0.0, 0, -1), 128, ["B64"], ["TRI"])
+    fill(T.W[:, 0:K * B], 1.0, ["W0"])
+    y_list(0, B, ["XS0"], "M2")
+    y_abs(B, 0, ["Y0"])
+    ent_split(0, B, "a", "K0")
+    ent_place(0, 1, ["a"])
+    tiles_n(0)
+    yrep(0)
+    crep(0)
+    tiles_p(0)
+    nb_lists(0)
+    for nm, src, w in [("BO", "BOF", 1.0), ("DC", "D1", 256.0), ("ID64", "IDF", -64.0), ("IDFM", "IDF", -1.0),
+                       ("BOS", "BOF", 1.0 / 256)]:
+        scaled(nm, src, w)
+    fill(T.AM[:, :], 0.0, ["AM"])
+    fill(T.ONE[:, :], 1.0, ["ONE"])
+    cp(T.REP[:, :], T.PJ[:, :], ["PJ"], ["REP"])
+    ts(T.DIAG[:, :], T.J16[:, :], col(0), None, ALU.is_equal, None, ["J16", "c0"], ["DIAG"])
+    ts(T.SEG[:, :], T.J16[:, 0:NC], 0.0, None, ALU.not_equal, None, ["J16"], ["SEG"])
+    ts(T.IB[:, :], T.C16[:, :], col(0), None, ALU.add, None, ["C16", "c0"], ["IB"])
+    ts(T.NDC[:, :], T.NDI[:, :], col(0), None, ALU.subtract, None, ["NDI", "c0"], ["NDC"])
+    ts(T.I17[:, :], T.IB[:, :], 17.0 * B, None, ALU.add, None, ["IB"], ["I17"])
+    ts(T.DUM[:, :], T.IB[:, :], float(NC), None, ALU.add, None, ["IB"], ["DUM"])
+    ts(T.THR[:, :], T.NDC[:, :], CAP - 255.0, None, ALU.add, None, ["NDC"], ["THR"])
+    ts(col(14), col(0), 1.0, None, ALU.is_equal, None, ["c0"], ["c14"])
+    ts(col(5), col(0), 2.0, None, ALU.is_ge, None, ["c0"], ["c5"])
+    ts(col(15), col(0), 2.0, 2.0, ALU.is_ge, ALU.mult, ["c0"], ["c15"])
+    ts(T.BC[:, 0:4], T.BI[:, 0:4], col(7), col(15), ALU.mult, ALU.add, ["BI", "c7", "c15"], ["BC"])
+    ts(T.BC[:, 4:8], T.BI[:, 4:8], col(7), None, ALU.mult, None, ["BI", "c7"], ["BC"])
+    e_lists(0)
+    ent_split(B, 3 * B, "b", "M2")
+    ent_split(3 * B, V, "c", "M2")
+    template(0)
+    bounds(0)
+    ucalc(0)
+    payload(0)
+    for x in range(4, 16):
+        if x >= 16 - C["pool"]:
+            w = V + (NC if x == 15 else 0)
+            iota("W", V * x, V * x + w, [[0, w]], 1, tag="Wf%d" % x)
+        else:
+            fill(T.W[:, V * x:V * (x + 1)], 1.0, ["Wf%d" % x])
+    ent_place(1, 4, ["b", "c"])
+    dma("s", [(T.WF[0::16, b * K * B:(b + 1) * K * B], blk("EF", b)) for b in range(4)], ["EFa", "EFb", "EFc"], ["WF"])
+
+    for t in range(R):
+        b = t % 4
+        ap = "AP%d" % (t % 2)
+        APALL = ["%s_%d" % (ap, j) for j in range(8)] + [ap + "x"]
+        nx = t + 1 < R
+        part_of[0] = "N%d" % t
+        tt(T.MN[:, 0:B], T.AN[:, 0:B], T.YB[:, 0:B], ALU.max, ["ANo", "YB"], ["MNo"])
+        for j in range(8):
+            lo = B + 2 * B * j
+            act(T.AN[:, lo:lo + 2 * B], ind(T.CT[:, :], T.NBU[:, b * B + 32 * j:b * B + 32 * j + 32]), ACT.Copy,
+                CTALL + ["NBU%d" % b], ["AN%d" % j])
+            tt(T.MN[:, lo:lo + 2 * B], T.AN[:, lo:lo + 2 * B], T.YB[:, :], ALU.max, ["AN%d" % j, "YB"], ["MN%d" % j])
+            if j % 2 == 1:
+                q = j // 2
+                bank = BANKS[q % 2]
+                c0, c1 = (0 if q == 0 else B + 4 * B * q), B + 4 * B * (q + 1)
+                w = (c1 - c0) // 16
+                ex = ["ANo", "MNo"] if q == 0 else []
+                out = T[bank][:, 0:w]
+                mm(out, [(sel("DA", r), T.AN[:, c0 + r:c1:16], ["DA", "AN%d" % (j - 1), "AN%d" % j] + ex) for r in range(16)],
+                   bank, True, False)
+                mm(T[bank][:, w - 64:w], [(T.ID[:, :], T.KO1[:, 64 * q:64 * q + 64], ["ID", "KO1"]),
+                                          (T.ID[:, :], T.KO2[:, b * B + 64 * q:b * B + 64 * q + 64], ["KO2%d" % b])], bank, False, False)
+                mm(out, [(sel("DM", r), T.MN[:, c0 + r:c1:16], ["DM", "MN%d" % (j - 1), "MN%d" % j] + ex) for r in range(16)],
+                   bank, False, True)
+            if t == 0 and j == 1:
+                y_list(B, 3 * B, ["XS1", "XS2", "XS3"], "M1")
+            if t > 0 and j == 1:
+                arrive_wf(t - 1)
+            if j in (2, 4, 6):
+                q = j // 2 - 1
+                bank = BANKS[q % 2]
+                if q == 0:
+                    ts(T.TH[:, :], T[bank][:, 0:16], T.AM[:, :], None, ALU.subtract, None, [bank, "AM"], ["TH"])
+                    cp(T.ACC[:, :], T[bank][:, 16:80], [bank], ["ACC"])
+                    tt(T.ACC[:, 0:16], T.ACC[:, 0:16], T.TH[:, :], ALU.min, ["ACC", "TH"], ["ACC"])
+                else:
+                    tt(T.ACC[:, :], T.ACC[:, :], T[bank][:, 0:64], ALU.min, [bank, "ACC"], ["ACC"])
+        part_of[0] = "T%d" % t
+        if nx:
+            send_free(t)
+        tt(T.ACC[:, :], T.ACC[:, :], T.KB1[:, 0:64], ALU.min, ["KB1", "ACC"], ["ACC"])
+        tt(T.A32[:, :], T.ACC[:, 0:32], T.ACC[:, 32:64], ALU.min, ["ACC"], ["A32"])
+        tt(T.KG[:, :], T.A32[:, 0:16], T.A32[:, 16:32], ALU.min, ["A32"], ["KG"])
+        ts(T.CODE[:, :], T.KG[:, :], 7, None, ALU.bitwise_and, None, ["KG"], ["CODE"])
+        ts(T.L1[:, :], T.KG[:, :], 3, 255, ALU.logical_shift_right, ALU.bitwise_and, ["KG"], ["L1"])
+        tt(T.H[:, :], ind(T.CODE[:, :], T.REP[:, :]), T.OC[:, :], ALU.is_equal, ["CODE", "REP", "OC"], ["H"])
+        cp(T.L1U[:, :], T.L1[:, :], ["L1"], ["L1U"])
+        scan(T.S[:, :], T.SEG[:, 0:64], T.H[:, :], ["SEG", "H"], ["S"])
+        mm(T.M2[:, 0:64], [(T.ID[:, :], T.NDC[:, :], ["ID", "NDC"]), (T.LM[:, :], T.H[:, :], ["LM", "H"]),
+                           (T.BO[:, :], T.S[:, :], ["BO", "S"])], "M2")
+        tt(T.X[:, :], ind(blk("TC", b), T.L1U[:, :]), T.DIAG[:, :], ALU.mult, ["TC%d" % b, "L1U", "DIAG"], ["X"])
+        tt(T.VV[:, :], T.M2[:, 0:64], T.THR[:, :], ALU.is_lt, ["M2", "THR"], ["VV"])
+        tt(T.Q[:, :], T.M2[:, 0:64], T.VV[:, :], ALU.mult, ["M2", "VV"], ["Q"])
+        tt(T.QA[:, :], T.Q[:, 0:32], T.Q[:, 32:64], ALU.add, ["Q"], ["QA"])
+        tt(T.QB[:, :], T.QA[:, 0:16], T.QA[:, 16:32], ALU.add, ["QA"], ["QB"])
+        tt(T.QC[:, :], T.QB[:, :], T.DUM[:, :], ALU.add, ["QB", "DUM"], ["QC"])
+        cp(T.PY[:, :], T.QC[:, :], ["QC"], ["PY"])
+        tt(ind(T["XB%d" % t][:, 144:XW_], T.PY[:, :]), T.X[:, :], T.YF[:, :], ALU.add, ["PY", "X", "YF"], ["XB%d" % t])
+        send_x(t)
+        tt(T.GO[:, :], T.KG[:, :], T.TH[:, :], ALU.is_lt, ["KG", "TH"], ["GO"])
+        tt(T.KEY[:, :], T.KG[:, :], T.TH[:, :], ALU.is_ge, ["KG", "TH"], ["KEY"])
+        tt(T.BP[:, :], T.KEY[:, :], T.I17[:, :], ALU.mult, ["KEY", "I17"], ["BP"])
+        part_of[0] = "P%d" % t
+        for j in range(8):
+            gp(t, j)
+            mp(t, j)
+        part_of[0] = "Q%d" % t
+        if t == 0:
+            act(T.G[:, :], T.HB[:, 0:B], ACT.Relu, ["HB"], ["G"], bias=2047.0, scale=-1.0)
+            y_abs(3 * B, B, ["Y1", "Y2", "Y3"])
+        else:
+            act(T.M1[:, 0:B], T.HB[:, 0:B], ACT.Relu, ["HB"], ["M1"], bias=2047.0, scale=-1.0)
+            tt(T.G[:, :], T.M1[:, 0:B], T.NN[:, :], ALU.mult, ["M1", "NN"], ["G"])
+        mm(blk("TB", 1), [(T.BOF[:, :], T.G[:, :], ["BOF", "G"])], "TB")
+        mm(blk("HB", 1), [(T.TRI[:, :], T.G[:, :], ["TRI", "G"])], "HB")
+        tt(T.UT[:, :], blk("TB", 1), T.U[:, :], ALU.mult, ["TB", "U"], ["UT"])
+        tt(T.NO[:, :], blk("HB", 1), T.UT[:, :], ALU.is_le, ["HB", "UT"], ["NO"])
+        mm(T.M1[:, 0:16], [(T.ID[:, :], T.IB[:, :], ["ID", "IB"])] +
+           [(sel("DC", r), T.NO[:, r:B:16], ["DC", "NO"]) for r in range(16)], "M1")
+        part_of[0] = "A%d" % t
+        arrive(t)
+        if not nx:
+            arrive_wf(t)
+            dma("s", [(T.ye[:, :], T.WF[0::16, 0:K * V])], ["WF"], [])
+            arrive_w(t)
+            dma("s", [(T.yn[:, :], T.W[2::16, 0:K * V])], WALL, [])
+            dma("s", [(T.yz[:, 5 * NC:6 * NC], T.PL[:, 5 * NC:6 * NC])], ["PL"], [])
+        part_of[0] = "Q%d" % t
+        tt(T.IX[:, :], T.M1[:, 0:16], T.BP[:, :], ALU.max, ["M1", "BP"], ["IX"])
+        cp(T.IXU[:, :], T.IX[:, :], ["IX"], ["IXU"])
+        tt(T.CN[:, :], ind(T[ap][:, :], T.IXU[:, :]), T.CM[:, :], ALU.max, APALL + ["IXU", "CM"], ["CN"])
+        tt(cown(t), T.CN[:, :], blk("TB", 0), ALU.min, ["CN", "TB"], ["CTo%d" % b])
+        if nx:
+            send_c(b * B, B, t, ["CTo%d" % b, "FR"])
+        act(blk("XS", b), ind(T[ap][:, :], T.IXU[:, :]), ACT.Copy, APALL + ["IXU"], ["XS%d" % b])
+        if not nx:
+            dma("a", [(T.yc[:, b * B:(b + 1) * B], cown(t))], ["CTo%d" % b], [])
+            dma("a", [(T.yx[:, b * B:(b + 1) * B], blk("XS", b))], ["XS%d" % b], [])
+            break
+        s = t + 1
+        part_of[0] = "A%d" % t
+        arrive_w(t)
+        e_lists(s)
+        part_of[0] = "W%d" % t
+        yrep(s)
+        crep(s)
+        tiles_n(s)
+        template(s)
+        acount()
+        if s < 4:
+            nb_lists(s)
+        bounds(s)
+        payload(s)
+        ucalc(s)
+        if t < 2:
+            y_list(t * B, B, ["XS%d" % t], "M2")
+            y_abs(B, (t + 4) * B, ["Y%d" % (t + 4)])
+        n_tile(s)
+        tiles_p(s)
+        if t >= 2:
+            dma("s", [(T.yc[:, b * B:(b + 1) * B], cown(t)), (T.yx[:, b * B:(b + 1) * B], blk("XS", b))],
+                ["CTo%d" % b, "XS%d" % b], [])
+        if t == R - 2:
+            dma("s", [(T.yz[:, 0:5 * NC], T.PL[:, 0:5 * NC]), (T.yz[:, 6 * NC:ZP], T.PL[:, 6 * NC:ZP])], ["PL"], [])
+    return ops

@@ -7,56 +7,91 @@ NC = N * CAP
 WW = K * V + NC
 XW_ = 592
 MAGIC = 3221225472.0
-CFG = {"nj": [0, 0, 1, 0, 1, 1], "cut": [0, 64, 128, 256], "pool": 7, "look": 1.0,
-       "lead": {'L': 41.3, 'N0': 2.5, 'N1': -1.3, 'N2': 2.6, 'N3': 1.1, 'N4': 3.8, 'N5': 1.7, 'T0': 3.2, 'T1': 15.4, 'T2': 2.0,
-                'T3': 1.9, 'T4': 21.2, 'T5': 0.4, 'A0': -4.7, 'A1': 20.6, 'A2': -4.3, 'A3': -4.6, 'A4': -7.0, 'A5': 0.6,
-                'P0': -3.6, 'P1': -0.1, 'P2': -2.1, 'P3': -1.8, 'P4': -4.7, 'P5': -1.5, 'Q0': 16.0, 'Q1': 45.2, 'Q2': 6.8,
-                'Q3': -7.8, 'Q4': -6.0, 'Q5': 2.2, 'W0': -10.7, 'W1': 1.7, 'W2': 8.0, 'W3': -2.2, 'W4': 11.3},
+BIG = 1.0e9
+CFG = {"nv": ["aavaaaaa", "avaaaaaa"] * 3, "pv": ["avaavvaa", "aaaaaava"] * 3, "cut": [0, 64, 128, 256], "fill": "vvvvggggdddddvvv",
+       "th": "v", "evac": "v", "slack": 300.0, "still": True, "half": 0.5,
+       "two": 38.7, "due": {"P0": 6.6, "N0": 13.6, "Q0": 14.8, "F0": 29.7, "T0": 44.1, "C0": 22.6, "X0": 25.9, "A0": 28.0,
+                            "N1": 37.7, "F1": 33.9, "T1": 34.0, "X1": 36.5, "P1": 31.8, "A1": 50.2, "Q1": 57.4, "C1": 52.3},
        "f": 1.25, "g": 1.56, "s": 3.8, "pe": 0.42, "dma": 1800.0, "rem": 2000.0, "row": 40.0, "bw": 20.0,
-       "wake": 70.0, "fix": 50.0}
+       "wake": 70.0, "fix": 55.0}
 
 f32, bf, i32, u16 = "float32", "bfloat16", "int32", "uint16"
 SCRATCH = {}
 for _n, _w, _d in [
     ("W", WW, bf), ("WF", WW, f32), ("CT", N * V, bf), ("PL", ZP, bf), ("JM", M, bf), ("XS", V, bf), ("Y", R * B, bf),
-    ("YF", B, f32), ("AN", 17 * B, bf), ("MN", 17 * B, bf), ("AP0", 18 * B, bf), ("AP1", 18 * B, bf), ("MP", 16 * B, bf),
+    ("YF", R * B, f32), ("AN", 17 * B, bf), ("MN", 17 * B, bf), ("AP0", 18 * B, bf), ("AP1", 18 * B, bf), ("MP", 16 * B, bf),
     ("NBI", V, i32), ("NBU", V, u16), ("TC", V, f32), ("KO2", V, bf), ("A8", B, bf), ("NBF", B, f32),
     ("EI", V, i32), ("EF", V, f32), ("EH", V, bf), ("EL", V, bf), ("EU", B, u16), ("NN", B, bf),
     ("XB0", XW_, f32), ("XB1", XW_, f32), ("XB2", XW_, f32), ("XB3", XW_, f32), ("XB4", XW_, f32), ("XB5", XW_, f32),
-    ("PI", 4, i32), ("PJ", 4, i32), ("COL", 16, f32), ("REP", 4, u16), ("X143", 144, f32), ("XG", 128, f32), ("J16", B, f32),
+    ("PI", 4, i32), ("PJ", 8, i32), ("COL", 16, f32), ("REP", 8, u16), ("X143", 144, f32), ("XG", 128, f32), ("J16", B, f32),
     ("DM", 144, bf), ("DA", 144, bf), ("DE", 144, bf), ("DW", 144, bf), ("DC", 144, bf), ("DP", 144, bf), ("DN", 144, bf),
     ("D1", 144, bf), ("ID", 128, bf), ("IDM", 128, bf), ("IDF", 128, f32), ("IDFM", 128, f32), ("ID8", 128, bf),
-    ("ID10", 128, bf), ("ID64", 128, bf), ("ONE", 128, bf), ("BO", 128, bf), ("BOM", 128, bf), ("BOF", 128, f32),
+    ("ID10", 128, bf), ("ID64", 128, bf), ("IDB", 128, bf), ("DG", 128, bf), ("ONES", V, bf), ("ZERO", B, bf),
+    ("BO", 128, bf), ("BOM", 128, bf), ("BO2", 8, bf), ("BOF", 128, f32),
     ("BOS", 128, f32), ("B64", 128, f32), ("TRI", 128, f32), ("LB", 128, bf), ("LM", 128, bf),
-    ("DIAG", B, f32), ("SEG", NC, f32), ("KO1", B, bf), ("K1", B, bf), ("OC", 64, f32), ("C16", 16, f32),
-    ("IB", 16, bf), ("I17", 16, f32), ("DUM", 16, f32), ("NDI", 64, f32), ("NDC", 64, bf), ("THR", 64, f32),
-    ("TPI", NC, f32), ("PB", NC, f32), ("PW", NC, bf), ("BI", 8, f32), ("BC", 8, f32),
-    ("HI", 48, i32), ("HU", 48, u16), ("DF", 768, bf), ("UF", B, bf), ("U", B, f32),
-    ("ACC", 64, f32), ("A32", 32, f32), ("KEY", 16, f32), ("TH", 16, f32), ("GO", 16, bf), ("BP", 16, f32),
-    ("KG", 16, i32), ("CODE", 16, i32), ("L1", 16, i32), ("L1U", 16, u16), ("H", 64, bf), ("S", 64, bf),
-    ("VV", 64, f32), ("Q", 64, f32), ("QA", 32, f32), ("QB", 16, f32), ("QC", 16, f32), ("PY", 16, u16),
-    ("X", B, f32), ("AG", 1, bf), ("AM", 1, f32),
-    ("G", B, f32), ("UT", B, f32), ("NO", B, bf), ("IX", 16, f32), ("IXU", 16, u16), ("CM", B, bf), ("CN", B, bf),
-    ("HX", NC, f32), ("MM", NC, f32), ("MS", NC, f32), ("MU0", 12, u16), ("MU1", 12, u16), ("TW", NC, bf),
+    ("DIAG", NC, f32), ("DMIN", B, f32), ("SEG", NC, f32), ("KO1", B, bf), ("K1", B, bf), ("OC", 80, f32), ("C16", 16, bf),
+    ("IB", 16, bf), ("I17", 16, f32), ("MONE", 16, bf), ("NDC", 64, bf), ("THR", 64, f32), ("C96", 2, bf),
+    ("TPI", NC, f32), ("TPL", NC, f32), ("PB", NC, bf), ("PW", NC, bf), ("PF", NC, f32), ("BI", 8, f32), ("BC", 8, f32),
+    ("HI", 48, i32), ("HU", 48, u16), ("DF", 768, bf), ("UF", B, bf), ("U", 2 * B, bf), ("YT", B, bf), ("CTT", B, bf),
+    ("INI", 64, f32), ("ACC", 64, f32), ("A32", 32, f32),
+    ("KG", 16, i32), ("CODE", 16, i32), ("L1", 16, i32), ("L1U", 16, u16), ("H", 80, bf), ("S", 80, bf),
+    ("VV", 64, bf), ("Q", 64, bf), ("PY", 16, u16), ("X", B, f32), ("AG", 2, bf), ("AM", 1, f32), ("RT", B, f32),
+    ("G", B, f32), ("UT", B, f32), ("NO", B, bf), ("IX", 16, f32), ("IXU", 16, u16), ("SG", B, bf),
+    ("HX", NC, f32), ("MM", NC, f32), ("MS", NC, f32), ("MU", 12, u16), ("TW", NC, bf), ("TF", NC, f32),
 ]:
-    SCRATCH[_n] = ("sbuf", [128, _w], _d)
+    if _n not in (("DN", "DP") if CFG["still"] else ("BO2", "ZERO", "RT")):
+        SCRATCH[_n] = ("sbuf", [128, _w], _d)
 BANKS = ("K0", "KB1", "HB", "YB", "CB", "TB", "M1", "M2")
 for _n in BANKS:
-    SCRATCH[_n] = ("psum", [128, 512], f32)
-SEMAPHORES = ["qv", "qa", "qp", "qg"] + ["d%d" % i for i in range(90)] + ["ax%d" % t for t in range(R)] + \
+    SCRATCH[_n] = ("psum", [128, 1024], bf) if _n in ("YB", "CB") else ("psum", [128, 512], f32)
+SEMAPHORES = ["qv", "qa", "qp", "qg"] + ["d%d" % i for i in range(100)] + ["ax%d" % t for t in range(R)] + \
     ["ac%d" % t for t in range(R)] + ["lx%d" % t for t in range(R)] + ["lc%d" % t for t in range(R)] + \
     ["af%d" % t for t in range(R - 1)] + ["lf%d" % t for t in range(R - 1)]
 
 
+def place(succ, ways, key):
+    left = {i: 0 for i in succ}
+    for i in succ:
+        for j in succ[i]:
+            left[j] += 1
+    est, start, way, taken = {i: 0.0 for i in succ}, {}, {}, {}
+    ready = [i for i in succ if not left[i]]
+    while ready:
+        i = min(ready, key=lambda x: key[x])
+        ready.remove(i)
+        for n, segs in enumerate(ways[i]):
+            t, again = est[i], True
+            while again:
+                again = False
+                for r, off, ln in segs:
+                    los, his = taken.setdefault(r, ([], []))
+                    k = int(np.searchsorted(his, t + off + 1e-6))
+                    while k < len(los) and los[k] < t + off + ln - 1e-6:
+                        t, again, k = his[k] - off, True, k + 1
+            if i not in start or t < start[i]:
+                start[i], way[i] = t, n
+        for r, off, ln in ways[i][way[i]]:
+            los, his = taken[r]
+            k = int(np.searchsorted(his, start[i] + off + 1e-6))
+            los.insert(k, start[i] + off)
+            his.insert(k, start[i] + off + ln)
+        for j, lag in succ[i].items():
+            est[j] = max(est[j], start[i] + lag)
+            left[j] -= 1
+            if not left[j]:
+                ready.append(j)
+    return start, way, est
+
+
 def arrange(ops):
     n = len(ops)
-    last, readers, pred = {}, {}, []
+    last, readers, pred, uses = {}, {}, [], {}
     for i, (q, fn, rd, wr, own, c) in enumerate(ops):
         need = set()
         for t in rd:
             if t in last:
                 need.add(last[t])
-            if t in BANKS:
+            if t in BANKS or t[:2] == "M#":
                 need.update(x for x in readers.get(t, []) if ops[x][0] != q)
         for t in wr:
             if t in last:
@@ -64,60 +99,50 @@ def arrange(ops):
             need.update(readers.get(t, []))
         if fn is None:
             need.add(i - 1)
-        pred.append(sorted(need))
+        pred.append(need)
         for t in rd:
             readers.setdefault(t, []).append(i)
         for t in wr:
             last[t] = i
             readers[t] = []
-    succ = [[] for _ in range(n)]
+        for t in set(rd + wr):
+            if t[:2] == "M#":
+                uses.setdefault(t, []).append(i)
+    dur = [max(o[5][0], o[5][1] + o[5][2]) for o in ops]
+    segs = [([(o[0], 0.0, o[5][0])] if o[1] else []) + ([("E", o[5][1], o[5][2])] if o[5][2] else []) for o in ops]
+
+    head, off = list(range(n)), [0.0] * n
+    ways = {i: [segs[i]] for i in range(n)}
+    for some in uses.values():
+        for x, y in zip(some[:-1], some[1:]):
+            head[y], off[y] = some[0], off[x] + dur[x] + CFG["wake"]
+            del ways[y]
+        both = [(r, off[y] + o, ln) for y in some for r, o, ln in segs[y]]
+        ways[some[0]] = [both + [(bank, 0.0, off[some[-1]] + dur[some[-1]] + CFG["wake"])] for bank in BANKS[6:]]
+    succ = {i: {} for i in ways}
     for i in range(n):
         for j in pred[i]:
-            succ[j].append(i)
-    hold = [o[5][0] for o in ops]
-    wake = CFG["wake"]
-    level = [0.0] * n
-    for i in range(n - 1, -1, -1):
-        level[i] = sum(ops[i][5][:3]) + max([level[j] + wake for j in succ[i]] + [0.0])
-    level = [level[i] + 1000.0 * ops[i][5][3] for i in range(n)]
-    left = [len(x) for x in pred]
-    est = [0.0] * n
-    ready = {q: [] for q in "vapsgx"}
-    free = {q: 0.0 for q in "vapsgx"}
-    engines = 0.0
+            if head[i] != head[j]:
+                gap = 0.0 if ops[i][0] == ops[j][0] == "p" or ops[i][1] is None else CFG["wake"]
+                succ[head[j]][head[i]] = max(succ[head[j]].get(head[i], 0.0), off[j] + dur[j] + gap - off[i])
+    key, far = {}, {}
     for i in range(n):
-        if not left[i]:
-            ready[ops[i][0]].append(i)
-    order = []
-    while len(order) < n:
-        pick = None
-        for q, lst in ready.items():
-            if not lst:
-                continue
-            t0 = max(free[q], min(est[i] for i in lst))
-            c = max((i for i in lst if est[i] <= t0), key=lambda i: level[i])
-            soon = [i for i in lst if t0 < est[i] < t0 + hold[c] and
-                    level[i] - level[c] > CFG["look"] * hold[c] and est[i] - t0 < t0 + hold[c] - est[i]]
-            if soon:
-                c = max(soon, key=lambda i: level[i])
-            st = max(t0, est[c])
-            if pick is None or st < pick[0]:
-                pick = (st, q, c)
-        st, q, c = pick
-        ready[q].remove(c)
-        order.append(c)
-        free[q] = st + hold[c]
-        if ops[c][5][2]:
-            engines = max(engines, st + ops[c][5][1]) + ops[c][5][2]
-            end = engines
-        else:
-            end = st + max(hold[c], ops[c][5][1])
-        for j in succ[c]:
-            est[j] = max(est[j], end + (0.0 if (q == "p" and ops[j][0] == "p") or ops[j][1] is None else wake))
-            left[j] -= 1
-            if not left[j]:
-                ready[ops[j][0]].append(j)
-    return [ops[i] for i in order]
+        x = (ops[i][0], ops[i][5][3])
+        key[i] = 1000.0 * x[1] + far.get(x, 0.0)
+        far[x] = far.get(x, 0.0) + ops[i][5][0]
+    for i in sorted(ways, reverse=True):
+        key[i] = min([key[i]] + [key[j] - lag for j, lag in succ[i].items()])
+    start, way, est = place(succ, ways, key)
+    start = [start[head[i]] + off[i] for i in range(n)]
+    pick = {t: BANKS[6 + way[some[0]]] for t, some in uses.items()}
+    pace = {}
+    ends = sorted((start[i] + dur[i], i) for i in range(n) if ops[i][0] in "vap")
+    for i in range(n):
+        if ops[i][0] == "s" and start[i] > est[i] + CFG["slack"]:
+            k = int(np.searchsorted([x[0] for x in ends], start[i])) - 1
+            if k >= 0:
+                pace[i] = ends[k][1]
+    return sorted(range(n), key=lambda i: (start[i], i)), pick, pace, start, dur
 
 
 def build(g, T, ops):
@@ -127,7 +152,7 @@ def build(g, T, ops):
     clock, waits, used = {}, [], set()
     seq = {q: 0 for q in queues}
     totals = {}
-    for n, (q, fn, rd, wr, own, cost) in enumerate(ops):
+    for n, (q, fn, rd, wr, own) in enumerate(ops):
         if own is None:
             seq[q] += 1
             tok = ("q" + q, seq[q])
@@ -167,7 +192,7 @@ def build(g, T, ops):
     for s in ("qv", "qa", "qp", "qg"):
         for k, x in enumerate(sorted(c for (s2, c) in used if s2 == s)):
             count[(s, x)] = k + 1
-    for n, (q, fn, rd, wr, own, cost) in enumerate(ops):
+    for n, (q, fn, rd, wr, own) in enumerate(ops):
         if fn is None:
             continue
         tok, mine = waits[n]
@@ -188,29 +213,41 @@ def rank_program(g, core, T, topo):
     if me is None:
         return
     kinds = {f32: "f4", i32: "i4", bf: "i2", u16: "u2"}
-    shapes = [(n, "f8" if w == "psum" else kinds[d], tuple(sh)) for n, (w, sh, d) in SCRATCH.items()]
+    shapes = [(n, ("f8" if d == f32 else "c8") if w == "psum" else kinds[d], tuple(sh)) for n, (w, sh, d) in SCRATCH.items()]
     shapes += [(n, "i2", tuple(T[n].shape)) for n in ("cen", "pl", "jmp", "wk", "yc", "yx", "yz", "yn")]
     shapes += [(n, "i4", tuple(T[n].shape)) for n in ("ent", "nb", "ye")]
-    sizes = calls(g, core, me, np.recarray((1,), shapes)[0], T, topo, False)
-    ops = calls(g, core, me, T, T, topo, True)
-    build(g, T, arrange([o[:5] + (z[5],) for o, z in zip(ops, sizes)]))
+    order, pick, pace = arrange(calls(g, core, me, np.recarray((1,), shapes)[0], T, topo, None))[:3]
+    ops = calls(g, core, me, T, T, topo, pick)
+    for i, j in pace.items():
+        ops[i][2].append("pace%d" % i)
+        ops[j][3].append("pace%d" % i)
+    build(g, T, [(q, fn, [pick.get(t, t) for t in rd], [pick.get(t, t) for t in wr], own)
+                 for q, fn, rd, wr, own, c in [ops[i] for i in order]])
 
 
-def calls(g, core, me, T, G, topo, real):
+def calls(g, core, me, T, G, topo, pick):
     ops = []
-    nd = [0]
+    nd, nb_ = [0], [0]
     v, a, p = g.vector, g.scalar, g.tensor
-    NJ, C = CFG["nj"], CFG
+    C = CFG
+    real = pick is not None
     part_of = [""]
+    due = {"L": 0.0, "": 1000.0}
+    for t in range(0, R, 2):
+        due.update({x[0] + str(t + int(x[1])): y + C["two"] * t / 2 for x, y in C["due"].items()})
 
     def op(q, fn, rd, wr, own=None, cost=None):
-        ops.append((q, fn, list(rd), list(wr), own, (cost or (0.0, 0.0, 0.0)) +
-                    (C["lead"].get(part_of[0], 0.0) + C["lead"].get(part_of[0] + q, 0.0),)))
+        ops.append((q, fn, list(rd), list(wr), own, (cost or (0.0, 0.0, 0.0)) + (due[part_of[0]],)))
 
     def join(n):
         some = ops[-n:]
         del ops[-n:]
         op(some[0][0], [f for o in some for f in o[1]], some[0][2], some[0][3], None, (C["fix"] * 2 + 250.0 * C["f"], 0.0, 0.0))
+
+    def lend():
+        nb_[0] += 1
+        tag = "M#%d" % nb_[0]
+        return T[pick[tag] if real else "M1"], tag
 
     def ind(win, off):
         return win.indirect(off) if real else (win, off)
@@ -223,21 +260,27 @@ def calls(g, core, me, T, G, topo, real):
         elif isinstance(ins[0], tuple):
             c = C["g"] * out.shape[1]
         else:
-            c = ins[0].shape[1] * (0.5 if all(x.itemsize == 2 for x in [out] + ins) else 1.0)
+            c = ins[0].shape[1]
+            if all(x.itemsize == 2 or x.dtype.kind == "c" for x in [out] + ins):
+                c = c * (C["half"] if two and any(x.itemsize == 8 for x in ins) else 0.5)
             if two and all(x.itemsize < 8 for x in ins):
                 c = 2 * c
-        return (C["fix"] + max(20.0, c) * 0.83 * C["f"], 0.0, 0.0)
+        return (C["fix"] + max(64.0, c) * 0.83 * C["f"], 0.0, 0.0)
 
     def moved(rows, nbytes, engines):
         return (rows * C["row"] + nbytes / C["bw"]) / engines
 
-    def dma(q, pairs, rd, wr):
+    def dma(q, pairs, rd, wr, add=False):
         s = "d%d" % nd[0]
         nd[0] += 1
-        e = g.sync if q == "s" else g.scalar
-        cost = None if real else (60.0 * len(pairs), C["dma"],
-                                  sum(moved(max(o.shape[0], i.shape[0], 16), o.nbytes, 16) for o, i in pairs))
-        op(q, [lambda o=o, i=i: e.dma_start(o, i) for o, i in pairs], rd, wr, (s, 16 * len(pairs)), cost)
+        e = {"s": g.sync, "a": g.scalar, "g": g}[q]
+        cost = None if real else ((900.0 if q == "g" else 60.0) * len(pairs), C["dma"] + (500.0 if q == "g" else 0.0),
+                                  sum(moved(max(o.shape[0], i.shape[0], 16), o.nbytes * (2 if add else 1), 16) for o, i in pairs))
+        if add:
+            op(q, [lambda o=o, i=i: g.dma_start(o, i, accum_op=ALU.add, max_dma_last_dim=4096) for o, i in pairs], rd, wr,
+               (s, 16 * len(pairs)), cost)
+        else:
+            op(q, [lambda o=o, i=i: e.dma_start(o, i) for o, i in pairs], rd, wr, (s, 16 * len(pairs)), cost)
 
     def ts(out, in0, s1, s2, o0, o1, rd, wr):
         if s2 is None:
@@ -257,27 +300,35 @@ def calls(g, core, me, T, G, topo, real):
     def scan(out, d0, d1, rd, wr):
         op("v", [lambda: v.tensor_tensor_scan(out, d0, d1, 0.0, ALU.mult, ALU.add)], rd, wr, None, work(out, [d0, d1]))
 
-    def act(out, in_, func, rd, wr, bias=0.0, scale=1.0, acc=None):
+    def act(out, in_, func, rd, wr, bias=0.0, scale=1.0):
         cost = None if real else work(out, [in_, T.COL])
         if func == ACT.Copy:
             op("a", [lambda: a.activation(out, in_, func)], rd, wr, None, cost)
-        elif acc is not None:
-            op("a", [lambda: a.activation(out, in_, func, bias=bias, scale=scale, accum_out=acc)], rd, wr, None, cost)
         else:
             op("a", [lambda: a.activation(out, in_, func, bias=bias, scale=scale)], rd, wr, None, cost)
 
-    def mm(out, terms, bank, first=True, final=True):
+    def move(e, out, src, rd, wr):
+        if e == "v":
+            cp(out, src, rd, wr)
+        else:
+            act(out, src, ACT.Copy, rd, wr)
+
+    def mm(terms, bank, first=True, final=True, after=()):
         fns, rd = [], []
-        for n, (l, r, x) in enumerate(terms):
+        for n, (o, l, r, x) in enumerate(terms):
             st, sp = first and n == 0, final and n == len(terms) - 1
-            fns.append(lambda l=l, r=r, st=st, sp=sp: p.matmul(out, l, r, st, sp))
+            fns.append(lambda o=o, l=l, r=r, st=st, sp=sp: p.matmul(o, l, r, st, sp))
             rd += x
-        cost = None if real else (sum(max(64, out.shape[1]) * (4 if l.itemsize == 4 else 1) for l, r, x in terms)
+        cost = None if real else (sum(max(64, o.shape[1]) * (4 if l.itemsize == 4 else 1) for o, l, r, x in terms)
                                   * C["pe"] * C["f"], 0.0, 0.0)
-        op("p", fns, sorted(set(rd)), [bank], None, cost)
+        op("p", fns, sorted(set(rd)), [bank] + list(after), None, cost)
+
+    def turn(pairs, rd, bank):
+        op("p", [lambda o=o, i=i: p.transpose(o, i, T.ID[:, :]) for o, i in pairs], rd + ["ID"], [bank], None,
+           (128 * len(pairs) * C["pe"] * C["f"], 0.0, 0.0))
 
     def pool(fn, w, rd, wr):
-        op("g", [fn], rd, wr, None, (150.0 + 2 * w * 0.83 * C["f"], 0.0, 0.0))
+        op("g", [fn], rd, wr, None, ((150.0 + 2 * w * 0.83) * C["f"], 0.0, 0.0))
 
     def iota(name, lo, hi, pat, base=0, cm=0, integer=False, tag=None):
         if integer:
@@ -303,7 +354,8 @@ def calls(g, core, me, T, G, topo, real):
         ap = T.CT[:, own0 + lo:own0 + lo + w]
         op("g", [lambda: g.remote_dma_fused([RemoteDMATransfer(
             dst_ids=[ids[q] for q in peers], dma_engine_mask=full, remote_sem=G.sem["ac%d" % t], srcs=[ap], dsts=[ap, ap, ap])],
-            local_sem=G.sem["lc%d" % t])], rd, [], ("lc%d" % t, len(eng)), (500.0, C["rem"], moved(384, 768 * w, len(eng))))
+            local_sem=G.sem["lc%d" % t])], rd, [], ("lc%d" % t, len(eng)),
+           (500.0, C["rem"] * (2 if w == V else 1), moved(384, 768 * w, len(eng))))
         op("x", None, [], ["CTr"], ("ac%d" % t, 3 * len(eng)))
 
     def send_x(t):
@@ -340,16 +392,20 @@ def calls(g, core, me, T, G, topo, real):
     def scaled(name, src, w):
         act(T[name][:, :], T[src][:, :], ACT.Identity, [src], [name], scale=w)
 
-    def y_list(xlo, n, rd, bank):
-        c = n // 16
-        mm(T[bank][:, 0:c], [(sel("DW", r), T.XS[:, xlo + r:xlo + n:16], ["DW"] + rd) for r in range(16)], bank)
-        cp(T.HI[:, 0:c], T[bank][:, 0:c], [bank], ["HI"])
+    def y_make(xlo, t0, t1, rd):
+        n = (t1 - t0) * B
+        c, tags = n // 16, ["Y%d" % t for t in range(t0, t1)]
+        ps, bank = lend()
+        mm([(ps[:, 0:c], sel("DW", r), T.XS[:, xlo + r:xlo + n:16], ["DW"] + rd) for r in range(16)], bank, after=["HI"])
+        cp(T.HI[:, 0:c], ps[:, 0:c], [bank], ["HI"])
         ts(T.HI[:, 0:c], T.HI[:, 0:c], M - 1, None, ALU.bitwise_and, None, ["HI"], ["HI"])
         cp(T.HU[:, 0:c], T.HI[:, 0:c], ["HI"], ["HU"])
-        tt(T.DF[:, 0:n], ind(T.JM[:, :], T.HU[:, 0:c]), T.XS[:, xlo:xlo + n], ALU.subtract, ["JM", "HU"] + rd, ["DF"])
-
-    def y_abs(n, ylo, wr):
-        act(T.Y[:, ylo:ylo + n], T.DF[:, 0:n], ACT.Abs, ["DF"], wr)
+        for t in range(t0, t1):
+            lo = (t - t0) * B
+            tt(T.DF[:, lo:lo + B], ind(T.JM[:, :], T.HU[:, lo // 16:lo // 16 + 16]), T.XS[:, xlo + lo:xlo + lo + B], ALU.subtract,
+               ["JM", "HU"] + rd, ["DF%d" % (t - t0)])
+            act(blk("Y", t), T.DF[:, lo:lo + B], ACT.Abs, ["DF%d" % (t - t0)], ["Y%d" % t])
+        dma("g", [(T.YF[:, t0 * B:t1 * B], T.Y[:, t0 * B:t1 * B])], tags, ["YF%d" % t for t in range(t0, t1)])
 
     def nb_lists(b):
         nbi, tg = blk("NBI", b), "NBI%d" % b
@@ -357,49 +413,66 @@ def calls(g, core, me, T, G, topo, real):
         ts(blk("KO2", b), nbi, 1.0 / 1024, 193.0 - 511.5 / 1024, ALU.mult, ALU.add, [tg], ["KO2%d" % b])
         ts(T.A8[:, :], nbi, 1.0 / 256, 192.0 - 127.5 / 256, ALU.mult, ALU.add, [tg], ["A8"])
         cp(T.NBF[:, :], nbi, [tg], ["NBF"])
-        mm(T.M1[:, 0:B], [(T.IDF[:, :], T.NBF[:, :], ["IDF", "NBF"]), (T.ID8[:, :], T.A8[:, :], ["ID8", "A8"]),
-                          (T.ID10[:, :], blk("KO2", b), ["ID10", "KO2%d" % b]), (T.ID[:, :], T.K1[:, :], ["ID", "K1"])], "M1")
-        act(blk("TC", b), T.M1[:, 0:B], ACT.Identity, ["M1"], ["TC%d" % b], bias=256.0 * (16384 * 193 - 3840 * 192), scale=256.0)
+        ps, bank = lend()
+        o = ps[:, 0:B]
+        mm([(o, T.IDF[:, :], T.NBF[:, :], ["IDF", "NBF"]), (o, T.ID8[:, :], T.A8[:, :], ["ID8", "A8"]),
+            (o, T.ID10[:, :], blk("KO2", b), ["ID10", "KO2%d" % b]), (o, T.ID[:, :], T.K1[:, :], ["ID", "K1"]),
+            (o, T.IDB[:, :], T.ONES[:, 0:B], ["IDB", "ONES"])], bank)
+        act(blk("TC", b), o, ACT.Identity, [bank], ["TC%d" % b], bias=-127.5, scale=256.0)
 
-    def ent_split(lo, hi, tag, bank):
-        cp(T.EF[:, lo:hi], T.EI[:, lo:hi], ["EI" + tag], ["EF" + tag])
-        act(T.EH[:, lo:hi], T.EF[:, lo:hi], ACT.Copy, ["EF" + tag], ["EH" + tag])
-        mm(T[bank][:, 0:hi - lo], [(T.IDF[:, :], T.EF[:, lo:hi], ["IDF", "EF" + tag]),
-                                   (T.IDM[:, :], T.EH[:, lo:hi], ["IDM", "EH" + tag])], bank)
-        act(T.EL[:, lo:hi], T[bank][:, 0:hi - lo], ACT.Copy, [bank], ["EL" + tag])
+    def ent_split(b):
+        cp(blk("EF", b), blk("EI", b), ["EI%d" % b], ["EF%d" % b])
+        act(blk("EH", b), blk("EF", b), ACT.Copy, ["EF%d" % b], ["EH%d" % b])
+        ps, bank = lend()
+        o = ps[:, 0:B]
+        mm([(o, T.IDF[:, :], blk("EF", b), ["IDF", "EF%d" % b]), (o, T.IDM[:, :], blk("EH", b), ["IDM", "EH%d" % b])], bank)
+        act(blk("EL", b), o, ACT.Copy, [bank], ["EL%d" % b])
+        w = slice(b * K * B, (b + 1) * K * B)
+        dma("s", [(T.W[0::16, w], blk("EH", b)), (T.W[1::16, w], blk("EL", b))], ["EH%d" % b, "EL%d" % b],
+            ["W%d" % b] + ["Wf%d" % x for x in range(4 * b, 4 * b + 4)])
 
-    def ent_place(b0, b1, tags):
-        pairs = []
-        for b in range(b0, b1):
-            w = slice(b * K * B, (b + 1) * K * B)
-            pairs += [(T.W[0::16, w], blk("EH", b)), (T.W[1::16, w], blk("EL", b))]
-        dma("s", pairs, ["EH" + x for x in tags] + ["EL" + x for x in tags],
-            ["W%d" % b for b in range(b0, b1)] + ["Wf%d" % x for x in range(4 * b0, 4 * b1)])
+    def w_fill(x0, x1):
+        for x in range(x0, x1):
+            lo, e = V * x, C["fill"][x]
+            if e == "g":
+                iota("W", lo, lo + V, [[0, V]], 1, tag="Wf%d" % x)
+            elif e == "v":
+                fill(T.W[:, lo:lo + V], 1.0, ["Wf%d" % x])
+            else:
+                dma("s", [(T.W[:, lo:lo + V], T.ONES[:, :])], ["ONES"], ["Wf%d" % x])
 
     def e_lists(t):
         b = t % 4
         for lo, hi in zip(C["cut"][:-1], C["cut"][1:]):
-            mm(T.M2[:, 0:hi - lo], [(sel("DE", r), T.W[:, b * K * B + 16 * lo + r:b * K * B + 16 * hi:16], ["DE", "W%d" % b])
-                                    for r in range(16)], "M2")
-            cp(T.EU[:, lo:hi], T.M2[:, 0:hi - lo], ["M2"], ["EU%d" % j for j in range(lo // 32, hi // 32)])
+            ps, bank = lend()
+            tags = ["EU%d" % j for j in range(lo // 32, hi // 32)]
+            mm([(ps[:, 0:hi - lo], sel("DE", r), T.W[:, b * K * B + 16 * lo + r:b * K * B + 16 * hi:16], ["DE", "W%d" % b])
+                for r in range(16)], bank, after=tags)
+            cp(T.EU[:, lo:hi], ps[:, 0:hi - lo], [bank], tags)
 
     def n_tile(t):
         b = t % 4
         dma("s", [(T.NN[:, :], T.W[2::16, b * K * B:(b + 1) * K * B])], ["W%d" % b], ["NN"])
 
     def ucalc(t):
-        mm(T.M1[:, 0:B], [(T.BO[:, :], blk("Y", t), ["BO", "Y%d" % t])], "M1")
-        act(T.UF[:, :], T.M1[:, 0:B], ACT.Identity, ["M1"], ["UF"], bias=192.0 - 31.5 / 64, scale=1.0 / 64)
-        mm(T.M1[:, B:2 * B], [(T.BO[:, :], blk("Y", t), ["BO", "Y%d" % t]), (T.ID64[:, :], T.UF[:, :], ["ID64", "UF"])], "M1")
-        act(T.U[:, :], T.M1[:, B:2 * B], ACT.Identity, ["M1"], ["U"], bias=64.0 * 192)
+        ps, bank = lend()
+        mm([(ps[:, 0:B], T.BO[:, :], blk("Y", t), ["BO", "Y%d" % t])], bank, after=["UF"])
+        act(T.UF[:, :], ps[:, 0:B], ACT.Identity, [bank], ["UF"], bias=192.0 - 31.5 / 64, scale=1.0 / 64)
+        ps, bank = lend()
+        o, u = ps[:, 0:B], "U%d" % (t % 2)
+        mm([(o, T.BO[:, :], blk("Y", t), ["BO", "Y%d" % t]), (o, T.ID64[:, :], T.UF[:, :], ["ID64", "UF"])], bank, after=[u])
+        act(blk("U", t % 2), o, ACT.Identity, [bank], [u], bias=64.0 * 192)
+
+    def twice(src, c, rd, stage, bank):
+        turn([(T[bank][:, 2 * B + h:2 * B + h + 128], T[src][:, c + h:c + h + 128]) for h in (0, 128)], rd, bank)
+        move(C["evac"], T[stage][:, :], blk(bank, 2), [bank], [stage])
+        turn([(T[bank][:, h:h + 128], T[stage][:, h % B:h % B + 128]) for h in range(0, 2 * B, 128)], [stage], bank)
 
     def yrep(t):
-        for h in (0, 1):
-            mm(blk("YB", h), [(T.ID[:, :], blk("Y", t), ["ID", "Y%d" % t])], "YB")
+        twice("Y", B * t, ["Y%d" % t], "YT", "YB")
 
     def crep(t):
-        for h in (0, 1):
-            mm(blk("CB", h), [(T.ID[:, :], cown(t), ["ID", "CTo%d" % (t % 4)])], "CB")
+        twice("CT", own0 + B * (t % 4), ["CTo%d" % (t % 4)], "CTT", "CB")
 
     def tiles_n(t):
         dma("s", [(T.AN[:, 0:B], cown(t))], ["CTo%d" % (t % 4)], ["ANo"])
@@ -408,102 +481,105 @@ def calls(g, core, me, T, G, topo, real):
         ap = "AP%d" % (t % 2)
         dma("s", [(blk(ap, 16), cown(t)), (blk(ap, 17), blk("Y", t))], ["CTo%d" % (t % 4), "Y%d" % t], [ap + "x"])
 
-    def bounds(t):
-        act(blk("TB", 0), cown(t), ACT.Identity, ["CTo%d" % (t % 4)], ["TB"], bias=1.0)
-        act(T.CM[:, :], cown(t), ACT.Identity, ["CTo%d" % (t % 4)], ["CM"], bias=-1.0)
-
     def payload(t):
-        act(T.PW[:, :], T.PB[:, :], ACT.Identity, ["PB", "BC", "c14"], ["PW"], bias=T.BC[:, t:t + 1], scale=col(14))
+        if t < 4:
+            ts(T.PW[:, :], T.PB[:, :], col(14), T.BC[:, t:t + 1], ALU.mult, ALU.add, ["PB", "BC", "c14"], ["PW"])
+        elif t == 4:
+            ts(T.PW[:, :], T.PB[:, :], col(14), None, ALU.mult, None, ["PB", "c14"], ["PW"])
+        else:
+            ts(T.PF[:, :], T.PB[:, :], col(7), None, ALU.mult, None, ["PB", "c7"], ["PF"])
 
     def template(t):
-        act(T["XB%d" % t][:, 144:336], T.TPI[:, :], ACT.Identity, ["TPI", "c7"], ["XB%d" % t], bias=-127.5, scale=col(7))
-        act(T.YF[:, :], blk("Y", t), ACT.Identity, ["Y%d" % t], ["YF"], bias=-127.5)
+        dma("s", [(T["XB%d" % t][:, 144:336], T.TPL[:, :])], ["TPL"], ["XB%d" % t])
 
     def acount():
-        mm(T.M1[:, 0:16], [(T.ONE[:, :], T.GO[:, :], ["ONE", "GO"])], "M1")
-        act(T.QB[:, :], T.M1[:, 0:16], ACT.Identity, ["M1"], ["QB", "AF"], bias=1572864.0, scale=2048.0, acc=col(8))
-        act(T.AG[:, :], col(8), ACT.Identity, ["AF"], ["AG"], bias=-31.5 / 64, scale=1.0 / 131072)
-        act(T.AM[:, :], T.AG[:, :], ACT.Identity, ["AF", "AG"], ["AM"], bias=col(8), scale=-131072.0)
+        ps, bank = lend()
+        o = ps[:, 0:1]
+        mm([(o, T.ONES[:, 0:128], T.S[:, 79:80], ["ONES", "S"]), (o, T.ONES[:, 0:128], T.C96[:, 0:1], ["C96"])], bank)
+        act(T.AG[:, 0:1], o, ACT.Identity, [bank], ["AG"], bias=-2048.0 * 31.5, scale=-2048.0)
+        act(T.AM[:, :], o, ACT.Identity, [bank, "AG"], ["AM"], bias=T.AG[:, 0:1], scale=2048.0)
 
     def arrive(t):
-        xb, tg, mu = T["XB%d" % t], ["XB%d" % t, "XL%d" % t], "MU%d" % (t % 2)
+        xb, tg = T["XB%d" % t], ["XB%d" % t, "XL%d" % t]
         ts(T.HX[:, :], xb[:, 0:NC], MAGIC, MAGIC, ALU.add, ALU.subtract, tg, ["HX"])
-        mm(T.M2[:, 0:NC], [(T.BOS[:, :], T.HX[:, :], ["BOS", "HX"])], "M2")
-        tt(T.MM[:, :], T.M2[:, 0:NC], T.DIAG[:, 0:NC], ALU.mult, ["M2", "DIAG"], ["MM"])
+        ps, bank = lend()
+        mm([(ps[:, 0:NC], T.BOS[:, :], T.HX[:, :], ["BOS", "HX"])], bank)
+        tt(T.MM[:, :], ps[:, 0:NC], T.DIAG[:, :], ALU.mult, [bank, "DIAG"], ["MM"])
         scan(T.MS[:, :], T.SEG[:, :], T.MM[:, :], ["SEG", "MM"], ["MS"])
-        cp(T[mu][:, :], T.MS[:, 15:NC:16], ["MS"], [mu])
-        mm(T.M2[:, NC:2 * NC], [(T.IDF[:, :], xb[:, 0:NC], ["IDF"] + tg), (T.IDFM[:, :], T.HX[:, :], ["IDFM", "HX"])], "M2")
+        cp(T.MU[:, :], T.MS[:, 15:NC:16], ["MS"], ["MU"])
+        ps, bank = lend()
+        o = ps[:, 0:NC]
+        mm([(o, T.IDF[:, :], xb[:, 0:NC], ["IDF"] + tg), (o, T.IDFM[:, :], T.HX[:, :], ["IDFM", "HX"])], bank, after=["PL"])
         if n1:
-            act(T.PL[:, NC * t + NC - n1:NC * t + NC], T.M2[:, NC:NC + n1], ACT.Identity, ["M2"], ["PL"], bias=127.5)
-        act(T.PL[:, NC * t:NC * t + NC - n1], T.M2[:, NC + n1:2 * NC], ACT.Identity, ["M2"], ["PL"], bias=127.5)
+            act(T.PL[:, NC * t + NC - n1:NC * t + NC], ps[:, 0:n1], ACT.Identity, [bank], ["PL"], bias=127.5)
+        act(T.PL[:, NC * t:NC * t + NC - n1], ps[:, n1:NC], ACT.Identity, [bank], ["PL"], bias=127.5)
         join(2 if n1 else 1)
 
     def arrive_w(t):
-        mu = "MU%d" % (t % 2)
         if t < 4:
-            cp(ind(T.W[:, :], T[mu][:, :]), T.PW[:, :], [mu, "PW"], WALL)
+            cp(ind(T.W[:, :], T.MU[:, :]), T.PW[:, :], ["MU", "PW"], WALL)
+            return
+        tw = "TW" if t == 4 else "TF"
+        ts(T[tw][:, :], ind(T.W[:, :], T.MU[:, :]), col(5), T.BC[:, t:t + 1], ALU.mult, ALU.add, ["MU", "c5", "BC"] + WALL, [tw])
+        if t == 4:
+            tt(ind(T.W[:, :], T.MU[:, :]), T.TW[:, :], T.PW[:, :], ALU.add, ["MU", "PW", "TW"], WALL)
         else:
-            ts(T.TW[:, :], ind(T.W[:, :], T[mu][:, :]), col(5), col(5), ALU.mult, ALU.add, [mu, "c5"] + WALL, ["TW"])
-            tt(ind(T.W[:, :], T[mu][:, :]), T.TW[:, :], T.PW[:, :], ALU.add, [mu, "PW", "TW"], WALL)
+            tt(ind(T.WF[:, :], T.MU[:, :]), T.TF[:, :], T.PF[:, :], ALU.add, ["MU", "PF", "TF"], ["WFe", "WFn"])
 
-    def arrive_wf(t):
-        mu = "MU%d" % (t % 2)
-        ts(ind(T.WF[:, :], T[mu][:, :]), T.PB[:, :], 1.0, float(NC * t), ALU.mult, ALU.add, [mu, "PB"], ["WF"])
-
-    def gp(t, j):
-        ap = "AP%d" % (t % 2)
-        act(T[ap][:, 2 * B * j:2 * B * (j + 1)], ind(T.PL[:, :], T.EU[:, 32 * j:32 * j + 32]), ACT.Copy,
-            ["PL", "EU%d" % j], ["%s_%d" % (ap, j)])
-
-    def mp(t, j):
-        ap, ct = "AP%d" % (t % 2), "CTo%d" % (t % 4)
+    def entry_piece(t, j):
+        ap, ct, c0 = "AP%d" % (t % 2), "CTo%d" % (t % 4), own0 + B * (t % 4)
         tg, ks, sl = "%s_%d" % (ap, j), (2 * j, 2 * j + 1), slice(2 * B * j, 2 * B * (j + 1))
-        terms = [(T.BOM[:, :], cown(t), ["BOM", ct])] if j == 0 else []
-        if j < 8 - NJ[t]:
-            terms += [(sel("DN", k), blk(ap, k), ["DN", tg]) for k in ks]
-            mm(T.HB[:, 0:B], terms, "HB", j == 0, False)
-            tt(T.MP[:, sl], T[ap][:, sl], T.CB[:, :], ALU.max, [tg, "CB"], ["MP%d" % j])
-            mm(T.HB[:, 0:B], [(sel("DP", k), blk("MP", k), ["DP", "MP%d" % j]) for k in ks], "HB", False, j == 7)
+        move(C["pv"][t][j], T[ap][:, sl], ind(T.PL[:, :], T.EU[:, 32 * j:32 * j + 32]), ["PL", "EU%d" % j], [tg])
+        if C["still"]:
+            def sums(name, w, x):
+                return [(T.HB[:, h + k:h + 128:16], T[name][:, B * k + h:B * k + h + 128], w, x) for k in ks for h in (0, 128)]
+            terms = []
+            if j == 0:
+                terms = [(T.HB[:, 0:B], T.ID[:, :], T.ZERO[:, :], ["ID", "ZERO"])] + \
+                    [(T.HB[:, h:h + 128], T.CT[:, c0 + h:c0 + h + 128], T.BOM[:, :], ["BOM", ct]) for h in (0, 128)]
+            mm(terms + sums(ap, T.BOM[:, 0::16], ["BOM", tg]), "HB", j == 0, False)
+            tt(T.MP[:, sl], T[ap][:, sl], T.CB[:, 0:2 * B], ALU.max, [tg, "CB"], ["MP%d" % j])
+            mm(sums("MP", T.BO2[:, :], ["BO2", "MP%d" % j]), "HB", False, j == 7)
         else:
-            bank = "M1"
-            for h in (0, 1):
-                mm(blk(bank, h), [(T.IDM[:, :], cown(t), ["IDM", ct]), (T.ID[:, :], blk(ap, ks[h]), ["ID", tg])], bank)
-            act(T.MP[:, sl], T[bank][:, :], ACT.Abs, [bank], ["MP%d" % j])
-            terms += [(sel("D1", k), cown(t), ["D1", ct]) for k in ks]
-            mm(T.HB[:, 0:B], terms, "HB", j == 0, False)
-            mm(T.HB[:, 0:B], [(sel("D1", k), blk("MP", k), ["D1", "MP%d" % j]) for k in ks], "HB", False, j == 7)
+            o = T.HB[:, 0:B]
+            terms = [(o, T.BOM[:, :], cown(t), ["BOM", ct])] if j == 0 else []
+            mm(terms + [(o, sel("DN", k), blk(ap, k), ["DN", tg]) for k in ks], "HB", j == 0, False)
+            tt(T.MP[:, sl], T[ap][:, sl], T.CB[:, 0:2 * B], ALU.max, [tg, "CB"], ["MP%d" % j])
+            mm([(o, sel("DP", k), blk("MP", k), ["DP", "MP%d" % j]) for k in ks], "HB", False, j == 7)
 
     part_of[0] = "L"
     dma("s", [(T.CT[:, own0:own0 + V], T.cen[:, :])], [], CTALL[:4])
+    send_c(0, V, 5, CTALL[:4])
     part_of[0] = ""
-    dma("s", [(blk("XS", 0), T.wk[:, 0:B])], [], ["XS0"])
     dma("s", [(T.JM[:, :], T.jmp[:, :])], [], ["JM"])
-    dma("s", [(blk("NBI", 0), T.nb[:, 0:B])], [], ["NBI0"])
-    dma("s", [(blk("EI", 0), T.ent[:, 0:K * B])], [], ["EIa"])
+    dma("s", [(T.PL[:, :], T.pl[:, :])], [], ["PL"])
+    for b0, b1 in ((0, 1), (1, 4)):
+        dma("s", [(blk("EI", b), T.ent[:, b * K * B:(b + 1) * K * B]) for b in range(b0, b1)], [], ["EI%d" % b for b in range(b0, b1)])
+        dma("s", [(T.XS[:, b0 * B:b1 * B], T.wk[:, b0 * B:b1 * B])], [], ["XS%d" % b for b in range(b0, b1)])
+        dma("s", [(T.NBI[:, b0 * B:b1 * B], T.nb[:, b0 * B:b1 * B])], [], ["NBI%d" % b for b in range(b0, b1)])
     iota("PI", 0, 4, [[0, 4]], 0, 1, True)
     iota("X143", 0, 144, [[1, 144]])
     iota("XG", 0, 128, [[1, 8], [0, 16]])
+    fill(T.ONES[:, :], 1.0, ["ONES"])
+    w_fill(0, 4)
     iota("KO1", 0, B, [[8, B]], -192)
-    send_c(0, V, 5, CTALL[:4])
-    dma("s", [(T.PL[:, :], T.pl[:, :])], ["CTr"], ["PL"])
-    dma("s", [(blk("EI", b), T.ent[:, b * K * B:(b + 1) * K * B]) for b in (1, 2, 3)], ["CTr"], ["EIb", "EIc"])
-    dma("s", [(T.XS[:, B:V], T.wk[:, B:V])], ["CTr"], ["XS1", "XS2", "XS3"])
-    dma("s", [(T.NBI[:, B:V], T.nb[:, B:V])], ["CTr"], ["NBI1", "NBI2", "NBI3"])
     iota("K1", 0, B, [[512, 8], [-256, 2], [0, 16]], 256)
     iota("J16", 0, B, [[0, 16], [1, 16]])
     iota("C16", 0, 16, [[16, 16]])
     iota("OC", 0, 16 * (N - me), [[1, N - me], [0, 16]], me + 1)
     if me:
         iota("OC", 16 * (N - me), 64, [[1, me], [0, 16]], 1)
-    join(2 if me else 1)
-    iota("NDI", 0, 64, [[CAP, 4], [-16, 16]], 63)
+    iota("OC", 64, 80, [[0, 16]], 0)
+    join(3 if me else 2)
+    iota("NDC", 0, 64, [[CAP, 4], [-16, 16]], 64)
+    iota("THR", 0, 64, [[CAP, 4], [-16, 16]], 48)
     iota("TPI", 0, NC, [[0, 4], [256, CAP]], 256 * (K * V + CAP * me))
     if n1:
         iota("PB", 0, n1, [[1, n1]], NC - n1)
     iota("PB", n1, NC, [[1, NC - n1]], 0)
     join(2 if n1 else 1)
     iota("BI", 0, 8, [[NC, 8]])
-    ts(T.PJ[:, :], T.PI[:, :], 15, None, ALU.bitwise_and, None, ["PI"], ["PJ"])
+    ts(T.PJ[:, 0:4], T.PI[:, :], 15, None, ALU.bitwise_and, None, ["PI"], ["PJ"])
     cp(col(1), T.PI[:, 0:1], ["PI"], ["c1"])
     cp(col(0), T.PJ[:, 0:1], ["PJ"], ["c0"])
     ts(col(2), col(1), col(0), 15.0, ALU.subtract, ALU.add, ["c0", "c1"], ["c2"])
@@ -513,59 +589,58 @@ def calls(g, core, me, T, G, topo, real):
     dmat("DW", col(3), ["c3"])
     ts(T.IDF[:, :], T.X143[:, 0:128], col(1), None, ALU.is_equal, None, ["X143", "c1"], ["IDF"])
     dmat("D1", 1.0)
+    dmat("DE", col(4), ["c4"])
     ts(col(6), col(2), -15.0, 0.0625, ALU.add, ALU.mult, ["c2"], ["c6"])
     ts(T.BOF[:, :], T.XG[:, :], col(6), None, ALU.is_equal, None, ["XG", "c6"], ["BOF"])
     for nm, src, w in [("ID", "IDF", 1.0), ("IDM", "IDF", -1.0), ("DA", "D1", -2048.0), ("DM", "D1", 4096.0),
                        ("BOM", "BOF", -1.0), ("B64", "BOF", 64.0), ("ID8", "IDF", 3840.0), ("ID10", "IDF", -16384.0),
-                       ("DN", "D1", -1.0), ("DP", "D1", 2.0)]:
+                       ("IDB", "IDF", 16384.0 * 193 - 3840.0 * 192), ("BO", "BOF", 1.0), ("DC", "D1", 256.0),
+                       ("ID64", "IDF", -64.0), ("IDFM", "IDF", -1.0), ("BOS", "BOF", 1.0 / 256)]:
         scaled(nm, src, w)
-    act(T.DE[:, :], T.D1[:, :], ACT.Identity, ["D1", "c4"], ["DE"], scale=col(4))
+    if C["still"]:
+        act(T.BO2[:, :], T.BOF[:, 0::16], ACT.Identity, ["BOF"], ["BO2"], scale=2.0)
+        fill(T.ZERO[:, :], 0.0, ["ZERO"])
+    else:
+        scaled("DN", "D1", -1.0)
+        scaled("DP", "D1", 2.0)
     pool(lambda: g.affine_select(T.LB[:, :], T.BOM[:, :], [[-1, 128]], ALU.is_ge, 0.0, 0, 1), 128, ["BOM"], ["LB"])
-    pool(lambda: g.affine_select(T.LM[:, :], T.LB[:, :], [[-1, 128]], ALU.not_equal, -256.0, 0, 1), 128, ["LB"], ["LM"])
+    pool(lambda: g.affine_select(T.LM[:, :], T.LB[:, :], [[-1, 128]], ALU.not_equal, -65.0, 0, 1), 128, ["LB"], ["LM"])
     pool(lambda: g.affine_select(T.TRI[:, :], T.B64[:, :], [[1, 128]], ALU.is_ge, 0.0, 0, -1), 128, ["B64"], ["TRI"])
-    fill(T.W[:, 0:K * B], 1.0, ["W0"])
-    y_list(0, B, ["XS0"], "M2")
-    y_abs(B, 0, ["Y0"])
-    ent_split(0, B, "a", "K0")
-    ent_place(0, 1, ["a"])
-    tiles_n(0)
-    yrep(0)
-    crep(0)
-    tiles_p(0)
-    nb_lists(0)
-    for nm, src, w in [("BO", "BOF", 1.0), ("DC", "D1", 256.0), ("ID64", "IDF", -64.0), ("IDFM", "IDF", -1.0),
-                       ("BOS", "BOF", 1.0 / 256)]:
-        scaled(nm, src, w)
     fill(T.AM[:, :], 0.0, ["AM"])
-    fill(T.ONE[:, :], 1.0, ["ONE"])
-    cp(T.REP[:, :], T.PJ[:, :], ["PJ"], ["REP"])
-    ts(T.DIAG[:, :], T.J16[:, :], col(0), None, ALU.is_equal, None, ["J16", "c0"], ["DIAG"])
+    fill(T.INI[:, :], BIG, ["INI"])
+    fill(T.C96[:, :], -96.0, ["C96"])
+    fill(T.MONE[:, :], -1.0, ["MONE"])
+    ts(T.REP[:, :], T.X143[:, 0:8], 0.0, col(0), ALU.mult, ALU.add, ["X143", "c0"], ["REP"])
+    ts(T.DIAG[:, :], T.J16[:, 0:NC], col(0), None, ALU.is_equal, None, ["J16", "c0"], ["DIAG"])
+    ts(T.X[:, :], T.J16[:, :], col(0), BIG, ALU.is_equal, ALU.mult, ["J16", "c0"], ["X"])
+    act(T.DMIN[:, :], T.X[:, :], ACT.Identity, ["X"], ["DMIN"], bias=-127.5)
     ts(T.SEG[:, :], T.J16[:, 0:NC], 0.0, None, ALU.not_equal, None, ["J16"], ["SEG"])
     ts(T.IB[:, :], T.C16[:, :], col(0), None, ALU.add, None, ["C16", "c0"], ["IB"])
-    ts(T.NDC[:, :], T.NDI[:, :], col(0), None, ALU.subtract, None, ["NDI", "c0"], ["NDC"])
     ts(T.I17[:, :], T.IB[:, :], 17.0 * B, None, ALU.add, None, ["IB"], ["I17"])
-    ts(T.DUM[:, :], T.IB[:, :], float(NC), None, ALU.add, None, ["IB"], ["DUM"])
-    ts(T.THR[:, :], T.NDC[:, :], CAP - 255.0, None, ALU.add, None, ["NDC"], ["THR"])
+    ts(col(8), col(0), -1.0, -float(NC), ALU.mult, ALU.add, ["c0"], ["c8"])
+    act(T.DG[:, :], T.IDF[:, :], ACT.Identity, ["IDF", "c8"], ["DG"], scale=col(8))
     ts(col(14), col(0), 1.0, None, ALU.is_equal, None, ["c0"], ["c14"])
     ts(col(5), col(0), 2.0, None, ALU.is_ge, None, ["c0"], ["c5"])
     ts(col(15), col(0), 2.0, 2.0, ALU.is_ge, ALU.mult, ["c0"], ["c15"])
     ts(T.BC[:, 0:4], T.BI[:, 0:4], col(7), col(15), ALU.mult, ALU.add, ["BI", "c7", "c15"], ["BC"])
-    ts(T.BC[:, 4:8], T.BI[:, 4:8], col(7), None, ALU.mult, None, ["BI", "c7"], ["BC"])
+    ts(T.BC[:, 4:8], T.BI[:, 4:8], col(7), col(5), ALU.mult, ALU.add, ["BI", "c7", "c5"], ["BC"])
+    act(T.TPL[:, :], T.TPI[:, :], ACT.Identity, ["TPI", "c7"], ["TPL"], bias=-127.5, scale=col(7))
+    ent_split(0)
     e_lists(0)
-    ent_split(B, 3 * B, "b", "M2")
-    ent_split(3 * B, V, "c", "M2")
+    crep(0)
+    y_make(0, 0, 1, ["XS0"])
+    tiles_n(0)
+    yrep(0)
+    tiles_p(0)
+    nb_lists(0)
     template(0)
-    bounds(0)
     ucalc(0)
     payload(0)
-    for x in range(4, 16):
-        if x >= 16 - C["pool"]:
-            w = V + (NC if x == 15 else 0)
-            iota("W", V * x, V * x + w, [[0, w]], 1, tag="Wf%d" % x)
-        else:
-            fill(T.W[:, V * x:V * (x + 1)], 1.0, ["Wf%d" % x])
-    ent_place(1, 4, ["b", "c"])
-    dma("s", [(T.WF[0::16, b * K * B:(b + 1) * K * B], blk("EF", b)) for b in range(4)], ["EFa", "EFb", "EFc"], ["WF"])
+    y_make(B, 1, 4, ["XS1", "XS2", "XS3"])
+    fill(T.W[:, K * V:WW], 1.0, ["Wf15"])
+    w_fill(4, 16)
+    for b in (1, 2, 3):
+        ent_split(b)
 
     for t in range(R):
         b = t % 4
@@ -576,117 +651,126 @@ def calls(g, core, me, T, G, topo, real):
         tt(T.MN[:, 0:B], T.AN[:, 0:B], T.YB[:, 0:B], ALU.max, ["ANo", "YB"], ["MNo"])
         for j in range(8):
             lo = B + 2 * B * j
-            act(T.AN[:, lo:lo + 2 * B], ind(T.CT[:, :], T.NBU[:, b * B + 32 * j:b * B + 32 * j + 32]), ACT.Copy,
-                CTALL + ["NBU%d" % b], ["AN%d" % j])
-            tt(T.MN[:, lo:lo + 2 * B], T.AN[:, lo:lo + 2 * B], T.YB[:, :], ALU.max, ["AN%d" % j, "YB"], ["MN%d" % j])
+            move(C["nv"][t][j], T.AN[:, lo:lo + 2 * B], ind(T.CT[:, :], T.NBU[:, b * B + 32 * j:b * B + 32 * j + 32]),
+                 CTALL + ["NBU%d" % b], ["AN%d" % j])
+            tt(T.MN[:, lo:lo + 2 * B], T.AN[:, lo:lo + 2 * B], T.YB[:, 0:2 * B], ALU.max, ["AN%d" % j, "YB"], ["MN%d" % j])
             if j % 2 == 1:
                 q = j // 2
                 bank = BANKS[q % 2]
                 c0, c1 = (0 if q == 0 else B + 4 * B * q), B + 4 * B * (q + 1)
                 w = (c1 - c0) // 16
-                ex = ["ANo", "MNo"] if q == 0 else []
                 out = T[bank][:, 0:w]
-                mm(out, [(sel("DA", r), T.AN[:, c0 + r:c1:16], ["DA", "AN%d" % (j - 1), "AN%d" % j] + ex) for r in range(16)],
-                   bank, True, False)
-                mm(T[bank][:, w - 64:w], [(T.ID[:, :], T.KO1[:, 64 * q:64 * q + 64], ["ID", "KO1"]),
-                                          (T.ID[:, :], T.KO2[:, b * B + 64 * q:b * B + 64 * q + 64], ["KO2%d" % b])], bank, False, False)
-                mm(out, [(sel("DM", r), T.MN[:, c0 + r:c1:16], ["DM", "MN%d" % (j - 1), "MN%d" % j] + ex) for r in range(16)],
-                   bank, False, True)
-            if t == 0 and j == 1:
-                y_list(B, 3 * B, ["XS1", "XS2", "XS3"], "M1")
-            if t > 0 and j == 1:
-                arrive_wf(t - 1)
-            if j in (2, 4, 6):
-                q = j // 2 - 1
-                bank = BANKS[q % 2]
+                mm([(out, sel("DA", r), T.AN[:, c0 + r:c1:16], ["DA", "AN%d" % (j - 1), "AN%d" % j] + ["ANo"] * (q == 0))
+                    for r in range(16)], bank, True, False)
+                o = T[bank][:, w - 64:w]
+                mm([(o, T.ID[:, :], T.KO1[:, 64 * q:64 * q + 64], ["ID", "KO1"]),
+                    (o, T.ID[:, :], T.KO2[:, b * B + 64 * q:b * B + 64 * q + 64], ["KO2%d" % b])], bank, False, False)
+                mm([(out, sel("DM", r), T.MN[:, c0 + r:c1:16], ["DM", "MN%d" % (j - 1), "MN%d" % j] + ["MNo"] * (q == 0))
+                    for r in range(16)], bank, False, True)
                 if q == 0:
-                    ts(T.TH[:, :], T[bank][:, 0:16], T.AM[:, :], None, ALU.subtract, None, [bank, "AM"], ["TH"])
-                    cp(T.ACC[:, :], T[bank][:, 16:80], [bank], ["ACC"])
-                    tt(T.ACC[:, 0:16], T.ACC[:, 0:16], T.TH[:, :], ALU.min, ["ACC", "TH"], ["ACC"])
+                    if C["th"] == "a":
+                        act(T.INI[:, 0:16], T.K0[:, 0:16], ACT.Identity, ["K0", "AM"], ["INI"], bias=T.AM[:, :])
+                    else:
+                        ts(T.INI[:, 0:16], T.K0[:, 0:16], T.AM[:, :], None, ALU.add, None, ["K0", "AM"], ["INI"])
+                    tt(T.ACC[:, :], T.K0[:, 16:80], T.INI[:, :], ALU.min, ["K0", "INI"], ["ACC"])
                 else:
-                    tt(T.ACC[:, :], T.ACC[:, :], T[bank][:, 0:64], ALU.min, [bank, "ACC"], ["ACC"])
-        part_of[0] = "T%d" % t
+                    tt(T.ACC[:, :], T[bank][:, 0:64], T.ACC[:, :], ALU.min, [bank, "ACC"], ["ACC"])
+        part_of[0] = "F%d" % t
         if nx:
             send_free(t)
-        tt(T.ACC[:, :], T.ACC[:, :], T.KB1[:, 0:64], ALU.min, ["KB1", "ACC"], ["ACC"])
+        part_of[0] = "T%d" % t
         tt(T.A32[:, :], T.ACC[:, 0:32], T.ACC[:, 32:64], ALU.min, ["ACC"], ["A32"])
         tt(T.KG[:, :], T.A32[:, 0:16], T.A32[:, 16:32], ALU.min, ["A32"], ["KG"])
         ts(T.CODE[:, :], T.KG[:, :], 7, None, ALU.bitwise_and, None, ["KG"], ["CODE"])
+        tt(T.H[:, :], ind(T.CODE[:, :], T.REP[:, 0:5]), T.OC[:, :], ALU.is_equal, ["CODE", "REP", "OC"], ["H"])
+        part_of[0] = "X%d" % t
+        scan(T.S[:, :], T.SEG[:, 0:80], T.H[:, :], ["SEG", "H"], ["S"])
+        o = T.K0[:, 0:64]
+        mm([(o, T.ID[:, :], T.NDC[:, :], ["ID", "NDC"]), (o, T.LM[:, :], T.H[:, 0:64], ["LM", "H"]),
+            (o, T.BO[:, :], T.S[:, 0:64], ["BO", "S"])], "K0")
         ts(T.L1[:, :], T.KG[:, :], 3, 255, ALU.logical_shift_right, ALU.bitwise_and, ["KG"], ["L1"])
-        tt(T.H[:, :], ind(T.CODE[:, :], T.REP[:, :]), T.OC[:, :], ALU.is_equal, ["CODE", "REP", "OC"], ["H"])
         cp(T.L1U[:, :], T.L1[:, :], ["L1"], ["L1U"])
-        scan(T.S[:, :], T.SEG[:, 0:64], T.H[:, :], ["SEG", "H"], ["S"])
-        mm(T.M2[:, 0:64], [(T.ID[:, :], T.NDC[:, :], ["ID", "NDC"]), (T.LM[:, :], T.H[:, :], ["LM", "H"]),
-                           (T.BO[:, :], T.S[:, :], ["BO", "S"])], "M2")
-        tt(T.X[:, :], ind(blk("TC", b), T.L1U[:, :]), T.DIAG[:, :], ALU.mult, ["TC%d" % b, "L1U", "DIAG"], ["X"])
-        tt(T.VV[:, :], T.M2[:, 0:64], T.THR[:, :], ALU.is_lt, ["M2", "THR"], ["VV"])
-        tt(T.Q[:, :], T.M2[:, 0:64], T.VV[:, :], ALU.mult, ["M2", "VV"], ["Q"])
-        tt(T.QA[:, :], T.Q[:, 0:32], T.Q[:, 32:64], ALU.add, ["Q"], ["QA"])
-        tt(T.QB[:, :], T.QA[:, 0:16], T.QA[:, 16:32], ALU.add, ["QA"], ["QB"])
-        tt(T.QC[:, :], T.QB[:, :], T.DUM[:, :], ALU.add, ["QB", "DUM"], ["QC"])
-        cp(T.PY[:, :], T.QC[:, :], ["QC"], ["PY"])
-        tt(ind(T["XB%d" % t][:, 144:XW_], T.PY[:, :]), T.X[:, :], T.YF[:, :], ALU.add, ["PY", "X", "YF"], ["XB%d" % t])
+        tt(T.VV[:, :], o, T.THR[:, :], ALU.is_lt, ["K0", "THR"], ["VV"])
+        tt(T.Q[:, :], o, T.VV[:, :], ALU.mult, ["K0", "VV"], ["Q"])
+        o = T.KB1[:, 0:16]
+        mm([(o, T.ID[:, :], T.C16[:, :], ["ID", "C16"]), (o, T.DG[:, :], T.MONE[:, :], ["DG", "MONE"])] +
+           [(o, T.DG[:, :], T.VV[:, 16 * d:16 * d + 16], ["VV"]) for d in range(4)], "KB1", True, False)
+        mm([(o, T.ID[:, :], T.Q[:, 16 * d:16 * d + 16], ["Q"]) for d in range(4)], "KB1", False, True)
+        tt(T.X[:, :], ind(blk("TC", b), T.L1U[:, :]), T.DMIN[:, :], ALU.min, ["TC%d" % b, "L1U", "DMIN"], ["X"])
+        cp(T.PY[:, :], o, ["KB1"], ["PY"])
+        tt(ind(T["XB%d" % t][:, 144:XW_], T.PY[:, :]), T.X[:, :], blk("YF", t), ALU.add, ["PY", "X", "YF%d" % t], ["XB%d" % t])
         send_x(t)
-        tt(T.GO[:, :], T.KG[:, :], T.TH[:, :], ALU.is_lt, ["KG", "TH"], ["GO"])
-        tt(T.KEY[:, :], T.KG[:, :], T.TH[:, :], ALU.is_ge, ["KG", "TH"], ["KEY"])
-        tt(T.BP[:, :], T.KEY[:, :], T.I17[:, :], ALU.mult, ["KEY", "I17"], ["BP"])
+        if nx:
+            part_of[0] = ""
+            acount()
+            if t in (1, 2):
+                y_make((t - 1) * B, t + 3, t + 4, ["XS%d" % (t - 1)])
+            yrep(t + 1)
+            tiles_n(t + 1)
+            template(t + 1)
+            if t < 3:
+                nb_lists(t + 1)
+            ucalc(t + 1)
         part_of[0] = "P%d" % t
         for j in range(8):
-            gp(t, j)
-            mp(t, j)
+            entry_piece(t, j)
         part_of[0] = "Q%d" % t
-        if t == 0:
+        if C["still"]:
+            act(T.RT[:, :], T.HB[:, 0:B], ACT.Relu, ["HB"], ["RT"], bias=2047.0, scale=-1.0)
+            for h in (0, 128):
+                mm([(T.HB[:, B + h:B + h + 128], T.RT[:, h:h + 128], T.IDF[:, :], ["RT", "IDF"])], "HB")
+            if t == 0:
+                cp(T.G[:, :], blk("HB", 1), ["HB"], ["G"])
+            else:
+                tt(T.G[:, :], blk("HB", 1), T.NN[:, :], ALU.mult, ["HB", "NN"], ["G"])
+        elif t == 0:
             act(T.G[:, :], T.HB[:, 0:B], ACT.Relu, ["HB"], ["G"], bias=2047.0, scale=-1.0)
-            y_abs(3 * B, B, ["Y1", "Y2", "Y3"])
         else:
-            act(T.M1[:, 0:B], T.HB[:, 0:B], ACT.Relu, ["HB"], ["M1"], bias=2047.0, scale=-1.0)
-            tt(T.G[:, :], T.M1[:, 0:B], T.NN[:, :], ALU.mult, ["M1", "NN"], ["G"])
-        mm(blk("TB", 1), [(T.BOF[:, :], T.G[:, :], ["BOF", "G"])], "TB")
-        mm(blk("HB", 1), [(T.TRI[:, :], T.G[:, :], ["TRI", "G"])], "HB")
-        tt(T.UT[:, :], blk("TB", 1), T.U[:, :], ALU.mult, ["TB", "U"], ["UT"])
-        tt(T.NO[:, :], blk("HB", 1), T.UT[:, :], ALU.is_le, ["HB", "UT"], ["NO"])
-        mm(T.M1[:, 0:16], [(T.ID[:, :], T.IB[:, :], ["ID", "IB"])] +
-           [(sel("DC", r), T.NO[:, r:B:16], ["DC", "NO"]) for r in range(16)], "M1")
-        part_of[0] = "A%d" % t
-        arrive(t)
-        if not nx:
-            arrive_wf(t)
-            dma("s", [(T.ye[:, :], T.WF[0::16, 0:K * V])], ["WF"], [])
-            arrive_w(t)
-            dma("s", [(T.yn[:, :], T.W[2::16, 0:K * V])], WALL, [])
-            dma("s", [(T.yz[:, 5 * NC:6 * NC], T.PL[:, 5 * NC:6 * NC])], ["PL"], [])
-        part_of[0] = "Q%d" % t
-        tt(T.IX[:, :], T.M1[:, 0:16], T.BP[:, :], ALU.max, ["M1", "BP"], ["IX"])
+            act(blk("HB", 1), T.HB[:, 0:B], ACT.Relu, ["HB"], ["HB"], bias=2047.0, scale=-1.0)
+            tt(T.G[:, :], blk("HB", 1), T.NN[:, :], ALU.mult, ["HB", "NN"], ["G"])
+        mm([(blk("TB", 0), T.BOF[:, :], T.G[:, :], ["BOF", "G"])], "TB")
+        mm([(blk("HB", 0), T.TRI[:, :], T.G[:, :], ["TRI", "G"])], "HB")
+        tt(T.UT[:, :], blk("TB", 0), blk("U", t % 2), ALU.mult, ["TB", "U%d" % (t % 2)], ["UT"])
+        tt(T.NO[:, :], blk("HB", 0), T.UT[:, :], ALU.is_le, ["HB", "UT"], ["NO"])
+        o = T.TB[:, B:B + 16]
+        mm([(o, T.ID[:, :], T.IB[:, :], ["ID", "IB"])] + [(o, sel("DC", r), T.NO[:, r:B:16], ["DC", "NO"]) for r in range(16)],
+           "TB", True, False)
+        part_of[0] = "C%d" % t
+        mm([(o, T.IDB[:, :], T.H[:, 64:80], ["IDB", "H"])], "TB", False, True)
+        tt(T.IX[:, :], o, T.I17[:, :], ALU.min, ["TB", "I17"], ["IX"])
         cp(T.IXU[:, :], T.IX[:, :], ["IX"], ["IXU"])
-        tt(T.CN[:, :], ind(T[ap][:, :], T.IXU[:, :]), T.CM[:, :], ALU.max, APALL + ["IXU", "CM"], ["CN"])
-        tt(cown(t), T.CN[:, :], blk("TB", 0), ALU.min, ["CN", "TB"], ["CTo%d" % b])
+        dv, dt_ = (blk("XS", b), "XS%d" % b) if nx else (T.DF[:, 0:B], "DF0")
+        tt(dv, ind(T[ap][:, :], T.IXU[:, :]), cown(t), ALU.subtract, APALL + ["IXU", "CTo%d" % b], [dt_])
+        ts(T.SG[:, :], dv, -1.0, 1.0, ALU.max, ALU.min, [dt_], ["SG"])
+        tt(cown(t), T.SG[:, :], T.CB[:, 0:B], ALU.add, ["SG", "CB"], ["CTo%d" % b])
         if nx:
             send_c(b * B, B, t, ["CTo%d" % b, "FR"])
-        act(blk("XS", b), ind(T[ap][:, :], T.IXU[:, :]), ACT.Copy, APALL + ["IXU"], ["XS%d" % b])
-        if not nx:
-            dma("a", [(T.yc[:, b * B:(b + 1) * B], cown(t))], ["CTo%d" % b], [])
+            part_of[0] = ""
+            dma("g", [(blk("XS", b), blk(ap, 16))], [ap + "x"], ["XS%d" % b], True)
+            crep(t + 1)
+        else:
+            act(blk("XS", b), ind(T[ap][:, :], T.IXU[:, :]), ACT.Copy, APALL + ["IXU"], ["XS%d" % b])
             dma("a", [(T.yx[:, b * B:(b + 1) * B], blk("XS", b))], ["XS%d" % b], [])
+            dma("s", [(T.yc[:, b * B:(b + 1) * B], cown(t))], ["CTo%d" % b], [])
+        part_of[0] = "A%d" % t
+        arrive(t)
+        arrive_w(t)
+        if not nx:
+            dma("s", [(T.ye[:, :], T.WF[0::16, 0:K * V])], ["WFe"], [])
+            dma("g", [(T.yn[:, :], T.WF[2::16, 0:K * V])], ["WFn"], [])
+            dma("s", [(T.yz[:, 5 * NC:6 * NC], T.PL[:, 5 * NC:6 * NC])], ["PL"], [])
             break
         s = t + 1
-        part_of[0] = "A%d" % t
-        arrive_w(t)
         e_lists(s)
-        part_of[0] = "W%d" % t
-        yrep(s)
-        crep(s)
-        tiles_n(s)
-        template(s)
-        acount()
-        if s < 4:
-            nb_lists(s)
-        bounds(s)
-        payload(s)
-        ucalc(s)
-        if t < 2:
-            y_list(t * B, B, ["XS%d" % t], "M2")
-            y_abs(B, (t + 4) * B, ["Y%d" % (t + 4)])
+        part_of[0] = ""
         n_tile(s)
+        payload(s)
         tiles_p(s)
+        if t == 4:
+            w = slice(0, K * V)
+            dma("g", [(T.WF[0::16, w], T.W[0::16, w])], WALL, ["WFe"])
+            dma("g", [(T.WF[2::16, w], T.W[2::16, w])], WALL, ["WFn"])
+            dma("g", [(T.WF[0::16, w], T.W[1::16, w])], WALL, ["WFe"], True)
         if t >= 2:
             dma("s", [(T.yc[:, b * B:(b + 1) * B], cown(t)), (T.yx[:, b * B:(b + 1) * B], blk("XS", b))],
                 ["CTo%d" % b, "XS%d" % b], [])

@@ -6,16 +6,18 @@ N, V, B, K, CAP, R, ZP, M = 4, 1024, 256, 16, 48, 6, 2048, 512
 NC = N * CAP
 WW = K * V + NC
 XW_ = 592
-MAGIC = 3221225472.0
+MAGIC = 6442450944.0
 BIG = 1.0e9
-CFG = {"nv": ["aavaaaaa", "avaaaaaa"] * 3, "pv": ["avaavvaa", "aaaaaava"] * 3, "cut": [0, 64, 128, 256], "fill": "vvvvggggdddddvvv",
-       "th": "v", "evac": "v", "slack": 300.0, "still": True, "half": 0.5,
-       "two": 38.7, "due": {"P0": 6.6, "N0": 13.6, "Q0": 14.8, "F0": 29.7, "T0": 44.1, "C0": 22.6, "X0": 25.9, "A0": 28.0,
-                            "N1": 37.7, "F1": 33.9, "T1": 34.0, "X1": 36.5, "P1": 31.8, "A1": 50.2, "Q1": 57.4, "C1": 52.3},
+CFG = {"nv": ["avaavaaa", "avaaaaaa"] * 3, "pv": ["avaavaaa", "aaaaaaaa"] * 3, "cut": [0, 64, 128, 192, 256], "fill": "vvvvgggggggddddd",
+       "slack": 300.0, "split": "vaaa", "half": 0.5,
+       "pl": "aaaaaa", "yt": "vvvvvv", "ct": "aaaaaa", "y": "vaaaaa", "dv": "vvvvvv", "nb": ["aa"] * 4,
        "f": 1.25, "g": 1.56, "s": 3.8, "pe": 0.42, "dma": 1800.0, "rem": 2000.0, "row": 40.0, "bw": 20.0,
        "wake": 70.0, "fix": 55.0}
+ORDER = """
+a:AN4'> a:AN5'> v:MN3'> v:ACC'> a:AN7'> v:MU> v:W> p:mPL> v:TW> v:PJ_ v:c1_ s:NN> g:YF> v:MN4'> p:a1'> p:m1'> v:ACC.1'> v:MN5'> a:AN6'> p:a2'> v:MONE_ v:c0_ v:Wf1_ v:IDF_ s:AP'> v:MN7'> a:ID_ p:CB_ v:HU'> v:c2_ v:D1_ v:c6_ a:DC_ v:Wf2_ g:WFe> p:mEU> a:AP0'> v:c3_ s:PL_ v:ONES_ v:DW_ a:ID10_ a:IDB_ v:EH0_ v:EL0_ s:W0_ v:MN6'> v:BOF_ a:IDM_ v:c4_ a:CTT_ p:mHI_ a:DA_ p:m2'> a:c8_ a:DG_ p:a3'> v:C96_ a:ID8_ a:BO_ a:BOS_ a:c5_ a:B64_ a:BO2_ v:ACC.2'> p:m3'> v:MP0'> v:ACC.3'> v:A32'> v:KG'> p:mEU.1> a:ID64_ v:CODE'> v:HI.1_ v:NBF_ v:H'> v:L1'> v:S'> v:HU_ p:hc'> p:CB.1_ a:AP1'> v:L1U'> p:mEU.2> a:A8_ a:DM_ p:rank'> v:DF0_ v:INI_ g:C16_ g:NDC_ s:outPL> a:Y0_ v:REP_ a:IB_ a:I17_ v:DE_ a:AP3'> v:Wf15_ v:NBU0_ v:VV'> v:Q'> p:mUF_ a:BOM_ a:KO20_ p:mU_ p:YB_ p:YB'> g:WFn> a:AP4'> a:AP5'> g:K1_ g:KO1_ v:SEG_ v:ZERO_ v:X'> p:pv'> g:BI_ v:BOH_ a:AP2'> g:Wf4_ v:AM_ p:pq'> v:PY'> v:XB'> v:YT'> v:DIAG_ v:YT_ g:lf'> p:mEU_ p:mEU.3> a:AP6'> v:MP1'> a:c15_ s:EI0_<< v:MP4'> v:MP2'> g:lx'> v:MP3'> s:EI1_ s:ANo_ v:MP5'> p:h0'> v:MP6'> a:AP7'> v:MP7'> p:YB.1'> g:THR_ p:mU'> p:h1'> p:h2'> a:PW> a:TPL_ v:HX'> a:BC_ p:h3'> p:h4'> p:h5'> p:h6'> p:h7'> a:RT'> p:back'> p:back.1'> v:G'> a:DF'> p:mMS'> a:A8'> p:CB'> p:mPL'> s:CTo0_<< s:XS0_<< v:MU'> v:MS.1'> a:CTT'> p:mA'> v:MASK_ p:all'> g:lc_ p:run'> v:W'> a:PW'> s:NN'> v:UT'> v:NO'> g:WFe.1> v:WFe'> p:mEU.1_ p:mEU'> a:AP0 v:AP1 p:mEU.1'> a:AP3 a:AP2 s:AP0x_ s:XS1_ s:Wf15_ p:cnt'> p:stay'> v:IX'> v:IXU'> a:XS'> v:DV'> v:SG'> p:mEU.2_ p:CB.1'> v:CTo'> p:mEU.3_ s:JM_<< s:NBI0_<< v:MP0 p:YB.1_ p:mEU.3'> p:mEU.2'> v:AP4 v:MP1 v:MP4 g:lc'> g:Wf7_ v:MP3 g:outWF'>> s:outCT'>> a:outXS'>> s:NBI1_ v:MP2 v:EF1_ a:AP6 a:AP5 v:MP6 v:MP5 a:AP7 a:EH1_ p:mTC'> v:EF2_ g:Wf5_ g:Wf6_ p:mHI a:AN0 p:hc p:h0 p:mTC_ g:TRI_ p:h1 p:h2 p:h3 p:h4 a:AN2 a:AN3 s:outPL'> v:MP7 p:h5 p:h6 p:mEL_ p:h7 a:RT v:AN1 a:EH2_ g:Wf8_ s:Wf13_ p:CB a:AN5 p:a0 s:Wf12_ g:OC_ v:MNo v:MN0 a:AN6 v:MN1 v:HI.1 v:AN4 v:MN2 v:EF3_ v:MN3 v:TRH_ v:MN4 p:m0 p:mHI.1_ g:Wf9_ g:Wf10_ a:AN7 p:a1 v:HU v:INI p:back p:back.1 p:m1 g:LB_ g:J16_< v:G v:NBU' v:HI.3_ v:ACC s:outWF'> g:lf p:mEL.1_ g:PI_< p:all a:EH3_ p:a2 v:NBF v:HU.1_ v:MN5 v:MN6 v:ACC.1 v:UT v:MN7 s:W1_ p:run a:DF0_ p:m2 v:NBU s:XB0_ p:a3 s:XB a:CTT a:IDFM_ s:Wf11_ v:NO s:XB' g:YF0_ g:X143_< s:Wf14_ g:XG_< v:ACC.2 a:DF1_ a:BC.1_ p:m3 a:A8 p:mY_ p:cnt a:DF2_ a:KO g:HX_< p:mY'> a:DF g:YF'> v:ACC.3 v:A32 v:KG v:CODE v:H v:L1 p:stay v:IX v:S v:IXU p:CB.1 p:mEL.2_ g:PB_ p:YB v:DV v:SG v:CTo p:rank v:VV g:LM_ v:L1U v:Q v:X p:mY.1_ v:Wf0_< p:mUF p:pv p:pq v:PY p:mA v:XB p:mY.2_ v:CUT_ v:YT a:XS a:PF<< a:PW_ g:lc p:mTC p:mU p:mUF' v:NBF' a:KO' v:AN1' p:YB.1 p:mY v:Wf3_< s:ANo v:MNo' g:lx a:AN0' v:MN0' v:MN1' s:W3_ a:AN2' a:AN3' s:W2_ p:mHI' v:HI.1' s:AP v:HX p:a0' s:ANo' p:m0' v:INI' s:outCT v:MN2' p:mMS g:YF1_
+"""
 
-f32, bf, i32, u16 = "float32", "bfloat16", "int32", "uint16"
+f32, bf, f16, i32, u16 = "float32", "bfloat16", "float16", "int32", "uint16"
 SCRATCH = {}
 for _n, _w, _d in [
     ("W", WW, bf), ("WF", WW, f32), ("CT", N * V, bf), ("PL", ZP, bf), ("JM", M, bf), ("XS", V, bf), ("Y", R * B, bf),
@@ -24,23 +26,22 @@ for _n, _w, _d in [
     ("EI", V, i32), ("EF", V, f32), ("EH", V, bf), ("EL", V, bf), ("EU", B, u16), ("NN", B, bf),
     ("XB0", XW_, f32), ("XB1", XW_, f32), ("XB2", XW_, f32), ("XB3", XW_, f32), ("XB4", XW_, f32), ("XB5", XW_, f32),
     ("PI", 4, i32), ("PJ", 8, i32), ("COL", 16, f32), ("REP", 8, u16), ("X143", 144, f32), ("XG", 128, f32), ("J16", B, f32),
-    ("DM", 144, bf), ("DA", 144, bf), ("DE", 144, bf), ("DW", 144, bf), ("DC", 144, bf), ("DP", 144, bf), ("DN", 144, bf),
-    ("D1", 144, bf), ("ID", 128, bf), ("IDM", 128, bf), ("IDF", 128, f32), ("IDFM", 128, f32), ("ID8", 128, bf),
-    ("ID10", 128, bf), ("ID64", 128, bf), ("IDB", 128, bf), ("DG", 128, bf), ("ONES", V, bf), ("ZERO", B, bf),
+    ("DM", 144, bf), ("DA", 144, bf), ("DE", 144, bf), ("DW", 144, bf), ("DC", 144, bf), ("GH", B, f16), ("TRH", 128, f16),
+    ("BOH", 128, f16), ("D1", 144, bf), ("ID", 128, bf), ("IDM", 128, bf), ("IDF", 128, f32), ("IDFM", 128, f32),
+    ("ID8", 128, bf), ("ID10", 128, bf), ("ID64", 128, bf), ("IDB", 128, bf), ("DG", 128, bf), ("ONES", V, bf), ("ZERO", B, bf),
     ("BO", 128, bf), ("BOM", 128, bf), ("BO2", 8, bf), ("BOF", 128, f32),
     ("BOS", 128, f32), ("B64", 128, f32), ("TRI", 128, f32), ("LB", 128, bf), ("LM", 128, bf),
-    ("DIAG", NC, f32), ("DMIN", B, f32), ("SEG", NC, f32), ("KO1", B, bf), ("K1", B, bf), ("OC", 80, f32), ("C16", 16, bf),
-    ("IB", 16, bf), ("I17", 16, f32), ("MONE", 16, bf), ("NDC", 64, bf), ("THR", 64, f32), ("C96", 2, bf),
-    ("TPI", NC, f32), ("TPL", NC, f32), ("PB", NC, bf), ("PW", NC, bf), ("PF", NC, f32), ("BI", 8, f32), ("BC", 8, f32),
+    ("MASK", NC, bf), ("DIAG", B, f32), ("SEG", 80, bf), ("CUT", NC, f32), ("KO1", B, bf), ("K1", B, bf), ("OC", 80, f32),
+    ("C16", 16, bf), ("IB", 16, bf), ("I17", 16, f32), ("MONE", 32, bf), ("NDC", 64, bf), ("THR", 64, f32),
+    ("TPL", NC, f32), ("PB", NC, bf), ("PW", NC, bf), ("PF", NC, f32), ("BI", 8, f32), ("BC", 8, f32),
     ("HI", 48, i32), ("HU", 48, u16), ("DF", 768, bf), ("UF", B, bf), ("U", 2 * B, bf), ("YT", B, bf), ("CTT", B, bf),
     ("INI", 64, f32), ("ACC", 64, f32), ("A32", 32, f32),
     ("KG", 16, i32), ("CODE", 16, i32), ("L1", 16, i32), ("L1U", 16, u16), ("H", 80, bf), ("S", 80, bf),
     ("VV", 64, bf), ("Q", 64, bf), ("PY", 16, u16), ("X", B, f32), ("AG", 2, bf), ("AM", 1, f32), ("RT", B, f32),
     ("G", B, f32), ("UT", B, f32), ("NO", B, bf), ("IX", 16, f32), ("IXU", 16, u16), ("SG", B, bf),
-    ("HX", NC, f32), ("MM", NC, f32), ("MS", NC, f32), ("MU", 12, u16), ("TW", NC, bf), ("TF", NC, f32),
+    ("HX", NC, f32), ("MS", NC, f32), ("DV", B, bf), ("MU", 12, u16), ("TW", NC, bf),
 ]:
-    if _n not in (("DN", "DP") if CFG["still"] else ("BO2", "ZERO", "RT")):
-        SCRATCH[_n] = ("sbuf", [128, _w], _d)
+    SCRATCH[_n] = ("sbuf", [128, _w], _d)
 BANKS = ("K0", "KB1", "HB", "YB", "CB", "TB", "M1", "M2")
 for _n in BANKS:
     SCRATCH[_n] = ("psum", [128, 1024], bf) if _n in ("YB", "CB") else ("psum", [128, 512], f32)
@@ -49,44 +50,13 @@ SEMAPHORES = ["qv", "qa", "qp", "qg"] + ["d%d" % i for i in range(100)] + ["ax%d
     ["af%d" % t for t in range(R - 1)] + ["lf%d" % t for t in range(R - 1)]
 
 
-def place(succ, ways, key):
-    left = {i: 0 for i in succ}
-    for i in succ:
-        for j in succ[i]:
-            left[j] += 1
-    est, start, way, taken = {i: 0.0 for i in succ}, {}, {}, {}
-    ready = [i for i in succ if not left[i]]
-    while ready:
-        i = min(ready, key=lambda x: key[x])
-        ready.remove(i)
-        for n, segs in enumerate(ways[i]):
-            t, again = est[i], True
-            while again:
-                again = False
-                for r, off, ln in segs:
-                    los, his = taken.setdefault(r, ([], []))
-                    k = int(np.searchsorted(his, t + off + 1e-6))
-                    while k < len(los) and los[k] < t + off + ln - 1e-6:
-                        t, again, k = his[k] - off, True, k + 1
-            if i not in start or t < start[i]:
-                start[i], way[i] = t, n
-        for r, off, ln in ways[i][way[i]]:
-            los, his = taken[r]
-            k = int(np.searchsorted(his, start[i] + off + 1e-6))
-            los.insert(k, start[i] + off)
-            his.insert(k, start[i] + off + ln)
-        for j, lag in succ[i].items():
-            est[j] = max(est[j], start[i] + lag)
-            left[j] -= 1
-            if not left[j]:
-                ready.append(j)
-    return start, way, est
-
-
 def arrange(ops):
     n = len(ops)
+    words = ORDER.split()
+    place = {x.rstrip("<>"): x.count(">") - x.count("<") + k / len(words) for k, x in enumerate(words)}
+    key = [place.get(o[6], -9.0) + (o[7] or 0) // 2 for o in ops]
     last, readers, pred, uses = {}, {}, [], {}
-    for i, (q, fn, rd, wr, own, c) in enumerate(ops):
+    for i, (q, fn, rd, wr, own, c, name, step) in enumerate(ops):
         need = set()
         for t in rd:
             if t in last:
@@ -108,41 +78,40 @@ def arrange(ops):
         for t in set(rd + wr):
             if t[:2] == "M#":
                 uses.setdefault(t, []).append(i)
-    dur = [max(o[5][0], o[5][1] + o[5][2]) for o in ops]
-    segs = [([(o[0], 0.0, o[5][0])] if o[1] else []) + ([("E", o[5][1], o[5][2])] if o[5][2] else []) for o in ops]
-
-    head, off = list(range(n)), [0.0] * n
-    ways = {i: [segs[i]] for i in range(n)}
-    for some in uses.values():
-        for x, y in zip(some[:-1], some[1:]):
-            head[y], off[y] = some[0], off[x] + dur[x] + CFG["wake"]
-            del ways[y]
-        both = [(r, off[y] + o, ln) for y in some for r, o, ln in segs[y]]
-        ways[some[0]] = [both + [(bank, 0.0, off[some[-1]] + dur[some[-1]] + CFG["wake"])] for bank in BANKS[6:]]
-    succ = {i: {} for i in ways}
-    for i in range(n):
-        for j in pred[i]:
-            if head[i] != head[j]:
-                gap = 0.0 if ops[i][0] == ops[j][0] == "p" or ops[i][1] is None else CFG["wake"]
-                succ[head[j]][head[i]] = max(succ[head[j]].get(head[i], 0.0), off[j] + dur[j] + gap - off[i])
-    key, far = {}, {}
-    for i in range(n):
-        x = (ops[i][0], ops[i][5][3])
-        key[i] = 1000.0 * x[1] + far.get(x, 0.0)
-        far[x] = far.get(x, 0.0) + ops[i][5][0]
-    for i in sorted(ways, reverse=True):
-        key[i] = min([key[i]] + [key[j] - lag for j, lag in succ[i].items()])
-    start, way, est = place(succ, ways, key)
-    start = [start[head[i]] + off[i] for i in range(n)]
-    pick = {t: BANKS[6 + way[some[0]]] for t, some in uses.items()}
-    pace = {}
-    ends = sorted((start[i] + dur[i], i) for i in range(n) if ops[i][0] in "vap")
-    for i in range(n):
-        if ops[i][0] == "s" and start[i] > est[i] + CFG["slack"]:
-            k = int(np.searchsorted([x[0] for x in ends], start[i])) - 1
-            if k >= 0:
-                pace[i] = ends[k][1]
-    return sorted(range(n), key=lambda i: (start[i], i)), pick, pace, start, dur
+    group = {i: [i] for i in range(n)}
+    tag = {}
+    for t, some in uses.items():
+        group[some[0]], tag[some[0]] = some, t
+        for x in some[1:]:
+            del group[x]
+    waits = {i: set().union(*[pred[x] for x in some]) - set(some) for i, some in group.items()}
+    order, done, pick, pace = [], set(), {}, {}
+    end, free, bank, engines, ends = {}, {}, {"M1": 0.0, "M2": 0.0}, 0.0, []
+    while waits:
+        i0 = min((i for i in waits if waits[i] <= done), key=lambda x: (key[x], x))
+        del waits[i0]
+        for i in group[i0]:
+            q, (hold, lat, et) = ops[i][0], ops[i][5]
+            t = max([free.get(q, 0.0)] + [end[j] + (0.0 if q == ops[j][0] == "p" or q == "x" else CFG["wake"]) for j in pred[i]])
+            if i in tag:
+                pick[tag[i]] = min(bank, key=lambda x: bank[x])
+                t = max(t, bank[pick[tag[i]]])
+            if et and engines > t + lat:
+                if q == "s" and engines > t + lat + CFG["slack"]:
+                    some = [x for x in ends if x[0] <= engines - lat]
+                    if some and max(some)[0] > t:
+                        pace[i] = max(some)[1]
+                t = engines - lat
+            end[i] = t + (lat + et if et else max(hold, lat))
+            engines = end[i] if et else engines
+            free[q] = t + hold if q != "x" else 0.0
+            if q in "vap":
+                ends.append((end[i], i))
+            order.append(i)
+            done.add(i)
+        if i0 in tag:
+            bank[pick[tag[i0]]] = end[i] + CFG["wake"]
+    return order, pick, pace
 
 
 def build(g, T, ops):
@@ -212,17 +181,17 @@ def rank_program(g, core, T, topo):
     me = T.rank_of(core)
     if me is None:
         return
-    kinds = {f32: "f4", i32: "i4", bf: "i2", u16: "u2"}
+    kinds = {f16: "f2", f32: "f4", i32: "i4", bf: "i2", u16: "u2"}
     shapes = [(n, ("f8" if d == f32 else "c8") if w == "psum" else kinds[d], tuple(sh)) for n, (w, sh, d) in SCRATCH.items()]
     shapes += [(n, "i2", tuple(T[n].shape)) for n in ("cen", "pl", "jmp", "wk", "yc", "yx", "yz", "yn")]
     shapes += [(n, "i4", tuple(T[n].shape)) for n in ("ent", "nb", "ye")]
-    order, pick, pace = arrange(calls(g, core, me, np.recarray((1,), shapes)[0], T, topo, None))[:3]
+    order, pick, pace = arrange(calls(g, core, me, np.recarray((1,), shapes)[0], T, topo, None))
     ops = calls(g, core, me, T, T, topo, pick)
     for i, j in pace.items():
         ops[i][2].append("pace%d" % i)
         ops[j][3].append("pace%d" % i)
-    build(g, T, [(q, fn, [pick.get(t, t) for t in rd], [pick.get(t, t) for t in wr], own)
-                 for q, fn, rd, wr, own, c in [ops[i] for i in order]])
+    build(g, T, [(o[0], o[1], [pick.get(t, t) for t in o[2]], [pick.get(t, t) for t in o[3]], o[4])
+                 for o in [ops[i] for i in order]])
 
 
 def calls(g, core, me, T, G, topo, pick):
@@ -231,22 +200,29 @@ def calls(g, core, me, T, G, topo, pick):
     v, a, p = g.vector, g.scalar, g.tensor
     C = CFG
     real = pick is not None
-    part_of = [""]
-    due = {"L": 0.0, "": 1000.0}
-    for t in range(0, R, 2):
-        due.update({x[0] + str(t + int(x[1])): y + C["two"] * t / 2 for x, y in C["due"].items()})
+    step, seen = [None], {}
 
-    def op(q, fn, rd, wr, own=None, cost=None):
-        ops.append((q, fn, list(rd), list(wr), own, (cost or (0.0, 0.0, 0.0)) + (due[part_of[0]],)))
+    def op(q, fn, rd, wr, own=None, cost=None, name=None):
+        if name is None:
+            name = (list(wr) + [own[0][:2] if own and own[0][0] == "l" else "out" + "".join(rd)[:2]])[0]
+            if name[:2] == "M#":
+                name = "m" + name.split("#")[2]
+            elif step[0] is not None:
+                name = "AP" + name[4:] if name[:2] == "AP" else \
+                    name if name[:2] in ("AN", "MN", "MP", "EU", "L1", "A3", "A8") else name.rstrip("0123456789")
+        k = seen[q, name, step[0]] = seen.get((q, name, step[0]), -1) + 1
+        name = q + ":" + name + (".%d" % k if k else "") + ("_" if step[0] is None else "'" * (step[0] % 2))
+        ops.append((q, fn, list(rd), list(wr), own, cost or (0.0, 0.0, 0.0), name, step[0]))
 
-    def join(n):
+    def join(n, w=250.0):
         some = ops[-n:]
         del ops[-n:]
-        op(some[0][0], [f for o in some for f in o[1]], some[0][2], some[0][3], None, (C["fix"] * 2 + 250.0 * C["f"], 0.0, 0.0))
+        ops.append(some[0][:1] + ([f for o in some for f in o[1]],) + some[0][2:5] +
+                   ((C["fix"] * 2 + w * 0.83 * C["f"], 0.0, 0.0),) + some[0][6:])
 
-    def lend():
+    def lend(what):
         nb_[0] += 1
-        tag = "M#%d" % nb_[0]
+        tag = "M#%d#%s" % (nb_[0], what)
         return T[pick[tag] if real else "M1"], tag
 
     def ind(win, off):
@@ -297,8 +273,8 @@ def calls(g, core, me, T, G, topo, pick):
     def fill(ap, x, wr):
         op("v", [lambda: v.memset(ap, x)], [], wr, None, work(ap, [ap]))
 
-    def scan(out, d0, d1, rd, wr):
-        op("v", [lambda: v.tensor_tensor_scan(out, d0, d1, 0.0, ALU.mult, ALU.add)], rd, wr, None, work(out, [d0, d1]))
+    def scan(out, d0, d1, o0, o1, rd, wr):
+        op("v", [lambda: v.tensor_tensor_scan(out, d0, d1, 0.0, o0, o1)], rd, wr, None, work(out, [d0, d1]))
 
     def act(out, in_, func, rd, wr, bias=0.0, scale=1.0):
         cost = None if real else work(out, [in_, T.COL])
@@ -313,7 +289,7 @@ def calls(g, core, me, T, G, topo, pick):
         else:
             act(out, src, ACT.Copy, rd, wr)
 
-    def mm(terms, bank, first=True, final=True, after=()):
+    def mm(terms, bank, first=True, final=True, after=(), name=None):
         fns, rd = [], []
         for n, (o, l, r, x) in enumerate(terms):
             st, sp = first and n == 0, final and n == len(terms) - 1
@@ -321,7 +297,7 @@ def calls(g, core, me, T, G, topo, pick):
             rd += x
         cost = None if real else (sum(max(64, o.shape[1]) * (4 if l.itemsize == 4 else 1) for o, l, r, x in terms)
                                   * C["pe"] * C["f"], 0.0, 0.0)
-        op("p", fns, sorted(set(rd)), [bank] + list(after), None, cost)
+        op("p", fns, sorted(set(rd)), [bank] + list(after), None, cost, name)
 
     def turn(pairs, rd, bank):
         op("p", [lambda o=o, i=i: p.transpose(o, i, T.ID[:, :]) for o, i in pairs], rd + ["ID"], [bank], None,
@@ -379,6 +355,9 @@ def calls(g, core, me, T, G, topo, pick):
     def col(j):
         return T.COL[:, j:j + 1]
 
+    def on(r):
+        return T.DIAG[:, r:r + 1]
+
     def blk(name, b):
         return T[name][:, b * B:(b + 1) * B]
 
@@ -395,38 +374,52 @@ def calls(g, core, me, T, G, topo, pick):
     def y_make(xlo, t0, t1, rd):
         n = (t1 - t0) * B
         c, tags = n // 16, ["Y%d" % t for t in range(t0, t1)]
-        ps, bank = lend()
+        ps, bank = lend("HI")
         mm([(ps[:, 0:c], sel("DW", r), T.XS[:, xlo + r:xlo + n:16], ["DW"] + rd) for r in range(16)], bank, after=["HI"])
         cp(T.HI[:, 0:c], ps[:, 0:c], [bank], ["HI"])
         ts(T.HI[:, 0:c], T.HI[:, 0:c], M - 1, None, ALU.bitwise_and, None, ["HI"], ["HI"])
         cp(T.HU[:, 0:c], T.HI[:, 0:c], ["HI"], ["HU"])
         for t in range(t0, t1):
             lo = (t - t0) * B
-            tt(T.DF[:, lo:lo + B], ind(T.JM[:, :], T.HU[:, lo // 16:lo // 16 + 16]), T.XS[:, xlo + lo:xlo + lo + B], ALU.subtract,
-               ["JM", "HU"] + rd, ["DF%d" % (t - t0)])
-            act(blk("Y", t), T.DF[:, lo:lo + B], ACT.Abs, ["DF%d" % (t - t0)], ["Y%d" % t])
+            df, tg, x = T.DF[:, lo:lo + B], "DF%d" % (t - t0), T.XS[:, xlo + lo:xlo + lo + B]
+            jump = ind(T.JM[:, :], T.HU[:, lo // 16:lo // 16 + 16])
+            if C["y"][t] == "v":
+                tt(df, jump, x, ALU.subtract, ["JM", "HU"] + rd, [tg])
+                act(blk("Y", t), df, ACT.Abs, [tg], ["Y%d" % t])
+            else:
+                act(df, jump, ACT.Copy, ["JM", "HU"], [tg])
+                ps, bank = lend("Y")
+                mm([(ps[:, 0:B], T.ID[:, :], df, ["ID", tg]), (ps[:, 0:B], T.IDM[:, :], x, ["IDM"] + rd)], bank)
+                act(blk("Y", t), ps[:, 0:B], ACT.Abs, [bank], ["Y%d" % t])
         dma("g", [(T.YF[:, t0 * B:t1 * B], T.Y[:, t0 * B:t1 * B])], tags, ["YF%d" % t for t in range(t0, t1)])
 
     def nb_lists(b):
         nbi, tg = blk("NBI", b), "NBI%d" % b
         cp(blk("NBU", b), nbi, [tg], ["NBU%d" % b])
-        ts(blk("KO2", b), nbi, 1.0 / 1024, 193.0 - 511.5 / 1024, ALU.mult, ALU.add, [tg], ["KO2%d" % b])
-        ts(T.A8[:, :], nbi, 1.0 / 256, 192.0 - 127.5 / 256, ALU.mult, ALU.add, [tg], ["A8"])
         cp(T.NBF[:, :], nbi, [tg], ["NBF"])
-        ps, bank = lend()
+        for e, out, w, x, tag in [(C["nb"][b][0], blk("KO2", b), 1.0 / 1024, 193.0 - 511.5 / 1024, "KO2%d" % b),
+                                  (C["nb"][b][1], T.A8[:, :], 1.0 / 256, 192.0 - 127.5 / 256, "A8")]:
+            if e == "v":
+                ts(out, nbi, w, x, ALU.mult, ALU.add, [tg], [tag])
+            else:
+                act(out, T.NBF[:, :], ACT.Identity, ["NBF"], [tag], bias=x, scale=w)
+        ps, bank = lend("TC")
         o = ps[:, 0:B]
         mm([(o, T.IDF[:, :], T.NBF[:, :], ["IDF", "NBF"]), (o, T.ID8[:, :], T.A8[:, :], ["ID8", "A8"]),
-            (o, T.ID10[:, :], blk("KO2", b), ["ID10", "KO2%d" % b]), (o, T.ID[:, :], T.K1[:, :], ["ID", "K1"]),
-            (o, T.IDB[:, :], T.ONES[:, 0:B], ["IDB", "ONES"])], bank)
-        act(blk("TC", b), o, ACT.Identity, [bank], ["TC%d" % b], bias=-127.5, scale=256.0)
+            (o, T.ID10[:, :], blk("KO2", b), ["ID10", "KO2%d" % b]), (o, T.ID[:, :], T.K1[:, :], ["ID", "K1"])], bank)
+        act(blk("TC", b), o, ACT.Identity, [bank], ["TC%d" % b], bias=512.0 * (16384 * 193 - 3840 * 192), scale=512.0)
 
     def ent_split(b):
-        cp(blk("EF", b), blk("EI", b), ["EI%d" % b], ["EF%d" % b])
-        act(blk("EH", b), blk("EF", b), ACT.Copy, ["EF%d" % b], ["EH%d" % b])
-        ps, bank = lend()
-        o = ps[:, 0:B]
-        mm([(o, T.IDF[:, :], blk("EF", b), ["IDF", "EF%d" % b]), (o, T.IDM[:, :], blk("EH", b), ["IDM", "EH%d" % b])], bank)
-        act(blk("EL", b), o, ACT.Copy, [bank], ["EL%d" % b])
+        if C["split"][b] == "v":
+            cp(blk("EH", b), blk("EI", b), ["EI%d" % b], ["EH%d" % b])
+            tt(blk("EL", b), blk("EI", b), blk("EH", b), ALU.subtract, ["EI%d" % b, "EH%d" % b], ["EL%d" % b])
+        else:
+            cp(blk("EF", b), blk("EI", b), ["EI%d" % b], ["EF%d" % b])
+            act(blk("EH", b), blk("EF", b), ACT.Copy, ["EF%d" % b], ["EH%d" % b])
+            ps, bank = lend("EL")
+            o = ps[:, 0:B]
+            mm([(o, T.IDF[:, :], blk("EF", b), ["IDF", "EF%d" % b]), (o, T.IDM[:, :], blk("EH", b), ["IDM", "EH%d" % b])], bank)
+            act(blk("EL", b), o, ACT.Copy, [bank], ["EL%d" % b])
         w = slice(b * K * B, (b + 1) * K * B)
         dma("s", [(T.W[0::16, w], blk("EH", b)), (T.W[1::16, w], blk("EL", b))], ["EH%d" % b, "EL%d" % b],
             ["W%d" % b] + ["Wf%d" % x for x in range(4 * b, 4 * b + 4)])
@@ -438,13 +431,15 @@ def calls(g, core, me, T, G, topo, pick):
                 iota("W", lo, lo + V, [[0, V]], 1, tag="Wf%d" % x)
             elif e == "v":
                 fill(T.W[:, lo:lo + V], 1.0, ["Wf%d" % x])
+            elif e == "a":
+                act(T.W[:, lo:lo + V], T.ONES[:, :], ACT.Copy, ["ONES"], ["Wf%d" % x])
             else:
                 dma("s", [(T.W[:, lo:lo + V], T.ONES[:, :])], ["ONES"], ["Wf%d" % x])
 
     def e_lists(t):
         b = t % 4
         for lo, hi in zip(C["cut"][:-1], C["cut"][1:]):
-            ps, bank = lend()
+            ps, bank = lend("EU")
             tags = ["EU%d" % j for j in range(lo // 32, hi // 32)]
             mm([(ps[:, 0:hi - lo], sel("DE", r), T.W[:, b * K * B + 16 * lo + r:b * K * B + 16 * hi:16], ["DE", "W%d" % b])
                 for r in range(16)], bank, after=tags)
@@ -455,24 +450,24 @@ def calls(g, core, me, T, G, topo, pick):
         dma("s", [(T.NN[:, :], T.W[2::16, b * K * B:(b + 1) * K * B])], ["W%d" % b], ["NN"])
 
     def ucalc(t):
-        ps, bank = lend()
+        ps, bank = lend("UF")
         mm([(ps[:, 0:B], T.BO[:, :], blk("Y", t), ["BO", "Y%d" % t])], bank, after=["UF"])
         act(T.UF[:, :], ps[:, 0:B], ACT.Identity, [bank], ["UF"], bias=192.0 - 31.5 / 64, scale=1.0 / 64)
-        ps, bank = lend()
+        ps, bank = lend("U")
         o, u = ps[:, 0:B], "U%d" % (t % 2)
         mm([(o, T.BO[:, :], blk("Y", t), ["BO", "Y%d" % t]), (o, T.ID64[:, :], T.UF[:, :], ["ID64", "UF"])], bank, after=[u])
         act(blk("U", t % 2), o, ACT.Identity, [bank], [u], bias=64.0 * 192)
 
-    def twice(src, c, rd, stage, bank):
-        turn([(T[bank][:, 2 * B + h:2 * B + h + 128], T[src][:, c + h:c + h + 128]) for h in (0, 128)], rd, bank)
-        move(C["evac"], T[stage][:, :], blk(bank, 2), [bank], [stage])
-        turn([(T[bank][:, h:h + 128], T[stage][:, h % B:h % B + 128]) for h in range(0, 2 * B, 128)], [stage], bank)
+    def twice(e, src, c, rd, stage, bank, lo=0):
+        turn([(T[bank][:, lo + h:lo + h + 128], T[src][:, c + h:c + h + 128]) for h in (0, 128)], rd, bank)
+        move(e, T[stage][:, :], T[bank][:, lo:lo + B], [bank], [stage])
+        turn([(T[bank][:, lo + h:lo + h + 128], T[stage][:, h % B:h % B + 128]) for h in range(0, 2 * B, 128)], [stage], bank)
 
     def yrep(t):
-        twice("Y", B * t, ["Y%d" % t], "YT", "YB")
+        twice(C["yt"][t], "Y", B * t, ["Y%d" % t], "YT", "YB")
 
     def crep(t):
-        twice("CT", own0 + B * (t % 4), ["CTo%d" % (t % 4)], "CTT", "CB")
+        twice(C["ct"][t], "CT", own0 + B * (t % 4), ["CTo%d" % (t % 4)], "CTT", "CB", 2 * B * (t % 2))
 
     def tiles_n(t):
         dma("s", [(T.AN[:, 0:B], cown(t))], ["CTo%d" % (t % 4)], ["ANo"])
@@ -483,74 +478,71 @@ def calls(g, core, me, T, G, topo, pick):
 
     def payload(t):
         if t < 4:
-            ts(T.PW[:, :], T.PB[:, :], col(14), T.BC[:, t:t + 1], ALU.mult, ALU.add, ["PB", "BC", "c14"], ["PW"])
+            act(T.PW[:, :], T.PB[:, :], ACT.Identity, ["PB", "BC", "DIAG"], ["PW"], bias=T.BC[:, t:t + 1], scale=on(1))
         elif t == 4:
-            ts(T.PW[:, :], T.PB[:, :], col(14), None, ALU.mult, None, ["PB", "c14"], ["PW"])
+            act(T.PW[:, :], T.PB[:, :], ACT.Identity, ["PB", "DIAG"], ["PW"], scale=on(1))
         else:
-            ts(T.PF[:, :], T.PB[:, :], col(7), None, ALU.mult, None, ["PB", "c7"], ["PF"])
+            act(T.PF[:, :], T.PB[:, :], ACT.Identity, ["PB", "DIAG"], ["PF"], scale=on(0))
 
     def template(t):
         dma("s", [(T["XB%d" % t][:, 144:336], T.TPL[:, :])], ["TPL"], ["XB%d" % t])
 
     def acount():
-        ps, bank = lend()
+        ps, bank = lend("A")
         o = ps[:, 0:1]
-        mm([(o, T.ONES[:, 0:128], T.S[:, 79:80], ["ONES", "S"]), (o, T.ONES[:, 0:128], T.C96[:, 0:1], ["C96"])], bank)
+        mm([(o, T.ONES[:, 0:128], T.S[:, 79:80], ["ONES", "S"]), (o, T.ONES[:, 0:128], T.MONE[:, 16:17], ["C96"])], bank)
         act(T.AG[:, 0:1], o, ACT.Identity, [bank], ["AG"], bias=-2048.0 * 31.5, scale=-2048.0)
         act(T.AM[:, :], o, ACT.Identity, [bank, "AG"], ["AM"], bias=T.AG[:, 0:1], scale=2048.0)
 
     def arrive(t):
         xb, tg = T["XB%d" % t], ["XB%d" % t, "XL%d" % t]
         ts(T.HX[:, :], xb[:, 0:NC], MAGIC, MAGIC, ALU.add, ALU.subtract, tg, ["HX"])
-        ps, bank = lend()
-        mm([(ps[:, 0:NC], T.BOS[:, :], T.HX[:, :], ["BOS", "HX"])], bank)
-        tt(T.MM[:, :], ps[:, 0:NC], T.DIAG[:, :], ALU.mult, [bank, "DIAG"], ["MM"])
-        scan(T.MS[:, :], T.SEG[:, :], T.MM[:, :], ["SEG", "MM"], ["MS"])
+        ps, bank = lend("MS")
+        o = ps[:, 0:NC]
+        mm([(o, T.ID[:, :], T.MASK[:, :], ["ID", "MASK"]), (o, T.BOS[:, :], T.HX[:, :], ["BOS", "HX"])], bank)
+        scan(T.MS[:, :], T.CUT[:, :], o, ALU.add, ALU.max, ["CUT", bank], ["MS"])
         cp(T.MU[:, :], T.MS[:, 15:NC:16], ["MS"], ["MU"])
-        ps, bank = lend()
+        cuts = [(NC - n1, 0, n1)] * (n1 > 0) + [(0, n1, NC - n1)]
+        if C["pl"][t] == "v":
+            for to, at, w in cuts:
+                tt(T.PL[:, NC * t + to:NC * t + to + w], xb[:, at:at + w], T.HX[:, at:at + w], ALU.subtract, tg + ["HX"], ["PL"])
+            join(len(cuts), 450.0)
+            return
+        ps, bank = lend("PL")
         o = ps[:, 0:NC]
         mm([(o, T.IDF[:, :], xb[:, 0:NC], ["IDF"] + tg), (o, T.IDFM[:, :], T.HX[:, :], ["IDFM", "HX"])], bank, after=["PL"])
-        if n1:
-            act(T.PL[:, NC * t + NC - n1:NC * t + NC], ps[:, 0:n1], ACT.Identity, [bank], ["PL"], bias=127.5)
-        act(T.PL[:, NC * t:NC * t + NC - n1], ps[:, n1:NC], ACT.Identity, [bank], ["PL"], bias=127.5)
-        join(2 if n1 else 1)
+        for to, at, w in cuts:
+            act(T.PL[:, NC * t + to:NC * t + to + w], ps[:, at:at + w], ACT.Copy, [bank], ["PL"])
+        join(len(cuts))
 
     def arrive_w(t):
         if t < 4:
             cp(ind(T.W[:, :], T.MU[:, :]), T.PW[:, :], ["MU", "PW"], WALL)
             return
-        tw = "TW" if t == 4 else "TF"
+        tw = "TW" if t == 4 else "MS"
         ts(T[tw][:, :], ind(T.W[:, :], T.MU[:, :]), col(5), T.BC[:, t:t + 1], ALU.mult, ALU.add, ["MU", "c5", "BC"] + WALL, [tw])
         if t == 4:
             tt(ind(T.W[:, :], T.MU[:, :]), T.TW[:, :], T.PW[:, :], ALU.add, ["MU", "PW", "TW"], WALL)
         else:
-            tt(ind(T.WF[:, :], T.MU[:, :]), T.TF[:, :], T.PF[:, :], ALU.add, ["MU", "PF", "TF"], ["WFe", "WFn"])
+            tt(ind(T.WF[:, :], T.MU[:, :]), T.MS[:, :], T.PF[:, :], ALU.add, ["MU", "PF", "MS"], ["WFe", "WFn"])
 
     def entry_piece(t, j):
         ap, ct, c0 = "AP%d" % (t % 2), "CTo%d" % (t % 4), own0 + B * (t % 4)
         tg, ks, sl = "%s_%d" % (ap, j), (2 * j, 2 * j + 1), slice(2 * B * j, 2 * B * (j + 1))
         move(C["pv"][t][j], T[ap][:, sl], ind(T.PL[:, :], T.EU[:, 32 * j:32 * j + 32]), ["PL", "EU%d" % j], [tg])
-        if C["still"]:
-            def sums(name, w, x):
-                return [(T.HB[:, h + k:h + 128:16], T[name][:, B * k + h:B * k + h + 128], w, x) for k in ks for h in (0, 128)]
-            terms = []
-            if j == 0:
-                terms = [(T.HB[:, 0:B], T.ID[:, :], T.ZERO[:, :], ["ID", "ZERO"])] + \
-                    [(T.HB[:, h:h + 128], T.CT[:, c0 + h:c0 + h + 128], T.BOM[:, :], ["BOM", ct]) for h in (0, 128)]
-            mm(terms + sums(ap, T.BOM[:, 0::16], ["BOM", tg]), "HB", j == 0, False)
-            tt(T.MP[:, sl], T[ap][:, sl], T.CB[:, 0:2 * B], ALU.max, [tg, "CB"], ["MP%d" % j])
-            mm(sums("MP", T.BO2[:, :], ["BO2", "MP%d" % j]), "HB", False, j == 7)
-        else:
-            o = T.HB[:, 0:B]
-            terms = [(o, T.BOM[:, :], cown(t), ["BOM", ct])] if j == 0 else []
-            mm(terms + [(o, sel("DN", k), blk(ap, k), ["DN", tg]) for k in ks], "HB", j == 0, False)
-            tt(T.MP[:, sl], T[ap][:, sl], T.CB[:, 0:2 * B], ALU.max, [tg, "CB"], ["MP%d" % j])
-            mm([(o, sel("DP", k), blk("MP", k), ["DP", "MP%d" % j]) for k in ks], "HB", False, j == 7)
 
-    part_of[0] = "L"
+        def sums(name, w, x):
+            return [(T.HB[:, h + k:h + 128:16], T[name][:, B * k + h:B * k + h + 128], w, x) for k in ks for h in (0, 128)]
+        if j == 0:
+            mm([(T.HB[:, 0:B], T.ID[:, :], T.ZERO[:, :], ["ID", "ZERO"])] +
+               [(T.HB[:, h:h + 128], T.CT[:, c0 + h:c0 + h + 128], T.BOM[:, :], ["BOM", ct]) for h in (0, 128)],
+               "HB", True, False, name="hc")
+        tt(T.MP[:, sl], T[ap][:, sl], T.CB[:, 2 * B * (t % 2):2 * B * (t % 2 + 1)], ALU.max, [tg, "CB"], ["MP%d" % j])
+        mm(sums(ap, T.BOM[:, 0::16], ["BOM", tg]) + sums("MP", T.BO2[:, :], ["BO2", "MP%d" % j]), "HB", False, j == 7,
+           name="h%d" % j)
+
     dma("s", [(T.CT[:, own0:own0 + V], T.cen[:, :])], [], CTALL[:4])
     send_c(0, V, 5, CTALL[:4])
-    part_of[0] = ""
     dma("s", [(T.JM[:, :], T.jmp[:, :])], [], ["JM"])
     dma("s", [(T.PL[:, :], T.pl[:, :])], [], ["PL"])
     for b0, b1 in ((0, 1), (1, 4)):
@@ -573,7 +565,7 @@ def calls(g, core, me, T, G, topo, pick):
     join(3 if me else 2)
     iota("NDC", 0, 64, [[CAP, 4], [-16, 16]], 64)
     iota("THR", 0, 64, [[CAP, 4], [-16, 16]], 48)
-    iota("TPI", 0, NC, [[0, 4], [256, CAP]], 256 * (K * V + CAP * me))
+    iota("HX", 0, NC, [[0, 4], [512, CAP]], 512 * (K * V + CAP * me))
     if n1:
         iota("PB", 0, n1, [[1, n1]], NC - n1)
     iota("PB", n1, NC, [[1, NC - n1]], 0)
@@ -585,7 +577,6 @@ def calls(g, core, me, T, G, topo, pick):
     ts(col(2), col(1), col(0), 15.0, ALU.subtract, ALU.add, ["c0", "c1"], ["c2"])
     ts(col(3), col(0), 2.0, 1.0, ALU.mult, ALU.add, ["c0"], ["c3"])
     ts(col(4), col(0), 2.0, None, ALU.is_lt, None, ["c0"], ["c4"])
-    ts(col(7), col(0), 0.0, None, ALU.is_equal, None, ["c0"], ["c7"])
     dmat("DW", col(3), ["c3"])
     ts(T.IDF[:, :], T.X143[:, 0:128], col(1), None, ALU.is_equal, None, ["X143", "c1"], ["IDF"])
     dmat("D1", 1.0)
@@ -594,37 +585,34 @@ def calls(g, core, me, T, G, topo, pick):
     ts(T.BOF[:, :], T.XG[:, :], col(6), None, ALU.is_equal, None, ["XG", "c6"], ["BOF"])
     for nm, src, w in [("ID", "IDF", 1.0), ("IDM", "IDF", -1.0), ("DA", "D1", -2048.0), ("DM", "D1", 4096.0),
                        ("BOM", "BOF", -1.0), ("B64", "BOF", 64.0), ("ID8", "IDF", 3840.0), ("ID10", "IDF", -16384.0),
-                       ("IDB", "IDF", 16384.0 * 193 - 3840.0 * 192), ("BO", "BOF", 1.0), ("DC", "D1", 256.0),
-                       ("ID64", "IDF", -64.0), ("IDFM", "IDF", -1.0), ("BOS", "BOF", 1.0 / 256)]:
+                       ("IDB", "IDF", 65536.0), ("BO", "BOF", 1.0), ("DC", "D1", 256.0),
+                       ("ID64", "IDF", -64.0), ("IDFM", "IDF", -1.0), ("BOS", "BOF", 1.0 / 512)]:
         scaled(nm, src, w)
-    if C["still"]:
-        act(T.BO2[:, :], T.BOF[:, 0::16], ACT.Identity, ["BOF"], ["BO2"], scale=2.0)
-        fill(T.ZERO[:, :], 0.0, ["ZERO"])
-    else:
-        scaled("DN", "D1", -1.0)
-        scaled("DP", "D1", 2.0)
+    act(T.BO2[:, :], T.BOF[:, 0::16], ACT.Identity, ["BOF"], ["BO2"], scale=2.0)
+    fill(T.ZERO[:, :], 0.0, ["ZERO"])
     pool(lambda: g.affine_select(T.LB[:, :], T.BOM[:, :], [[-1, 128]], ALU.is_ge, 0.0, 0, 1), 128, ["BOM"], ["LB"])
     pool(lambda: g.affine_select(T.LM[:, :], T.LB[:, :], [[-1, 128]], ALU.not_equal, -65.0, 0, 1), 128, ["LB"], ["LM"])
     pool(lambda: g.affine_select(T.TRI[:, :], T.B64[:, :], [[1, 128]], ALU.is_ge, 0.0, 0, -1), 128, ["B64"], ["TRI"])
     fill(T.AM[:, :], 0.0, ["AM"])
     fill(T.INI[:, :], BIG, ["INI"])
-    fill(T.C96[:, :], -96.0, ["C96"])
-    fill(T.MONE[:, :], -1.0, ["MONE"])
+    fill(T.MONE[:, 16:32], -96.0, ["C96"])
+    fill(T.MONE[:, 0:16], -1.0, ["MONE"])
     ts(T.REP[:, :], T.X143[:, 0:8], 0.0, col(0), ALU.mult, ALU.add, ["X143", "c0"], ["REP"])
-    ts(T.DIAG[:, :], T.J16[:, 0:NC], col(0), None, ALU.is_equal, None, ["J16", "c0"], ["DIAG"])
-    ts(T.X[:, :], T.J16[:, :], col(0), BIG, ALU.is_equal, ALU.mult, ["J16", "c0"], ["X"])
-    act(T.DMIN[:, :], T.X[:, :], ACT.Identity, ["X"], ["DMIN"], bias=-127.5)
-    ts(T.SEG[:, :], T.J16[:, 0:NC], 0.0, None, ALU.not_equal, None, ["J16"], ["SEG"])
-    ts(T.IB[:, :], T.C16[:, :], col(0), None, ALU.add, None, ["C16", "c0"], ["IB"])
-    ts(T.I17[:, :], T.IB[:, :], 17.0 * B, None, ALU.add, None, ["IB"], ["I17"])
-    ts(col(8), col(0), -1.0, -float(NC), ALU.mult, ALU.add, ["c0"], ["c8"])
+    ts(T.MASK[:, :], T.J16[:, 0:NC], col(0), -32768.0, ALU.not_equal, ALU.mult, ["J16", "c0"], ["MASK"])
+    ts(T.CUT[:, :], T.J16[:, 0:NC], 0.0, -65536.0, ALU.is_equal, ALU.mult, ["J16"], ["CUT"])
+    ts(T.DIAG[:, :], T.J16[:, :], col(0), None, ALU.is_equal, None, ["J16", "c0"], ["DIAG"])
+    cp(T.TRH[:, :], T.TRI[:, :], ["TRI"], ["TRH"])
+    cp(T.BOH[:, :], T.BO[:, :], ["BO"], ["BOH"])
+    ts(T.SEG[:, :], T.J16[:, 0:80], 0.0, None, ALU.not_equal, None, ["J16"], ["SEG"])
+    act(T.IB[:, :], T.C16[:, :], ACT.Identity, ["C16", "c0"], ["IB"], bias=col(0))
+    act(T.I17[:, :], T.IB[:, :], ACT.Identity, ["IB"], ["I17"], bias=17.0 * B)
+    act(col(8), col(0), ACT.Identity, ["c0"], ["c8"], bias=-float(NC), scale=-1.0)
     act(T.DG[:, :], T.IDF[:, :], ACT.Identity, ["IDF", "c8"], ["DG"], scale=col(8))
-    ts(col(14), col(0), 1.0, None, ALU.is_equal, None, ["c0"], ["c14"])
-    ts(col(5), col(0), 2.0, None, ALU.is_ge, None, ["c0"], ["c5"])
-    ts(col(15), col(0), 2.0, 2.0, ALU.is_ge, ALU.mult, ["c0"], ["c15"])
-    ts(T.BC[:, 0:4], T.BI[:, 0:4], col(7), col(15), ALU.mult, ALU.add, ["BI", "c7", "c15"], ["BC"])
-    ts(T.BC[:, 4:8], T.BI[:, 4:8], col(7), col(5), ALU.mult, ALU.add, ["BI", "c7", "c5"], ["BC"])
-    act(T.TPL[:, :], T.TPI[:, :], ACT.Identity, ["TPI", "c7"], ["TPL"], bias=-127.5, scale=col(7))
+    act(col(5), col(4), ACT.Identity, ["c4"], ["c5"], bias=1.0, scale=-1.0)
+    act(col(15), col(4), ACT.Identity, ["c4"], ["c15"], bias=2.0, scale=-2.0)
+    act(T.BC[:, 0:4], T.BI[:, 0:4], ACT.Identity, ["BI", "DIAG", "c15"], ["BC"], bias=col(15), scale=on(0))
+    act(T.BC[:, 4:8], T.BI[:, 4:8], ACT.Identity, ["BI", "DIAG", "c5"], ["BC"], bias=col(5), scale=on(0))
+    act(T.TPL[:, :], T.HX[:, :], ACT.Identity, ["HX", "DIAG"], ["TPL"], scale=on(0))
     ent_split(0)
     e_lists(0)
     crep(0)
@@ -647,7 +635,7 @@ def calls(g, core, me, T, G, topo, pick):
         ap = "AP%d" % (t % 2)
         APALL = ["%s_%d" % (ap, j) for j in range(8)] + [ap + "x"]
         nx = t + 1 < R
-        part_of[0] = "N%d" % t
+        step[0] = t
         tt(T.MN[:, 0:B], T.AN[:, 0:B], T.YB[:, 0:B], ALU.max, ["ANo", "YB"], ["MNo"])
         for j in range(8):
             lo = B + 2 * B * j
@@ -659,49 +647,41 @@ def calls(g, core, me, T, G, topo, pick):
                 bank = BANKS[q % 2]
                 c0, c1 = (0 if q == 0 else B + 4 * B * q), B + 4 * B * (q + 1)
                 w = (c1 - c0) // 16
-                out = T[bank][:, 0:w]
+                out, o = T[bank][:, 0:w], T[bank][:, w - 64:w]
                 mm([(out, sel("DA", r), T.AN[:, c0 + r:c1:16], ["DA", "AN%d" % (j - 1), "AN%d" % j] + ["ANo"] * (q == 0))
-                    for r in range(16)], bank, True, False)
-                o = T[bank][:, w - 64:w]
-                mm([(o, T.ID[:, :], T.KO1[:, 64 * q:64 * q + 64], ["ID", "KO1"]),
-                    (o, T.ID[:, :], T.KO2[:, b * B + 64 * q:b * B + 64 * q + 64], ["KO2%d" % b])], bank, False, False)
+                    for r in range(16)] +
+                   [(o, T.ID[:, :], T.KO1[:, 64 * q:64 * q + 64], ["ID", "KO1"]),
+                    (o, T.ID[:, :], T.KO2[:, b * B + 64 * q:b * B + 64 * q + 64], ["KO2%d" % b])], bank, True, False, name="a%d" % q)
                 mm([(out, sel("DM", r), T.MN[:, c0 + r:c1:16], ["DM", "MN%d" % (j - 1), "MN%d" % j] + ["MNo"] * (q == 0))
-                    for r in range(16)], bank, False, True)
+                    for r in range(16)], bank, False, True, name="m%d" % q)
                 if q == 0:
-                    if C["th"] == "a":
-                        act(T.INI[:, 0:16], T.K0[:, 0:16], ACT.Identity, ["K0", "AM"], ["INI"], bias=T.AM[:, :])
-                    else:
-                        ts(T.INI[:, 0:16], T.K0[:, 0:16], T.AM[:, :], None, ALU.add, None, ["K0", "AM"], ["INI"])
+                    ts(T.INI[:, 0:16], T.K0[:, 0:16], T.AM[:, :], None, ALU.add, None, ["K0", "AM"], ["INI"])
                     tt(T.ACC[:, :], T.K0[:, 16:80], T.INI[:, :], ALU.min, ["K0", "INI"], ["ACC"])
                 else:
                     tt(T.ACC[:, :], T[bank][:, 0:64], T.ACC[:, :], ALU.min, [bank, "ACC"], ["ACC"])
-        part_of[0] = "F%d" % t
         if nx:
             send_free(t)
-        part_of[0] = "T%d" % t
         tt(T.A32[:, :], T.ACC[:, 0:32], T.ACC[:, 32:64], ALU.min, ["ACC"], ["A32"])
         tt(T.KG[:, :], T.A32[:, 0:16], T.A32[:, 16:32], ALU.min, ["A32"], ["KG"])
         ts(T.CODE[:, :], T.KG[:, :], 7, None, ALU.bitwise_and, None, ["KG"], ["CODE"])
         tt(T.H[:, :], ind(T.CODE[:, :], T.REP[:, 0:5]), T.OC[:, :], ALU.is_equal, ["CODE", "REP", "OC"], ["H"])
-        part_of[0] = "X%d" % t
-        scan(T.S[:, :], T.SEG[:, 0:80], T.H[:, :], ["SEG", "H"], ["S"])
+        scan(T.S[:, :], T.SEG[:, :], T.H[:, :], ALU.mult, ALU.add, ["SEG", "H"], ["S"])
         o = T.K0[:, 0:64]
         mm([(o, T.ID[:, :], T.NDC[:, :], ["ID", "NDC"]), (o, T.LM[:, :], T.H[:, 0:64], ["LM", "H"]),
-            (o, T.BO[:, :], T.S[:, 0:64], ["BO", "S"])], "K0")
+            (o, T.BO[:, :], T.S[:, 0:64], ["BO", "S"])], "K0", name="rank")
         ts(T.L1[:, :], T.KG[:, :], 3, 255, ALU.logical_shift_right, ALU.bitwise_and, ["KG"], ["L1"])
         cp(T.L1U[:, :], T.L1[:, :], ["L1"], ["L1U"])
         tt(T.VV[:, :], o, T.THR[:, :], ALU.is_lt, ["K0", "THR"], ["VV"])
         tt(T.Q[:, :], o, T.VV[:, :], ALU.mult, ["K0", "VV"], ["Q"])
         o = T.KB1[:, 0:16]
-        mm([(o, T.ID[:, :], T.C16[:, :], ["ID", "C16"]), (o, T.DG[:, :], T.MONE[:, :], ["DG", "MONE"])] +
-           [(o, T.DG[:, :], T.VV[:, 16 * d:16 * d + 16], ["VV"]) for d in range(4)], "KB1", True, False)
-        mm([(o, T.ID[:, :], T.Q[:, 16 * d:16 * d + 16], ["Q"]) for d in range(4)], "KB1", False, True)
-        tt(T.X[:, :], ind(blk("TC", b), T.L1U[:, :]), T.DMIN[:, :], ALU.min, ["TC%d" % b, "L1U", "DMIN"], ["X"])
+        mm([(o, T.ID[:, :], T.C16[:, :], ["ID", "C16"]), (o, T.DG[:, :], T.MONE[:, 0:16], ["DG", "MONE"])] +
+           [(o, T.DG[:, :], T.VV[:, 16 * d:16 * d + 16], ["VV"]) for d in range(4)], "KB1", True, False, name="pv")
+        mm([(o, T.ID[:, :], T.Q[:, 16 * d:16 * d + 16], ["Q"]) for d in range(4)], "KB1", False, True, name="pq")
+        tt(T.X[:, :], ind(blk("TC", b), T.L1U[:, :]), T.DIAG[:, :], ALU.mult, ["TC%d" % b, "L1U", "DIAG"], ["X"])
         cp(T.PY[:, :], o, ["KB1"], ["PY"])
         tt(ind(T["XB%d" % t][:, 144:XW_], T.PY[:, :]), T.X[:, :], blk("YF", t), ALU.add, ["PY", "X", "YF%d" % t], ["XB%d" % t])
         send_x(t)
         if nx:
-            part_of[0] = ""
             acount()
             if t in (1, 2):
                 y_make((t - 1) * B, t + 3, t + 4, ["XS%d" % (t - 1)])
@@ -711,48 +691,43 @@ def calls(g, core, me, T, G, topo, pick):
             if t < 3:
                 nb_lists(t + 1)
             ucalc(t + 1)
-        part_of[0] = "P%d" % t
         for j in range(8):
             entry_piece(t, j)
-        part_of[0] = "Q%d" % t
-        if C["still"]:
-            act(T.RT[:, :], T.HB[:, 0:B], ACT.Relu, ["HB"], ["RT"], bias=2047.0, scale=-1.0)
-            for h in (0, 128):
-                mm([(T.HB[:, B + h:B + h + 128], T.RT[:, h:h + 128], T.IDF[:, :], ["RT", "IDF"])], "HB")
-            if t == 0:
-                cp(T.G[:, :], blk("HB", 1), ["HB"], ["G"])
-            else:
-                tt(T.G[:, :], blk("HB", 1), T.NN[:, :], ALU.mult, ["HB", "NN"], ["G"])
-        elif t == 0:
-            act(T.G[:, :], T.HB[:, 0:B], ACT.Relu, ["HB"], ["G"], bias=2047.0, scale=-1.0)
+        if nx:
+            crep(t + 1)
+        act(T.RT[:, :], T.HB[:, 0:B], ACT.Relu, ["HB"], ["RT"], bias=2047.0, scale=-1.0)
+        for h in (0, 128):
+            mm([(T.HB[:, B + h:B + h + 128], T.RT[:, h:h + 128], T.IDF[:, :], ["RT", "IDF"])], "HB", name="back")
+        gg, bo, tri = ("GH", "BOH", "TRH") if nx else ("G", "BOF", "TRI")
+        if t == 0:
+            cp(T[gg][:, :], blk("HB", 1), ["HB"], ["G"])
         else:
-            act(blk("HB", 1), T.HB[:, 0:B], ACT.Relu, ["HB"], ["HB"], bias=2047.0, scale=-1.0)
-            tt(T.G[:, :], blk("HB", 1), T.NN[:, :], ALU.mult, ["HB", "NN"], ["G"])
-        mm([(blk("TB", 0), T.BOF[:, :], T.G[:, :], ["BOF", "G"])], "TB")
-        mm([(blk("HB", 0), T.TRI[:, :], T.G[:, :], ["TRI", "G"])], "HB")
+            tt(T[gg][:, :], blk("HB", 1), T.NN[:, :], ALU.mult, ["HB", "NN"], ["G"])
+        mm([(blk("TB", 0), T[bo][:, :], T[gg][:, :], [bo, "G"])], "TB", name="all")
+        mm([(blk("HB", 0), T[tri][:, :], T[gg][:, :], [tri, "G"])], "HB", name="run")
         tt(T.UT[:, :], blk("TB", 0), blk("U", t % 2), ALU.mult, ["TB", "U%d" % (t % 2)], ["UT"])
         tt(T.NO[:, :], blk("HB", 0), T.UT[:, :], ALU.is_le, ["HB", "UT"], ["NO"])
         o = T.TB[:, B:B + 16]
         mm([(o, T.ID[:, :], T.IB[:, :], ["ID", "IB"])] + [(o, sel("DC", r), T.NO[:, r:B:16], ["DC", "NO"]) for r in range(16)],
-           "TB", True, False)
-        part_of[0] = "C%d" % t
-        mm([(o, T.IDB[:, :], T.H[:, 64:80], ["IDB", "H"])], "TB", False, True)
+           "TB", True, False, name="cnt")
+        mm([(o, T.IDB[:, :], T.H[:, 64:80], ["IDB", "H"])], "TB", False, True, name="stay")
         tt(T.IX[:, :], o, T.I17[:, :], ALU.min, ["TB", "I17"], ["IX"])
         cp(T.IXU[:, :], T.IX[:, :], ["IX"], ["IXU"])
-        dv, dt_ = (blk("XS", b), "XS%d" % b) if nx else (T.DF[:, 0:B], "DF0")
-        tt(dv, ind(T[ap][:, :], T.IXU[:, :]), cown(t), ALU.subtract, APALL + ["IXU", "CTo%d" % b], [dt_])
-        ts(T.SG[:, :], dv, -1.0, 1.0, ALU.max, ALU.min, [dt_], ["SG"])
-        tt(cown(t), T.SG[:, :], T.CB[:, 0:B], ALU.add, ["SG", "CB"], ["CTo%d" % b])
+        new = ind(T[ap][:, :], T.IXU[:, :])
+        if C["dv"][t] == "v":
+            tt(T.DV[:, :], new, cown(t), ALU.subtract, APALL + ["IXU", "CTo%d" % b], ["DV"])
+        else:
+            act(blk("XS", b), new, ACT.Copy, APALL + ["IXU"], ["XS%d" % b])
+            tt(T.DV[:, :], blk("XS", b), blk("CB", 2 * (t % 2)), ALU.subtract, ["XS%d" % b, "CB"], ["DV"])
+        ts(T.SG[:, :], T.DV[:, :], -1.0, 1.0, ALU.max, ALU.min, ["DV"], ["SG"])
+        tt(cown(t), T.SG[:, :], blk("CB", 2 * (t % 2)), ALU.add, ["SG", "CB"], ["CTo%d" % b])
         if nx:
             send_c(b * B, B, t, ["CTo%d" % b, "FR"])
-            part_of[0] = ""
-            dma("g", [(blk("XS", b), blk(ap, 16))], [ap + "x"], ["XS%d" % b], True)
-            crep(t + 1)
-        else:
-            act(blk("XS", b), ind(T[ap][:, :], T.IXU[:, :]), ACT.Copy, APALL + ["IXU"], ["XS%d" % b])
+        if C["dv"][t] == "v":
+            act(blk("XS", b), new, ACT.Copy, APALL + ["IXU"], ["XS%d" % b])
+        if not nx:
             dma("a", [(T.yx[:, b * B:(b + 1) * B], blk("XS", b))], ["XS%d" % b], [])
             dma("s", [(T.yc[:, b * B:(b + 1) * B], cown(t))], ["CTo%d" % b], [])
-        part_of[0] = "A%d" % t
         arrive(t)
         arrive_w(t)
         if not nx:
@@ -760,20 +735,17 @@ def calls(g, core, me, T, G, topo, pick):
             dma("g", [(T.yn[:, :], T.WF[2::16, 0:K * V])], ["WFn"], [])
             dma("s", [(T.yz[:, 5 * NC:6 * NC], T.PL[:, 5 * NC:6 * NC])], ["PL"], [])
             break
-        s = t + 1
-        e_lists(s)
-        part_of[0] = ""
-        n_tile(s)
-        payload(s)
-        tiles_p(s)
+        e_lists(t + 1)
+        n_tile(t + 1)
+        payload(t + 1)
+        tiles_p(t + 1)
         if t == 4:
             w = slice(0, K * V)
             dma("g", [(T.WF[0::16, w], T.W[0::16, w])], WALL, ["WFe"])
             dma("g", [(T.WF[2::16, w], T.W[2::16, w])], WALL, ["WFn"])
             dma("g", [(T.WF[0::16, w], T.W[1::16, w])], WALL, ["WFe"], True)
+            dma("s", [(T.yz[:, 0:5 * NC], T.PL[:, 0:5 * NC]), (T.yz[:, 6 * NC:ZP], T.PL[:, 6 * NC:ZP])], ["PL"], [])
         if t >= 2:
             dma("s", [(T.yc[:, b * B:(b + 1) * B], cown(t)), (T.yx[:, b * B:(b + 1) * B], blk("XS", b))],
                 ["CTo%d" % b, "XS%d" % b], [])
-        if t == R - 2:
-            dma("s", [(T.yz[:, 0:5 * NC], T.PL[:, 0:5 * NC]), (T.yz[:, 6 * NC:ZP], T.PL[:, 6 * NC:ZP])], ["PL"], [])
     return ops

@@ -9,12 +9,16 @@ XW_ = 592
 MAGIC = 6442450944.0
 BIG = 1.0e9
 CFG = {"nv": ["avaavaaa", "avaaaaaa"] * 3, "pv": ["avaavaaa", "aaaaaaaa"] * 3, "cut": [0, 64, 128, 192, 256], "fill": "vvvvgggggggddddd",
-       "slack": 300.0, "split": "vaaa", "half": 0.5,
+       "slack": 300.0, "split": "vaaa", "half": 0.5, "wide": 0, "th": "vvvvvv", "hi": "vvvvvv", "x2": 0, "pw": 0, "hx": "vvvvvv", "bulk": 0, "rt": "aaaaaa", "key": "hhhhhh",
        "pl": "aaaaaa", "yt": "vvvvvv", "ct": "aaaaaa", "y": "vaaaaa", "dv": "vvvvvv", "nb": ["aa"] * 4,
        "f": 1.25, "g": 1.56, "s": 3.8, "pe": 0.42, "dma": 1800.0, "rem": 2000.0, "row": 40.0, "bw": 20.0,
        "wake": 70.0, "fix": 55.0}
 ORDER = """
 a:AN4'> a:AN5'> v:MN3'> v:ACC'> a:AN7'> v:MU> v:W> p:mPL> v:TW> v:PJ_ v:c1_ s:NN> g:YF> v:MN4'> p:a1'> p:m1'> v:ACC.1'> v:MN5'> a:AN6'> p:a2'> v:MONE_ v:c0_ v:Wf1_ v:IDF_ s:AP'> v:MN7'> a:ID_ p:CB_ v:HU'> v:c2_ v:D1_ v:c6_ a:DC_ v:Wf2_ g:WFe> p:mEU> a:AP0'> v:c3_ s:PL_ v:ONES_ v:DW_ a:ID10_ a:IDB_ v:EH0_ v:EL0_ s:W0_ v:MN6'> v:BOF_ a:IDM_ v:c4_ a:CTT_ p:mHI_ a:DA_ p:m2'> a:c8_ a:DG_ p:a3'> v:C96_ a:ID8_ a:BO_ a:BOS_ a:c5_ a:B64_ a:BO2_ v:ACC.2'> p:m3'> v:MP0'> v:ACC.3'> v:A32'> v:KG'> p:mEU.1> a:ID64_ v:CODE'> v:HI.1_ v:NBF_ v:H'> v:L1'> v:S'> v:HU_ p:hc'> p:CB.1_ a:AP1'> v:L1U'> p:mEU.2> a:A8_ a:DM_ p:rank'> v:DF0_ v:INI_ g:C16_ g:NDC_ s:outPL> a:Y0_ v:REP_ a:IB_ a:I17_ v:DE_ a:AP3'> v:Wf15_ v:NBU0_ v:VV'> v:Q'> p:mUF_ a:BOM_ a:KO20_ p:mU_ p:YB_ p:YB'> g:WFn> a:AP4'> a:AP5'> g:K1_ g:KO1_ v:SEG_ v:ZERO_ v:X'> p:pv'> g:BI_ v:BOH_ a:AP2'> g:Wf4_ v:AM_ p:pq'> v:PY'> v:XB'> v:YT'> v:DIAG_ v:YT_ g:lf'> p:mEU_ p:mEU.3> a:AP6'> v:MP1'> a:c15_ s:EI0_<< v:MP4'> v:MP2'> g:lx'> v:MP3'> s:EI1_ s:ANo_ v:MP5'> p:h0'> v:MP6'> a:AP7'> v:MP7'> p:YB.1'> g:THR_ p:mU'> p:h1'> p:h2'> a:PW> a:TPL_ v:HX'> a:BC_ p:h3'> p:h4'> p:h5'> p:h6'> p:h7'> a:RT'> p:back'> p:back.1'> v:G'> a:DF'> p:mMS'> a:A8'> p:CB'> p:mPL'> s:CTo0_<< s:XS0_<< v:MU'> v:MS.1'> a:CTT'> p:mA'> v:MASK_ p:all'> g:lc_ p:run'> v:W'> a:PW'> s:NN'> v:UT'> v:NO'> g:WFe.1> v:WFe'> p:mEU.1_ p:mEU'> a:AP0 v:AP1 p:mEU.1'> a:AP3 a:AP2 s:AP0x_ s:XS1_ s:Wf15_ p:cnt'> p:stay'> v:IX'> v:IXU'> a:XS'> v:DV'> v:SG'> p:mEU.2_ p:CB.1'> v:CTo'> p:mEU.3_ s:JM_<< s:NBI0_<< v:MP0 p:YB.1_ p:mEU.3'> p:mEU.2'> v:AP4 v:MP1 v:MP4 g:lc'> g:Wf7_ v:MP3 g:outWF'>> s:outCT'>> a:outXS'>> s:NBI1_ v:MP2 v:EF1_ a:AP6 a:AP5 v:MP6 v:MP5 a:AP7 a:EH1_ p:mTC'> v:EF2_ g:Wf5_ g:Wf6_ p:mHI a:AN0 p:hc p:h0 p:mTC_ g:TRI_ p:h1 p:h2 p:h3 p:h4 a:AN2 a:AN3 s:outPL'> v:MP7 p:h5 p:h6 p:mEL_ p:h7 a:RT v:AN1 a:EH2_ g:Wf8_ s:Wf13_ p:CB a:AN5 p:a0 s:Wf12_ g:OC_ v:MNo v:MN0 a:AN6 v:MN1 v:HI.1 v:AN4 v:MN2 v:EF3_ v:MN3 v:TRH_ v:MN4 p:m0 p:mHI.1_ g:Wf9_ g:Wf10_ a:AN7 p:a1 v:HU v:INI p:back p:back.1 p:m1 g:LB_ g:J16_< v:G v:NBU' v:HI.3_ v:ACC s:outWF'> g:lf p:mEL.1_ g:PI_< p:all a:EH3_ p:a2 v:NBF v:HU.1_ v:MN5 v:MN6 v:ACC.1 v:UT v:MN7 s:W1_ p:run a:DF0_ p:m2 v:NBU s:XB0_ p:a3 s:XB a:CTT a:IDFM_ s:Wf11_ v:NO s:XB' g:YF0_ g:X143_< s:Wf14_ g:XG_< v:ACC.2 a:DF1_ a:BC.1_ p:m3 a:A8 p:mY_ p:cnt a:DF2_ a:KO g:HX_< p:mY'> a:DF g:YF'> v:ACC.3 v:A32 v:KG v:CODE v:H v:L1 p:stay v:IX v:S v:IXU p:CB.1 p:mEL.2_ g:PB_ p:YB v:DV v:SG v:CTo p:rank v:VV g:LM_ v:L1U v:Q v:X p:mY.1_ v:Wf0_< p:mUF p:pv p:pq v:PY p:mA v:XB p:mY.2_ v:CUT_ v:YT a:XS a:PF<< a:PW_ g:lc p:mTC p:mU p:mUF' v:NBF' a:KO' v:AN1' p:YB.1 p:mY v:Wf3_< s:ANo v:MNo' g:lx a:AN0' v:MN0' v:MN1' s:W3_ a:AN2' a:AN3' s:W2_ p:mHI' v:HI.1' s:AP v:HX p:a0' s:ANo' p:m0' v:INI' s:outCT v:MN2' p:mMS g:YF1_
+"""
+CFG.update({"key": "khkhkh", "pl": "vavava", "rt": "avavav", "yt": "vaaaaa", "ct": "vaaaaa", "nv": ["vvaaavaa", "avvaaaaa", "avaavaaa", "avvaaaaa", "avaavaaa", "avvaaaaa"], "pv": ["vavaaaaa", "aaaaaaaa", "vaaavaaa", "aaaaaaaa", "vaaavaaa", "aaaaaaaa"], "wide": 6, "x2": 1, "bulk": 1, "f": 1.2, "fix": 70.0, "wake": 100.0, "rem": 1700.0, "row": 32.0, "bw": 27.0, "dma": 1600.0})
+ORDER = """
+p:a1'> p:m1'> v:ONES_<< p:a2'> v:MN5'> g:YF1_> p:m2'> v:W> v:TW> v:PL> v:ACC.1'> s:NN> s:ANo'> p:mEU> a:AP1'_> g:WFe> a:AP0'_> v:MN7'> s:outPL> v:MN6'> a:AP1'> p:mEU.2> p:a3'> p:m3'> a:AP4'> a:AP0'> s:outCT> v:ACC.2'> a:AP5'_> v:NBF'> v:HU'> v:MP1'> v:ACC.3'> v:A32'> v:KG'> a:AP4'_> p:mEU.1> v:CODE'> a:AP2'_> a:AP3'> a:AP2'> a:AP3'_> v:L1'> v:H'> g:WFn> p:mEU.3> a:AP5'> s:AP'> g:lf'> p:YB'> v:S'> a:AP6'> a:AP6'_> v:MP0'> p:rank'> v:VV'> v:L1U'> p:pv'> v:Q'> p:pq'> v:X'> v:PY'> v:XB'> g:lx'> v:MP3'> v:MP2'> v:MP4'> a:AP7'> a:AP7'_> v:MP5'> a:YT'> p:hc'> v:MP6'> p:mU'> v:MP7'> p:h0'> p:h1'> a:KO'> p:h2'> p:h3'> p:h4'> p:h5'> p:h6'> p:h7'> p:YB.1'> v:RT'> p:back'> a:PW> v:HX'> a:DF'> p:back.1'> v:G'> p:mMS'> a:A8'> p:CB'> p:mA'> a:CTT'> v:MU'> v:W'> s:NN'> p:all'> p:run'> p:mPL'> a:PW'> v:UT'> v:MS.1'> p:mEU'> a:AP1 v:NO'> p:mEU.3'> p:cnt'> p:stay'> g:WFe.1> v:WFe'> v:AP0 v:IX'> v:IXU'> v:DV'> p:mEU.2'> a:AP6 a:XS'> a:AP7 p:mEU.3_ a:AP7_ v:SG'> p:mEU.1'> a:AP2 v:NBF_ v:HU_ a:AP3 p:mEU_ s:Wf12_ p:hc p:CB.1'> v:CTo'> g:lc'> a:AP1_ a:AP6_ a:AP5 v:NBU0_ v:AP0_ p:mEU.1_ p:mEU.2_ v:AP4 v:AP2_ p:mHI v:MP0 p:mTC'> g:outWF'>> a:AN0 v:MP2 v:DF0_ a:AP5_ a:AP4_ a:AN3 p:h0 v:MP1 p:h1 p:h2 a:outXS'>> s:outCT'>> v:MP7 a:Y0_ s:AP0x_ a:AP3_ a:KO20_ a:AN3_ p:YB_ v:AN0_ p:mUF_ v:YT_ p:YB.1_ v:MP4 v:MP3 s:Wf11_ s:Wf14_ v:MP5 v:MP6 p:h3 p:h4 p:h5 p:h6 p:h7 p:CB a:RT v:AN1 v:HI.1 v:MNo v:MN1 a:AN2_ v:AN1_ p:mHI.1_ v:AN5_ s:Wf13_ p:a0 p:back a:AN2 a:AN5 v:AN4 a:AN7 a:AN6 p:m0 p:back.1 v:HI.3_ v:MN3 a:AN7_ a:AN4_ g:lf p:a1 p:mU_ v:INI v:G v:HU.1_ a:AN6_ v:ACC p:m1 v:MN5 p:all s:Wf15_ g:YF0_ v:ACC.1 g:Wf10_ v:UT v:MN7 v:MN6 a:DF0_ v:NBF v:EF1_ p:a2 p:m2 p:run v:ACC.2 a:A8_ s:XB0_ a:CTT v:NO p:mY_ p:a3 p:m3 v:ACC.3 v:A32 v:HU a:EH1_ a:DF1_ v:KG v:KEY p:mUF p:CB.1 p:cnt a:PW_ a:KO a:A8 v:CODE p:stay v:IX s:XB a:DF2_ p:mY.1_ v:H v:IXU v:S v:DV p:mTC_ v:SG p:YB p:rank p:mEL.1_ s:outPL'> v:VV v:CTo s:outWF'> v:Q v:L1 v:L1U p:mY'> a:DF s:ANo s:AP g:lc p:pv a:YT p:mA p:pq v:PY v:NBU v:X s:XB' a:XS p:mEL_ p:mY p:mU v:NBU' v:XB p:YB.1 v:AN1' v:MNo' a:AN0' a:AN0'_ p:mTC a:PF< p:mHI' a:AN3' a:AN3'_ v:AN1'_ p:mY.2_ a:AN5' a:AN4' a:AN4'_ s:W3_ a:AN5'_ v:MN1' a:AN7'_ v:AN2' p:mUF' a:AN6' a:AN7' g:Wf4_ g:lx s:W1_ p:a0' p:m0' g:YF v:AN2'_ v:HX v:MN3' v:INI' v:HI.1' p:mMS g:YF'> s:EI0_<<< s:CTo0_<<< s:NBI0_<<< g:PI_<<< g:X143_<<< g:J16_<<< g:BI_<<< v:Wf0_<<< v:c1_<<< v:PJ_<<< v:Wf3_<<< g:XG_<<< g:C16_<<< v:c0_<<< v:IDF_<<< v:Wf1_<<< v:c2_<<< a:C96_<<< a:INI_<<< a:AM_<<< a:MONE_<<< a:SEG_<<< a:ID10_<<< a:ID_<<< a:c3_<<< a:IDM_<<< a:IB_<<< a:AN6'_ s:XS0_<<< s:PL_<<< v:EH0_<<< v:D1_<<< v:Wf2_<<< a:IDB_<<< a:IDFM_<<< v:EL0_<<< a:I17_<<< v:c6_<<< g:KO1_<<< s:W0_<<< s:JM_<<< g:lc_<<< a:DC_<<< p:CB_<<< a:DW_<<< a:ID8_<<< a:ID64_<<< v:BOF_<<< v:ACC' g:HX_<<< a:DM_<<< a:DA_<<< a:BOM_<<< a:B64_<<< a:BO_<<< v:CTT_<<< v:DIAG_<<< p:CB.1_<<< v:ZERO_<<< a:MASK_<<< a:TPL_<<< a:BOS_<<< v:c4_<<< a:DE_<<< a:c15_<<< a:BO2_<<< a:c5_<<< a:c8_<<< a:BC_<<< v:BOH_<<< v:REP_<<< v:IDH_<<< a:DG_<<< g:TRI_<<< v:MU g:Wf9_<<< g:K1_<<< p:mHI_<<< v:TRH_<<< g:PB_<<< g:NDC_<<< g:Wf6_<<< g:LB_<<< a:BC.1_<<< g:LM_<<< g:Wf8_<<< s:ANo_<<< s:XS1_<<< s:EI1_<<< s:NBI1_<<< g:Wf7_<<< g:OC_<<< g:THR_<<< g:Wf5_<<< v:Wf15_<<< v:HI.1_<<<
 """
 
 f32, bf, f16, i32, u16 = "float32", "bfloat16", "float16", "int32", "uint16"
@@ -25,15 +29,15 @@ for _n, _w, _d in [
     ("NBI", V, i32), ("NBU", V, u16), ("TC", V, f32), ("KO2", V, bf), ("A8", B, bf), ("NBF", B, f32),
     ("EI", V, i32), ("EF", V, f32), ("EH", V, bf), ("EL", V, bf), ("EU", B, u16), ("NN", B, bf),
     ("XB0", XW_, f32), ("XB1", XW_, f32), ("XB2", XW_, f32), ("XB3", XW_, f32), ("XB4", XW_, f32), ("XB5", XW_, f32),
-    ("PI", 4, i32), ("PJ", 8, i32), ("COL", 16, f32), ("REP", 8, u16), ("X143", 144, f32), ("XG", 128, f32), ("J16", B, f32),
+    ("PI", 8, i32), ("RH", B, f16), ("IDH", 128, f16), ("COL", 16, f32), ("REP", 8, u16), ("X143", 144, f32), ("XG", 128, f32), ("J16", B, f32),
     ("DM", 144, bf), ("DA", 144, bf), ("DE", 144, bf), ("DW", 144, bf), ("DC", 144, bf), ("GH", B, f16), ("TRH", 128, f16),
     ("BOH", 128, f16), ("D1", 144, bf), ("ID", 128, bf), ("IDM", 128, bf), ("IDF", 128, f32), ("IDFM", 128, f32),
     ("ID8", 128, bf), ("ID10", 128, bf), ("ID64", 128, bf), ("IDB", 128, bf), ("DG", 128, bf), ("ONES", V, bf), ("ZERO", B, bf),
     ("BO", 128, bf), ("BOM", 128, bf), ("BO2", 8, bf), ("BOF", 128, f32),
     ("BOS", 128, f32), ("B64", 128, f32), ("TRI", 128, f32), ("LB", 128, bf), ("LM", 128, bf),
-    ("MASK", NC, bf), ("DIAG", B, f32), ("SEG", 80, bf), ("CUT", NC, f32), ("KO1", B, bf), ("K1", B, bf), ("OC", 80, f32),
-    ("C16", 16, bf), ("IB", 16, bf), ("I17", 16, f32), ("MONE", 32, bf), ("NDC", 64, bf), ("THR", 64, f32),
-    ("TPL", NC, f32), ("PB", NC, bf), ("PW", NC, bf), ("PF", NC, f32), ("BI", 8, f32), ("BC", 8, f32),
+    ("MASK", NC, bf), ("DIAG", B, f32), ("SEG", NC, bf), ("KO1", B, bf), ("K1", B, bf), ("OC", 80, f32),
+    ("C16", 16, bf), ("IB", 16, bf), ("I17", 16, f32), ("MONE", 48, bf), ("NDC", 64, bf), ("THR", 64, f32),
+    ("TPL", NC, f32), ("PB", NC, bf), ("PW", 6 * NC, bf), ("BC", 16, f32),
     ("HI", 48, i32), ("HU", 48, u16), ("DF", 768, bf), ("UF", B, bf), ("U", 2 * B, bf), ("YT", B, bf), ("CTT", B, bf),
     ("INI", 64, f32), ("ACC", 64, f32), ("A32", 32, f32),
     ("KG", 16, i32), ("CODE", 16, i32), ("L1", 16, i32), ("L1U", 16, u16), ("H", 80, bf), ("S", 80, bf),
@@ -54,7 +58,7 @@ def arrange(ops):
     n = len(ops)
     words = ORDER.split()
     place = {x.rstrip("<>"): x.count(">") - x.count("<") + k / len(words) for k, x in enumerate(words)}
-    key = [place.get(o[6], -9.0) + (o[7] or 0) // 2 for o in ops]
+    key = [place.get(o[6] + "_" * (o[7] in (0, R - 1) and o[6][:4] in ("a:AN", "v:AN", "a:AP", "v:AP")), place.get(o[6], -9.0)) + (o[7] or 0) // 2 for o in ops]
     last, readers, pred, uses = {}, {}, [], {}
     for i, (q, fn, rd, wr, own, c, name, step) in enumerate(ops):
         need = set()
@@ -341,6 +345,17 @@ def calls(g, core, me, T, G, topo, pick):
             return [RemoteDMATransfer(dst_ids=[ids[q]], dma_engine_mask=sum(1 << e for e in eng[d * part:(d + 1) * part]),
                                       remote_sem=G.sem["ax%d" % t], src=xb[:, NC + CAP * d:NC + CAP * (d + 1)],
                                       dst=xb[:, CAP * (2 - d):CAP * (3 - d)]) for d, q in enumerate(peers)]
+        if C["x2"]:
+            def tr(d, es):
+                return RemoteDMATransfer(dst_ids=[ids[peers[d]]], dma_engine_mask=sum(1 << e for e in es),
+                                         remote_sem=G.sem["ax%d" % t], src=xb[:, NC + CAP * d:NC + CAP * (d + 1)],
+                                         dst=xb[:, CAP * (2 - d):CAP * (3 - d)])
+            far = sorted(range(3), key=lambda d: topo.die(G.cores[peers[d]]) == topo.die(core))
+            op("g", [lambda: g.remote_dma_fused([tr(far[0], eng[:2 * part]), tr(far[1], eng[2 * part:])], local_sem=G.sem["lx%d" % t]),
+                     lambda: g.remote_dma_fused([tr(far[2], eng)], local_sem=G.sem["lx%d" % t])],
+               ["XB%d" % t], [], ("lx%d" % t, 8 * part), (1000.0, C["rem"], moved(384, 384 * 192, len(eng))))
+            op("x", None, [], ["XL%d" % t], ("ax%d" % t, 8 * part))
+            return
         op("g", [lambda: g.remote_dma_fused(trs(), local_sem=G.sem["lx%d" % t])], ["XB%d" % t], [], ("lx%d" % t, 3 * part),
            (500.0, C["rem"], moved(128, 128 * 192, part)))
         op("x", None, [], ["XL%d" % t], ("ax%d" % t, 3 * part))
@@ -375,10 +390,16 @@ def calls(g, core, me, T, G, topo, pick):
         n = (t1 - t0) * B
         c, tags = n // 16, ["Y%d" % t for t in range(t0, t1)]
         ps, bank = lend("HI")
-        mm([(ps[:, 0:c], sel("DW", r), T.XS[:, xlo + r:xlo + n:16], ["DW"] + rd) for r in range(16)], bank, after=["HI"])
-        cp(T.HI[:, 0:c], ps[:, 0:c], [bank], ["HI"])
-        ts(T.HI[:, 0:c], T.HI[:, 0:c], M - 1, None, ALU.bitwise_and, None, ["HI"], ["HI"])
-        cp(T.HU[:, 0:c], T.HI[:, 0:c], ["HI"], ["HU"])
+        if C["hi"][t0] == "v":
+            mm([(ps[:, 0:c], sel("DW", r), T.XS[:, xlo + r:xlo + n:16], ["DW"] + rd) for r in range(16)], bank, after=["HI"])
+            cp(T.HI[:, 0:c], ps[:, 0:c], [bank], ["HI"])
+            ts(T.HI[:, 0:c], T.HI[:, 0:c], M - 1, None, ALU.bitwise_and, None, ["HI"], ["HI"])
+            cp(T.HU[:, 0:c], T.HI[:, 0:c], ["HI"], ["HU"])
+        else:
+            mm([(ps[:, 0:c], sel("DW", r), T.XS[:, xlo + r:xlo + n:16], ["DW"] + rd) for r in range(16)], bank, after=["HI", "HU"])
+            act(T.SG[:, 0:c], ps[:, 0:c], ACT.Identity, [bank], ["HI", "SG"], bias=1024.0 - 255.5 / 64, scale=1.0 / 64)
+            mm([(ps[:, 0:c], T.ID64[:, :], T.SG[:, 0:c], ["ID64", "SG"])], bank, False, True, name="mod")
+            ts(T.HU[:, 0:c], ps[:, 0:c], 65536.0, None, ALU.add, None, [bank], ["HU"])
         for t in range(t0, t1):
             lo = (t - t0) * B
             df, tg, x = T.DF[:, lo:lo + B], "DF%d" % (t - t0), T.XS[:, xlo + lo:xlo + lo + B]
@@ -458,16 +479,21 @@ def calls(g, core, me, T, G, topo, pick):
         mm([(o, T.BO[:, :], blk("Y", t), ["BO", "Y%d" % t]), (o, T.ID64[:, :], T.UF[:, :], ["ID64", "UF"])], bank, after=[u])
         act(blk("U", t % 2), o, ACT.Identity, [bank], [u], bias=64.0 * 192)
 
-    def twice(e, src, c, rd, stage, bank, lo=0):
+    def twice(e, src, c, rd, stage, bank, lo=0, n=2):
         turn([(T[bank][:, lo + h:lo + h + 128], T[src][:, c + h:c + h + 128]) for h in (0, 128)], rd, bank)
         move(e, T[stage][:, :], T[bank][:, lo:lo + B], [bank], [stage])
-        turn([(T[bank][:, lo + h:lo + h + 128], T[stage][:, h % B:h % B + 128]) for h in range(0, 2 * B, 128)], [stage], bank)
+        turn([(T[bank][:, lo + h:lo + h + 128], T[stage][:, h % B:h % B + 128]) for h in range(0, n * B, 128)], [stage], bank)
 
     def yrep(t):
-        twice(C["yt"][t], "Y", B * t, ["Y%d" % t], "YT", "YB")
+        twice(C["yt"][t], "Y", B * t, ["Y%d" % t], "YT", "YB", 0, 4 if C["wide"] else 2)
 
     def crep(t):
         twice(C["ct"][t], "CT", own0 + B * (t % 4), ["CTo%d" % (t % 4)], "CTT", "CB", 2 * B * (t % 2))
+        if C["dv"][t] == "m":
+            act(blk("CM", t % 2), cown(t), ACT.Identity, ["CTo%d" % (t % 4)], ["CM%d" % (t % 2)], bias=-1.0)
+            act(blk("CM", 2), T.CTT[:, :], ACT.Identity, ["CTT"], ["CP"], bias=1.0)
+            turn([(T.YB[:, B * (2 + t % 2) + h:B * (2 + t % 2) + h + 128], T.CM[:, 2 * B + h:2 * B + h + 128]) for h in (0, 128)],
+                 ["CP"], "YB")
 
     def tiles_n(t):
         dma("s", [(T.AN[:, 0:B], cown(t))], ["CTo%d" % (t % 4)], ["ANo"])
@@ -477,12 +503,14 @@ def calls(g, core, me, T, G, topo, pick):
         dma("s", [(blk(ap, 16), cown(t)), (blk(ap, 17), blk("Y", t))], ["CTo%d" % (t % 4), "Y%d" % t], [ap + "x"])
 
     def payload(t):
+        if C["pw"] and t < 5:
+            return
         if t < 4:
-            act(T.PW[:, :], T.PB[:, :], ACT.Identity, ["PB", "BC", "DIAG"], ["PW"], bias=T.BC[:, t:t + 1], scale=on(1))
+            act(T.PW[:, 0:NC], T.PB[:, :], ACT.Identity, ["PB", "BC", "DIAG"], ["PW"], bias=T.BC[:, t:t + 1], scale=on(1))
         elif t == 4:
-            act(T.PW[:, :], T.PB[:, :], ACT.Identity, ["PB", "DIAG"], ["PW"], scale=on(1))
+            act(T.PW[:, 0:NC], T.PB[:, :], ACT.Identity, ["PB", "DIAG"], ["PW"], scale=on(1))
         else:
-            act(T.PF[:, :], T.PB[:, :], ACT.Identity, ["PB", "DIAG"], ["PF"], scale=on(0))
+            act(T.NBF[:, 0:NC], T.PB[:, :], ACT.Identity, ["PB", "DIAG"], ["PF", "NBF"], scale=on(0))
 
     def template(t):
         dma("s", [(T["XB%d" % t][:, 144:336], T.TPL[:, :])], ["TPL"], ["XB%d" % t])
@@ -496,11 +524,15 @@ def calls(g, core, me, T, G, topo, pick):
 
     def arrive(t):
         xb, tg = T["XB%d" % t], ["XB%d" % t, "XL%d" % t]
-        ts(T.HX[:, :], xb[:, 0:NC], MAGIC, MAGIC, ALU.add, ALU.subtract, tg, ["HX"])
+        if C["hx"][t] == "v":
+            ts(T.HX[:, :], xb[:, 0:NC], MAGIC, MAGIC, ALU.add, ALU.subtract, tg, ["HX"])
+        else:
+            act(T.HX[:, :], xb[:, 0:NC], ACT.Identity, tg, ["HX"], bias=MAGIC)
+            act(T.HX[:, :], T.HX[:, :], ACT.Identity, ["HX"], ["HX"], bias=-MAGIC)
         ps, bank = lend("MS")
         o = ps[:, 0:NC]
         mm([(o, T.ID[:, :], T.MASK[:, :], ["ID", "MASK"]), (o, T.BOS[:, :], T.HX[:, :], ["BOS", "HX"])], bank)
-        scan(T.MS[:, :], T.CUT[:, :], o, ALU.add, ALU.max, ["CUT", bank], ["MS"])
+        scan(T.MS[:, :], T.SEG[:, :], o, ALU.mult, ALU.max, ["SEG", bank], ["MS"])
         cp(T.MU[:, :], T.MS[:, 15:NC:16], ["MS"], ["MU"])
         cuts = [(NC - n1, 0, n1)] * (n1 > 0) + [(0, n1, NC - n1)]
         if C["pl"][t] == "v":
@@ -517,14 +549,14 @@ def calls(g, core, me, T, G, topo, pick):
 
     def arrive_w(t):
         if t < 4:
-            cp(ind(T.W[:, :], T.MU[:, :]), T.PW[:, :], ["MU", "PW"], WALL)
+            cp(ind(T.W[:, :], T.MU[:, :]), T.PW[:, NC * t * C["pw"]:NC * (t * C["pw"] + 1)], ["MU", "PW"], WALL)
             return
         tw = "TW" if t == 4 else "MS"
         ts(T[tw][:, :], ind(T.W[:, :], T.MU[:, :]), col(5), T.BC[:, t:t + 1], ALU.mult, ALU.add, ["MU", "c5", "BC"] + WALL, [tw])
         if t == 4:
-            tt(ind(T.W[:, :], T.MU[:, :]), T.TW[:, :], T.PW[:, :], ALU.add, ["MU", "PW", "TW"], WALL)
+            tt(ind(T.W[:, :], T.MU[:, :]), T.TW[:, :], T.PW[:, NC * t * C["pw"]:NC * (t * C["pw"] + 1)], ALU.add, ["MU", "PW", "TW"], WALL)
         else:
-            tt(ind(T.WF[:, :], T.MU[:, :]), T.MS[:, :], T.PF[:, :], ALU.add, ["MU", "PF", "MS"], ["WFe", "WFn"])
+            tt(ind(T.WF[:, :], T.MU[:, :]), T.MS[:, :], T.NBF[:, 0:NC], ALU.add, ["MU", "PF", "MS"], ["WFe", "WFn"])
 
     def entry_piece(t, j):
         ap, ct, c0 = "AP%d" % (t % 2), "CTo%d" % (t % 4), own0 + B * (t % 4)
@@ -570,17 +602,17 @@ def calls(g, core, me, T, G, topo, pick):
         iota("PB", 0, n1, [[1, n1]], NC - n1)
     iota("PB", n1, NC, [[1, NC - n1]], 0)
     join(2 if n1 else 1)
-    iota("BI", 0, 8, [[NC, 8]])
-    ts(T.PJ[:, 0:4], T.PI[:, :], 15, None, ALU.bitwise_and, None, ["PI"], ["PJ"])
+    iota("BC", 8, 16, [[NC, 8]], tag="BI")
+    ts(T.PI[:, 4:8], T.PI[:, 0:4], 15, None, ALU.bitwise_and, None, ["PI"], ["PJ"])
     cp(col(1), T.PI[:, 0:1], ["PI"], ["c1"])
-    cp(col(0), T.PJ[:, 0:1], ["PJ"], ["c0"])
+    cp(col(0), T.PI[:, 4:5], ["PJ"], ["c0"])
     ts(col(2), col(1), col(0), 15.0, ALU.subtract, ALU.add, ["c0", "c1"], ["c2"])
-    ts(col(3), col(0), 2.0, 1.0, ALU.mult, ALU.add, ["c0"], ["c3"])
+    act(col(3), col(0), ACT.Identity, ["c0"], ["c3"], bias=1.0, scale=2.0)
     ts(col(4), col(0), 2.0, None, ALU.is_lt, None, ["c0"], ["c4"])
-    dmat("DW", col(3), ["c3"])
     ts(T.IDF[:, :], T.X143[:, 0:128], col(1), None, ALU.is_equal, None, ["X143", "c1"], ["IDF"])
-    dmat("D1", 1.0)
-    dmat("DE", col(4), ["c4"])
+    ts(T.D1[:, :], T.X143[:, :], col(2), None, ALU.is_equal, None, ["X143", "c2"], ["D1"])
+    act(T.DW[:, :], T.D1[:, :], ACT.Identity, ["D1", "c3"], ["DW"], scale=col(3))
+    act(T.DE[:, :], T.D1[:, :], ACT.Identity, ["D1", "c4"], ["DE"], scale=col(4))
     ts(col(6), col(2), -15.0, 0.0625, ALU.add, ALU.mult, ["c2"], ["c6"])
     ts(T.BOF[:, :], T.XG[:, :], col(6), None, ALU.is_equal, None, ["XG", "c6"], ["BOF"])
     for nm, src, w in [("ID", "IDF", 1.0), ("IDM", "IDF", -1.0), ("DA", "D1", -2048.0), ("DM", "D1", 4096.0),
@@ -593,26 +625,31 @@ def calls(g, core, me, T, G, topo, pick):
     pool(lambda: g.affine_select(T.LB[:, :], T.BOM[:, :], [[-1, 128]], ALU.is_ge, 0.0, 0, 1), 128, ["BOM"], ["LB"])
     pool(lambda: g.affine_select(T.LM[:, :], T.LB[:, :], [[-1, 128]], ALU.not_equal, -65.0, 0, 1), 128, ["LB"], ["LM"])
     pool(lambda: g.affine_select(T.TRI[:, :], T.B64[:, :], [[1, 128]], ALU.is_ge, 0.0, 0, -1), 128, ["B64"], ["TRI"])
-    fill(T.AM[:, :], 0.0, ["AM"])
-    fill(T.INI[:, :], BIG, ["INI"])
-    fill(T.MONE[:, 16:32], -96.0, ["C96"])
-    fill(T.MONE[:, 0:16], -1.0, ["MONE"])
+    for ap, w, x, tag in [(T.AM[:, :], 1, 0.0, "AM"), (T.INI[:, :], 64, BIG, "INI"), (T.MONE[:, 16:32], 16, -96.0, "C96"),
+                          (T.MONE[:, 0:16], 16, -1.0, "MONE")]:
+        act(ap, T.X143[:, 0:w], ACT.Identity, ["X143"], [tag], bias=x, scale=0.0)
     ts(T.REP[:, :], T.X143[:, 0:8], 0.0, col(0), ALU.mult, ALU.add, ["X143", "c0"], ["REP"])
-    ts(T.MASK[:, :], T.J16[:, 0:NC], col(0), -32768.0, ALU.not_equal, ALU.mult, ["J16", "c0"], ["MASK"])
-    ts(T.CUT[:, :], T.J16[:, 0:NC], 0.0, -65536.0, ALU.is_equal, ALU.mult, ["J16"], ["CUT"])
     ts(T.DIAG[:, :], T.J16[:, :], col(0), None, ALU.is_equal, None, ["J16", "c0"], ["DIAG"])
+    act(T.MASK[:, :], T.DIAG[:, 0:NC], ACT.Identity, ["DIAG"], ["MASK"], bias=-32768.0, scale=32768.0)
     cp(T.TRH[:, :], T.TRI[:, :], ["TRI"], ["TRH"])
     cp(T.BOH[:, :], T.BO[:, :], ["BO"], ["BOH"])
-    ts(T.SEG[:, :], T.J16[:, 0:80], 0.0, None, ALU.not_equal, None, ["J16"], ["SEG"])
+    if "v" in C["rt"]:
+        cp(T.IDH[:, :], T.IDM[:, :], ["IDM"], ["IDH"])
+    act(T.SEG[:, :], T.J16[:, 0:NC], ACT.Sign, ["J16"], ["SEG"])
     act(T.IB[:, :], T.C16[:, :], ACT.Identity, ["C16", "c0"], ["IB"], bias=col(0))
     act(T.I17[:, :], T.IB[:, :], ACT.Identity, ["IB"], ["I17"], bias=17.0 * B)
     act(col(8), col(0), ACT.Identity, ["c0"], ["c8"], bias=-float(NC), scale=-1.0)
     act(T.DG[:, :], T.IDF[:, :], ACT.Identity, ["IDF", "c8"], ["DG"], scale=col(8))
     act(col(5), col(4), ACT.Identity, ["c4"], ["c5"], bias=1.0, scale=-1.0)
     act(col(15), col(4), ACT.Identity, ["c4"], ["c15"], bias=2.0, scale=-2.0)
-    act(T.BC[:, 0:4], T.BI[:, 0:4], ACT.Identity, ["BI", "DIAG", "c15"], ["BC"], bias=col(15), scale=on(0))
-    act(T.BC[:, 4:8], T.BI[:, 4:8], ACT.Identity, ["BI", "DIAG", "c5"], ["BC"], bias=col(5), scale=on(0))
+    act(T.BC[:, 0:4], T.BC[:, 8:12], ACT.Identity, ["BI", "DIAG", "c15"], ["BC"], bias=col(15), scale=on(0))
+    act(T.BC[:, 4:8], T.BC[:, 12:16], ACT.Identity, ["BI", "DIAG", "c5"], ["BC"], bias=col(5), scale=on(0))
     act(T.TPL[:, :], T.HX[:, :], ACT.Identity, ["HX", "DIAG"], ["TPL"], scale=on(0))
+    if C["pw"]:
+        iota("PW", 0, 4 * NC, [[NC, 4], [0, NC]], tag="PWa")
+        iota("PW", 4 * NC, 6 * NC, [[2, 2], [0, NC]], tag="PWb")
+        dma("s", [(T.PW[1::16, NC * t:NC * (t + 1)], T.PB[1::16, :]) for t in range(5)] +
+            [(T.PW[2::16, NC * t:NC * (t + 1)], T.PW[3::16, 5 * NC:6 * NC]) for t in range(4)], ["PB", "PWa", "PWb"], ["PW"])
     ent_split(0)
     e_lists(0)
     crep(0)
@@ -627,7 +664,17 @@ def calls(g, core, me, T, G, topo, pick):
     y_make(B, 1, 4, ["XS1", "XS2", "XS3"])
     fill(T.W[:, K * V:WW], 1.0, ["Wf15"])
     w_fill(4, 16)
-    for b in (1, 2, 3):
+    if C["bulk"]:
+        cp(T.EF[:, B:V], T.EI[:, B:V], ["EI1", "EI2", "EI3"], ["EF1"])
+        act(T.EH[:, B:V], T.EF[:, B:V], ACT.Copy, ["EF1"], ["EH1"])
+        for b0, b1 in ((1, 3), (3, 4)):
+            ps, bank = lend("EL")
+            o, w = ps[:, 0:B * (b1 - b0)], slice(b0 * B, b1 * B)
+            mm([(o, T.IDF[:, :], T.EF[:, w], ["IDF", "EF1"]), (o, T.IDM[:, :], T.EH[:, w], ["IDM", "EH1"])], bank)
+            act(T.EL[:, w], o, ACT.Copy, [bank], ["EL%d" % b0])
+            dma("s", [(T.W[x::16, b * K * B:(b + 1) * K * B], blk(("EH", "EL")[x], b)) for b in range(b0, b1) for x in (0, 1)],
+                ["EH1", "EL%d" % b0], ["W%d" % b for b in range(b0, b1)] + ["Wf%d" % x for x in range(4 * b0, 4 * b1)])
+    for b in (1, 2, 3)[3 * C["bulk"]:]:
         ent_split(b)
 
     for t in range(R):
@@ -641,7 +688,11 @@ def calls(g, core, me, T, G, topo, pick):
             lo = B + 2 * B * j
             move(C["nv"][t][j], T.AN[:, lo:lo + 2 * B], ind(T.CT[:, :], T.NBU[:, b * B + 32 * j:b * B + 32 * j + 32]),
                  CTALL + ["NBU%d" % b], ["AN%d" % j])
-            tt(T.MN[:, lo:lo + 2 * B], T.AN[:, lo:lo + 2 * B], T.YB[:, 0:2 * B], ALU.max, ["AN%d" % j, "YB"], ["MN%d" % j])
+            if j >= C["wide"]:
+                tt(T.MN[:, lo:lo + 2 * B], T.AN[:, lo:lo + 2 * B], T.YB[:, 0:2 * B], ALU.max, ["AN%d" % j, "YB"], ["MN%d" % j])
+            elif j % 2:
+                tt(T.MN[:, lo - 2 * B:lo + 2 * B], T.AN[:, lo - 2 * B:lo + 2 * B], T.YB[:, :], ALU.max,
+                   ["AN%d" % (j - 1), "AN%d" % j, "YB"], ["MN%d" % j, "MN%d" % (j - 1)])
             if j % 2 == 1:
                 q = j // 2
                 bank = BANKS[q % 2]
@@ -655,7 +706,10 @@ def calls(g, core, me, T, G, topo, pick):
                 mm([(out, sel("DM", r), T.MN[:, c0 + r:c1:16], ["DM", "MN%d" % (j - 1), "MN%d" % j] + ["MNo"] * (q == 0))
                     for r in range(16)], bank, False, True, name="m%d" % q)
                 if q == 0:
-                    ts(T.INI[:, 0:16], T.K0[:, 0:16], T.AM[:, :], None, ALU.add, None, ["K0", "AM"], ["INI"])
+                    if C["th"][t] == "v":
+                        ts(T.INI[:, 0:16], T.K0[:, 0:16], T.AM[:, :], None, ALU.add, None, ["K0", "AM"], ["INI"])
+                    else:
+                        act(T.INI[:, 0:16], T.K0[:, 0:16], ACT.Identity, ["K0", "AM"], ["INI"], bias=T.AM[:, :])
                     tt(T.ACC[:, :], T.K0[:, 16:80], T.INI[:, :], ALU.min, ["K0", "INI"], ["ACC"])
                 else:
                     tt(T.ACC[:, :], T[bank][:, 0:64], T.ACC[:, :], ALU.min, [bank, "ACC"], ["ACC"])
@@ -663,9 +717,11 @@ def calls(g, core, me, T, G, topo, pick):
             send_free(t)
         tt(T.A32[:, :], T.ACC[:, 0:32], T.ACC[:, 32:64], ALU.min, ["ACC"], ["A32"])
         tt(T.KG[:, :], T.A32[:, 0:16], T.A32[:, 16:32], ALU.min, ["A32"], ["KG"])
+        if C["key"][t] == "k":
+            tt(T.MONE[:, 32:48], T.KG[:, :], T.INI[:, 0:16], ALU.is_ge, ["KG", "INI"], ["KEY"])
         ts(T.CODE[:, :], T.KG[:, :], 7, None, ALU.bitwise_and, None, ["KG"], ["CODE"])
         tt(T.H[:, :], ind(T.CODE[:, :], T.REP[:, 0:5]), T.OC[:, :], ALU.is_equal, ["CODE", "REP", "OC"], ["H"])
-        scan(T.S[:, :], T.SEG[:, :], T.H[:, :], ALU.mult, ALU.add, ["SEG", "H"], ["S"])
+        scan(T.S[:, :], T.SEG[:, 0:80], T.H[:, :], ALU.mult, ALU.add, ["SEG", "H"], ["S"])
         o = T.K0[:, 0:64]
         mm([(o, T.ID[:, :], T.NDC[:, :], ["ID", "NDC"]), (o, T.LM[:, :], T.H[:, 0:64], ["LM", "H"]),
             (o, T.BO[:, :], T.S[:, 0:64], ["BO", "S"])], "K0", name="rank")
@@ -695,9 +751,14 @@ def calls(g, core, me, T, G, topo, pick):
             entry_piece(t, j)
         if nx:
             crep(t + 1)
-        act(T.RT[:, :], T.HB[:, 0:B], ACT.Relu, ["HB"], ["RT"], bias=2047.0, scale=-1.0)
-        for h in (0, 128):
-            mm([(T.HB[:, B + h:B + h + 128], T.RT[:, h:h + 128], T.IDF[:, :], ["RT", "IDF"])], "HB", name="back")
+        if C["rt"][t] == "a":
+            act(T.RT[:, :], T.HB[:, 0:B], ACT.Relu, ["HB"], ["RT"], bias=2047.0, scale=-1.0)
+            for h in (0, 128):
+                mm([(T.HB[:, B + h:B + h + 128], T.RT[:, h:h + 128], T.IDF[:, :], ["RT", "IDF"])], "HB", name="back")
+        else:
+            ts(T.RH[:, :], T.HB[:, 0:B], 2047.0, 2047.0, ALU.min, ALU.subtract, ["HB"], ["RT"])
+            mm([(T.HB[:, B:B + 128], T.RH[:, 0:128], T.IDH[:, :], ["RT", "IDH"])], "HB", name="back")
+            mm([(T.HB[:, B + 128:2 * B], T.RH[:, 128:B], T.IDH[:, :], ["RT", "IDH"])], "HB", name="back")
         gg, bo, tri = ("GH", "BOH", "TRH") if nx else ("G", "BOF", "TRI")
         if t == 0:
             cp(T[gg][:, :], blk("HB", 1), ["HB"], ["G"])
@@ -710,21 +771,31 @@ def calls(g, core, me, T, G, topo, pick):
         o = T.TB[:, B:B + 16]
         mm([(o, T.ID[:, :], T.IB[:, :], ["ID", "IB"])] + [(o, sel("DC", r), T.NO[:, r:B:16], ["DC", "NO"]) for r in range(16)],
            "TB", True, False, name="cnt")
-        mm([(o, T.IDB[:, :], T.H[:, 64:80], ["IDB", "H"])], "TB", False, True, name="stay")
+        if C["key"][t] == "k":
+            mm([(o, T.IDB[:, :], T.MONE[:, 32:48], ["IDB", "KEY"])], "TB", False, True, name="stay")
+        else:
+            mm([(o, T.IDB[:, :], T.H[:, 64:80], ["IDB", "H"])], "TB", False, True, name="stay")
         tt(T.IX[:, :], o, T.I17[:, :], ALU.min, ["TB", "I17"], ["IX"])
         cp(T.IXU[:, :], T.IX[:, :], ["IX"], ["IXU"])
         new = ind(T[ap][:, :], T.IXU[:, :])
-        if C["dv"][t] == "v":
-            tt(T.DV[:, :], new, cown(t), ALU.subtract, APALL + ["IXU", "CTo%d" % b], ["DV"])
+        dv, dt_ = (blk("XS", b), ["DV", "XS%d" % b]) if C["dv"][t] == "d" else (T.DV[:, :], ["DV"])
+        if C["dv"][t] == "m":
+            tt(T.DV[:, :], new, blk("CM", t % 2), ALU.max, APALL + ["IXU", "CM%d" % (t % 2)], ["DV"])
+            tt(cown(t), T.DV[:, :], blk("YB", 2 + t % 2), ALU.min, ["DV", "YB"], ["CTo%d" % b])
         else:
-            act(blk("XS", b), new, ACT.Copy, APALL + ["IXU"], ["XS%d" % b])
-            tt(T.DV[:, :], blk("XS", b), blk("CB", 2 * (t % 2)), ALU.subtract, ["XS%d" % b, "CB"], ["DV"])
-        ts(T.SG[:, :], T.DV[:, :], -1.0, 1.0, ALU.max, ALU.min, ["DV"], ["SG"])
-        tt(cown(t), T.SG[:, :], blk("CB", 2 * (t % 2)), ALU.add, ["SG", "CB"], ["CTo%d" % b])
+            if C["dv"][t] != "a":
+                tt(dv, new, cown(t), ALU.subtract, APALL + ["IXU", "CTo%d" % b], dt_)
+            else:
+                act(blk("XS", b), new, ACT.Copy, APALL + ["IXU"], ["XS%d" % b])
+                tt(T.DV[:, :], blk("XS", b), blk("CB", 2 * (t % 2)), ALU.subtract, ["XS%d" % b, "CB"], ["DV"])
+            ts(T.SG[:, :], dv, -1.0, 1.0, ALU.max, ALU.min, dt_, ["SG"])
+            tt(cown(t), T.SG[:, :], blk("CB", 2 * (t % 2)), ALU.add, ["SG", "CB"], ["CTo%d" % b])
         if nx:
             send_c(b * B, B, t, ["CTo%d" % b, "FR"])
-        if C["dv"][t] == "v":
+        if C["dv"][t] in "vm":
             act(blk("XS", b), new, ACT.Copy, APALL + ["IXU"], ["XS%d" % b])
+        if C["dv"][t] == "d":
+            dma("g", [(blk("XS", b), blk(ap, 16))], [ap + "x"], ["XS%d" % b], True)
         if not nx:
             dma("a", [(T.yx[:, b * B:(b + 1) * B], blk("XS", b))], ["XS%d" % b], [])
             dma("s", [(T.yc[:, b * B:(b + 1) * B], cown(t))], ["CTo%d" % b], [])

import numpy as np
from concourse.bass import DstId, RemoteDMATransfer
from concourse.mybir import AluOpType as ALU, ActivationFunctionType as ACT

N, V, B, K, CAP, R, ZP, M = 4, 1024, 256, 16, 48, 6, 2048, 512
NC = N * CAP
WW = K * V + NC
XW_ = 592
MAGIC = 6442450944.0
BIG = 1.0e9
CFG = {"nv": ["avaavaaa", "avaaaaaa"] * 3, "pv": ["avaavaaa", "aaaaaaaa"] * 3, "cut": [0, 64, 128, 192, 256], "fill": "vvvvgggggggddddd",
       "slack": 300.0, "split": "vaaa", "half": 0.5, "wide": 0, "th": "vvvvvv", "hi": "vvvvvv", "x2": 0, "pw": 0, "hx": "vvvvvv", "bulk": 0, "rt": "aaaaaa", "key": "hhhhhh",
       "pl": "aaaaaa", "yt": "vvvvvv", "ct": "aaaaaa", "y": "vaaaaa", "dv": "vvvvvv", "nb": ["aa"] * 4,
       "f": 1.25, "g": 1.56, "s": 3.8, "pe": 0.42, "dma": 1800.0, "rem": 2000.0, "row": 40.0, "bw": 20.0,
       "wake": 70.0, "fix": 55.0}
ORDER = """
a:AN4'> a:AN5'> v:MN3'> v:ACC'> a:AN7'> v:MU> v:W> p:mPL> v:TW> v:PJ_ v:c1_ s:NN> g:YF> v:MN4'> p:a1'> p:m1'> v:ACC.1'> v:MN5'> a:AN6'> p:a2'> v:MONE_ v:c0_ v:Wf1_ v:IDF_ s:AP'> v:MN7'> a:ID_ p:CB_ v:HU'> v:c2_ v:D1_ v:c6_ a:DC_ v:Wf2_ g:WFe> p:mEU> a:AP0'> v:c3_ s:PL_ v:ONES_ v:DW_ a:ID10_ a:IDB_ v:EH0_ v:EL0_ s:W0_ v:MN6'> v:BOF_ a:IDM_ v:c4_ a:CTT_ p:mHI_ a:DA_ p:m2'> a:c8_ a:DG_ p:a3'> v:C96_ a:ID8_ a:BO_ a:BOS_ a:c5_ a:B64_ a:BO2_ v:ACC.2'> p:m3'> v:MP0'> v:ACC.3'> v:A32'> v:KG'> p:mEU.1> a:ID64_ v:CODE'> v:HI.1_ v:NBF_ v:H'> v:L1'> v:S'> v:HU_ p:hc'> p:CB.1_ a:AP1'> v:L1U'> p:mEU.2> a:A8_ a:DM_ p:rank'> v:DF0_ v:INI_ g:C16_ g:NDC_ s:outPL> a:Y0_ v:REP_ a:IB_ a:I17_ v:DE_ a:AP3'> v:Wf15_ v:NBU0_ v:VV'> v:Q'> p:mUF_ a:BOM_ a:KO20_ p:mU_ p:YB_ p:YB'> g:WFn> a:AP4'> a:AP5'> g:K1_ g:KO1_ v:SEG_ v:ZERO_ v:X'> p:pv'> g:BI_ v:BOH_ a:AP2'> g:Wf4_ v:AM_ p:pq'> v:PY'> v:XB'> v:YT'> v:DIAG_ v:YT_ g:lf'> p:mEU_ p:mEU.3> a:AP6'> v:MP1'> a:c15_ s:EI0_<< v:MP4'> v:MP2'> g:lx'> v:MP3'> s:EI1_ s:ANo_ v:MP5'> p:h0'> v:MP6'> a:AP7'> v:MP7'> p:YB.1'> g:THR_ p:mU'> p:h1'> p:h2'> a:PW> a:TPL_ v:HX'> a:BC_ p:h3'> p:h4'> p:h5'> p:h6'> p:h7'> a:RT'> p:back'> p:back.1'> v:G'> a:DF'> p:mMS'> a:A8'> p:CB'> p:mPL'> s:CTo0_<< s:XS0_<< v:MU'> v:MS.1'> a:CTT'> p:mA'> v:MASK_ p:all'> g:lc_ p:run'> v:W'> a:PW'> s:NN'> v:UT'> v:NO'> g:WFe.1> v:WFe'> p:mEU.1_ p:mEU'> a:AP0 v:AP1 p:mEU.1'> a:AP3 a:AP2 s:AP0x_ s:XS1_ s:Wf15_ p:cnt'> p:stay'> v:IX'> v:IXU'> a:XS'> v:DV'> v:SG'> p:mEU.2_ p:CB.1'> v:CTo'> p:mEU.3_ s:JM_<< s:NBI0_<< v:MP0 p:YB.1_ p:mEU.3'> p:mEU.2'> v:AP4 v:MP1 v:MP4 g:lc'> g:Wf7_ v:MP3 g:outWF'>> s:outCT'>> a:outXS'>> s:NBI1_ v:MP2 v:EF1_ a:AP6 a:AP5 v:MP6 v:MP5 a:AP7 a:EH1_ p:mTC'> v:EF2_ g:Wf5_ g:Wf6_ p:mHI a:AN0 p:hc p:h0 p:mTC_ g:TRI_ p:h1 p:h2 p:h3 p:h4 a:AN2 a:AN3 s:outPL'> v:MP7 p:h5 p:h6 p:mEL_ p:h7 a:RT v:AN1 a:EH2_ g:Wf8_ s:Wf13_ p:CB a:AN5 p:a0 s:Wf12_ g:OC_ v:MNo v:MN0 a:AN6 v:MN1 v:HI.1 v:AN4 v:MN2 v:EF3_ v:MN3 v:TRH_ v:MN4 p:m0 p:mHI.1_ g:Wf9_ g:Wf10_ a:AN7 p:a1 v:HU v:INI p:back p:back.1 p:m1 g:LB_ g:J16_< v:G v:NBU' v:HI.3_ v:ACC s:outWF'> g:lf p:mEL.1_ g:PI_< p:all a:EH3_ p:a2 v:NBF v:HU.1_ v:MN5 v:MN6 v:ACC.1 v:UT v:MN7 s:W1_ p:run a:DF0_ p:m2 v:NBU s:XB0_ p:a3 s:XB a:CTT a:IDFM_ s:Wf11_ v:NO s:XB' g:YF0_ g:X143_< s:Wf14_ g:XG_< v:ACC.2 a:DF1_ a:BC.1_ p:m3 a:A8 p:mY_ p:cnt a:DF2_ a:KO g:HX_< p:mY'> a:DF g:YF'> v:ACC.3 v:A32 v:KG v:CODE v:H v:L1 p:stay v:IX v:S v:IXU p:CB.1 p:mEL.2_ g:PB_ p:YB v:DV v:SG v:CTo p:rank v:VV g:LM_ v:L1U v:Q v:X p:mY.1_ v:Wf0_< p:mUF p:pv p:pq v:PY p:mA v:XB p:mY.2_ v:CUT_ v:YT a:XS a:PF<< a:PW_ g:lc p:mTC p:mU p:mUF' v:NBF' a:KO' v:AN1' p:YB.1 p:mY v:Wf3_< s:ANo v:MNo' g:lx a:AN0' v:MN0' v:MN1' s:W3_ a:AN2' a:AN3' s:W2_ p:mHI' v:HI.1' s:AP v:HX p:a0' s:ANo' p:m0' v:INI' s:outCT v:MN2' p:mMS g:YF1_
"""
CFG.update({"key": "khkhkh", "pl": "vavava", "rt": "avavav", "yt": "vaaaaa", "ct": "vaaaaa", "nv": ["vvaaavaa", "avvaaaaa", "avaavaaa", "avvaaaaa", "avaavaaa", "avvaaaaa"], "pv": ["vavaaaaa", "aaaaaaaa", "vaaavaaa", "aaaaaaaa", "vaaavaaa", "aaaaaaaa"], "wide": 6, "x2": 1, "bulk": 1, "f": 1.2, "fix": 70.0, "wake": 100.0, "rem": 1700.0, "row": 32.0, "bw": 27.0, "dma": 1600.0})
ORDER = """
p:a1'> p:m1'> v:ONES_<< p:a2'> v:MN5'> g:YF1_> p:m2'> v:W> v:TW> v:PL> v:ACC.1'> s:NN> s:ANo'> p:mEU> a:AP1'_> g:WFe> a:AP0'_> v:MN7'> s:outPL> v:MN6'> a:AP1'> p:mEU.2> p:a3'> p:m3'> a:AP4'> a:AP0'> s:outCT> v:ACC.2'> a:AP5'_> v:NBF'> v:HU'> v:MP1'> v:ACC.3'> v:A32'> v:KG'> a:AP4'_> p:mEU.1> v:CODE'> a:AP2'_> a:AP3'> a:AP2'> a:AP3'_> v:L1'> v:H'> g:WFn> p:mEU.3> a:AP5'> s:AP'> g:lf'> p:YB'> v:S'> a:AP6'> a:AP6'_> v:MP0'> p:rank'> v:VV'> v:L1U'> p:pv'> v:Q'> p:pq'> v:X'> v:PY'> v:XB'> g:lx'> v:MP3'> v:MP2'> v:MP4'> a:AP7'> a:AP7'_> v:MP5'> a:YT'> p:hc'> v:MP6'> p:mU'> v:MP7'> p:h0'> p:h1'> a:KO'> p:h2'> p:h3'> p:h4'> p:h5'> p:h6'> p:h7'> p:YB.1'> v:RT'> p:back'> a:PW> v:HX'> a:DF'> p:back.1'> v:G'> p:mMS'> a:A8'> p:CB'> p:mA'> a:CTT'> v:MU'> v:W'> s:NN'> p:all'> p:run'> p:mPL'> a:PW'> v:UT'> v:MS.1'> p:mEU'> a:AP1 v:NO'> p:mEU.3'> p:cnt'> p:stay'> g:WFe.1> v:WFe'> v:AP0 v:IX'> v:IXU'> v:DV'> p:mEU.2'> a:AP6 a:XS'> a:AP7 p:mEU.3_ a:AP7_ v:SG'> p:mEU.1'> a:AP2 v:NBF_ v:HU_ a:AP3 p:mEU_ s:Wf12_ p:hc p:CB.1'> v:CTo'> g:lc'> a:AP1_ a:AP6_ a:AP5 v:NBU0_ v:AP0_ p:mEU.1_ p:mEU.2_ v:AP4 v:AP2_ p:mHI v:MP0 p:mTC'> g:outWF'>> a:AN0 v:MP2 v:DF0_ a:AP5_ a:AP4_ a:AN3 p:h0 v:MP1 p:h1 p:h2 a:outXS'>> s:outCT'>> v:MP7 a:Y0_ s:AP0x_ a:AP3_ a:KO20_ a:AN3_ p:YB_ v:AN0_ p:mUF_ v:YT_ p:YB.1_ v:MP4 v:MP3 s:Wf11_ s:Wf14_ v:MP5 v:MP6 p:h3 p:h4 p:h5 p:h6 p:h7 p:CB a:RT v:AN1 v:HI.1 v:MNo v:MN1 a:AN2_ v:AN1_ p:mHI.1_ v:AN5_ s:Wf13_ p:a0 p:back a:AN2 a:AN5 v:AN4 a:AN7 a:AN6 p:m0 p:back.1 v:HI.3_ v:MN3 a:AN7_ a:AN4_ g:lf p:a1 p:mU_ v:INI v:G v:HU.1_ a:AN6_ v:ACC p:m1 v:MN5 p:all s:Wf15_ g:YF0_ v:ACC.1 g:Wf10_ v:UT v:MN7 v:MN6 a:DF0_ v:NBF v:EF1_ p:a2 p:m2 p:run v:ACC.2 a:A8_ s:XB0_ a:CTT v:NO p:mY_ p:a3 p:m3 v:ACC.3 v:A32 v:HU a:EH1_ a:DF1_ v:KG v:KEY p:mUF p:CB.1 p:cnt a:PW_ a:KO a:A8 v:CODE p:stay v:IX s:XB a:DF2_ p:mY.1_ v:H v:IXU v:S v:DV p:mTC_ v:SG p:YB p:rank p:mEL.1_ s:outPL'> v:VV v:CTo s:outWF'> v:Q v:L1 v:L1U p:mY'> a:DF s:ANo s:AP g:lc p:pv a:YT p:mA p:pq v:PY v:NBU v:X s:XB' a:XS p:mEL_ p:mY p:mU v:NBU' v:XB p:YB.1 v:AN1' v:MNo' a:AN0' a:AN0'_ p:mTC a:PF< p:mHI' a:AN3' a:AN3'_ v:AN1'_ p:mY.2_ a:AN5' a:AN4' a:AN4'_ s:W3_ a:AN5'_ v:MN1' a:AN7'_ v:AN2' p:mUF' a:AN6' a:AN7' g:Wf4_ g:lx s:W1_ p:a0' p:m0' g:YF v:AN2'_ v:HX v:MN3' v:INI' v:HI.1' p:mMS g:YF'> s:EI0_<<< s:CTo0_<<< s:NBI0_<<< g:PI_<<< g:X143_<<< g:J16_<<< g:BI_<<< v:Wf0_<<< v:c1_<<< v:PJ_<<< v:Wf3_<<< g:XG_<<< g:C16_<<< v:c0_<<< v:IDF_<<< v:Wf1_<<< v:c2_<<< a:C96_<<< a:INI_<<< a:AM_<<< a:MONE_<<< a:SEG_<<< a:ID10_<<< a:ID_<<< a:c3_<<< a:IDM_<<< a:IB_<<< a:AN6'_ s:XS0_<<< s:PL_<<< v:EH0_<<< v:D1_<<< v:Wf2_<<< a:IDB_<<< a:IDFM_<<< v:EL0_<<< a:I17_<<< v:c6_<<< g:KO1_<<< s:W0_<<< s:JM_<<< g:lc_<<< a:DC_<<< p:CB_<<< a:DW_<<< a:ID8_<<< a:ID64_<<< v:BOF_<<< v:ACC' g:HX_<<< a:DM_<<< a:DA_<<< a:BOM_<<< a:B64_<<< a:BO_<<< v:CTT_<<< v:DIAG_<<< p:CB.1_<<< v:ZERO_<<< a:MASK_<<< a:TPL_<<< a:BOS_<<< v:c4_<<< a:DE_<<< a:c15_<<< a:BO2_<<< a:c5_<<< a:c8_<<< a:BC_<<< v:BOH_<<< v:REP_<<< v:IDH_<<< a:DG_<<< g:TRI_<<< v:MU g:Wf9_<<< g:K1_<<< p:mHI_<<< v:TRH_<<< g:PB_<<< g:NDC_<<< g:Wf6_<<< g:LB_<<< a:BC.1_<<< g:LM_<<< g:Wf8_<<< s:ANo_<<< s:XS1_<<< s:EI1_<<< s:NBI1_<<< g:Wf7_<<< g:OC_<<< g:THR_<<< g:Wf5_<<< v:Wf15_<<< v:HI.1_<<<
"""

f32, bf, f16, i32, u16 = "float32", "bfloat16", "float16", "int32", "uint16"
SCRATCH = {}
for _n, _w, _d in [
    ("W", WW, bf), ("WF", WW, f32), ("CT", N * V, bf), ("PL", ZP, bf), ("JM", M, bf), ("XS", V, bf), ("Y", R * B, bf),
    ("YF", R * B, f32), ("AN", 17 * B, bf), ("MN", 17 * B, bf), ("AP0", 18 * B, bf), ("AP1", 18 * B, bf), ("MP", 16 * B, bf),
    ("NBI", V, i32), ("NBU", V, u16), ("TC", V, f32), ("KO2", V, bf), ("A8", B, bf), ("NBF", B, f32),
    ("EI", V, i32), ("EF", V, f32), ("EH", V, bf), ("EL", V, bf), ("EU", B, u16), ("NN", B, bf),
    ("XB0", XW_, f32), ("XB1", XW_, f32), ("XB2", XW_, f32), ("XB3", XW_, f32), ("XB4", XW_, f32), ("XB5", XW_, f32),
    ("PI", 8, i32), ("RH", B, f16), ("IDH", 128, f16), ("COL", 16, f32), ("REP", 8, u16), ("X143", 144, f32), ("XG", 128, f32), ("J16", B, f32),
    ("DM", 144, bf), ("DA", 144, bf), ("DE", 144, bf), ("DW", 144, bf), ("DC", 144, bf), ("GH", B, f16), ("TRH", 128, f16),
    ("BOH", 128, f16), ("D1", 144, bf), ("ID", 128, bf), ("IDM", 128, bf), ("IDF", 128, f32), ("IDFM", 128, f32),
    ("ID8", 128, bf), ("ID10", 128, bf), ("ID64", 128, bf), ("IDB", 128, bf), ("DG", 128, bf), ("ONES", V, bf), ("ZERO", B, bf),
    ("BO", 128, bf), ("BOM", 128, bf), ("BO2", 8, bf), ("BOF", 128, f32),
    ("BOS", 128, f32), ("B64", 128, f32), ("TRI", 128, f32), ("LB", 128, bf), ("LM", 128, bf),
    ("MASK", NC, bf), ("DIAG", B, f32), ("SEG", NC, bf), ("KO1", B, bf), ("K1", B, bf), ("OC", 80, f32),
    ("C16", 16, bf), ("IB", 16, bf), ("I17", 16, f32), ("MONE", 48, bf), ("NDC", 64, bf), ("THR", 64, f32),
    ("TPL", NC, f32), ("PB", NC, bf), ("PW", 6 * NC, bf), ("BC", 16, f32),
    ("HI", 48, i32), ("HU", 48, u16), ("DF", 768, bf), ("UF", B, bf), ("U", 2 * B, bf), ("YT", B, bf), ("CTT", B, bf),
    ("INI", 64, f32), ("ACC", 64, f32), ("A32", 32, f32),
    ("KG", 16, i32), ("CODE", 16, i32), ("L1", 16, i32), ("L1U", 16, u16), ("H", 80, bf), ("S", 80, bf),
    ("VV", 64, bf), ("Q", 64, bf), ("PY", 16, u16), ("X", B, f32), ("AG", 2, bf), ("AM", 1, f32), ("RT", B, f32),
    ("G", B, f32), ("UT", B, f32), ("NO", B, bf), ("IX", 16, f32), ("IXU", 16, u16), ("SG", B, bf),
    ("HX", NC, f32), ("MS", NC, f32), ("DV", B, bf), ("MU", 12, u16), ("TW", NC, bf),
]:
    SCRATCH[_n] = ("sbuf", [128, _w], _d)
BANKS = ("K0", "KB1", "HB", "YB", "CB", "TB", "M1", "M2")
for _n in BANKS:
    SCRATCH[_n] = ("psum", [128, 1024], bf) if _n in ("YB", "CB") else ("psum", [128, 512], f32)
SEMAPHORES = ["qv", "qa", "qp", "qg"] + ["d%d" % i for i in range(100)] + ["ax%d" % t for t in range(R)] + \
    ["ac%d" % t for t in range(R)] + ["lx%d" % t for t in range(R)] + ["lc%d" % t for t in range(R)] + \
    ["af%d" % t for t in range(R - 1)] + ["lf%d" % t for t in range(R - 1)]


def arrange(ops):
    n = len(ops)
    words = ORDER.split()
    place = {x.rstrip("<>"): x.count(">") - x.count("<") + k / len(words) for k, x in enumerate(words)}
    key = [place.get(o[6] + "_" * (o[7] in (0, R - 1) and o[6][:4] in ("a:AN", "v:AN", "a:AP", "v:AP")), place.get(o[6], -9.0)) + (o[7] or 0) // 2 for o in ops]
    last, readers, pred, uses = {}, {}, [], {}
    for i, (q, fn, rd, wr, own, c, name, step) in enumerate(ops):
        need = set()
        for t in rd:
            if t in last:
                need.add(last[t])
            if t in BANKS or t[:2] == "M#":
                need.update(x for x in readers.get(t, []) if ops[x][0] != q)
        for t in wr:
            if t in last:
                need.add(last[t])
            need.update(readers.get(t, []))
        if fn is None:
            need.add(i - 1)
        pred.append(need)
        for t in rd:
            readers.setdefault(t, []).append(i)
        for t in wr:
            last[t] = i
            readers[t] = []
        for t in set(rd + wr):
            if t[:2] == "M#":
                uses.setdefault(t, []).append(i)
    group = {i: [i] for i in range(n)}
    tag = {}
    for t, some in uses.items():
        group[some[0]], tag[some[0]] = some, t
        for x in some[1:]:
            del group[x]
    waits = {i: set().union(*[pred[x] for x in some]) - set(some) for i, some in group.items()}
    order, done, pick, pace = [], set(), {}, {}
    end, free, bank, engines, ends = {}, {}, {"M1": 0.0, "M2": 0.0}, 0.0, []
    while waits:
        i0 = min((i for i in waits if waits[i] <= done), key=lambda x: (key[x], x))
        del waits[i0]
        for i in group[i0]:
            q, (hold, lat, et) = ops[i][0], ops[i][5]
            t = max([free.get(q, 0.0)] + [end[j] + (0.0 if q == ops[j][0] == "p" or q == "x" else CFG["wake"]) for j in pred[i]])
            if i in tag:
                pick[tag[i]] = min(bank, key=lambda x: bank[x])
                t = max(t, bank[pick[tag[i]]])
            if et and engines > t + lat:
                if q == "s" and engines > t + lat + CFG["slack"]:
                    some = [x for x in ends if x[0] <= engines - lat]
                    if some and max(some)[0] > t:
                        pace[i] = max(some)[1]
                t = engines - lat
            end[i] = t + (lat + et if et else max(hold, lat))
            engines = end[i] if et else engines
            free[q] = t + hold if q != "x" else 0.0
            if q in "vap":
                ends.append((end[i], i))
            order.append(i)
            done.add(i)
        if i0 in tag:
            bank[pick[tag[i0]]] = end[i] + CFG["wake"]
    return order, pick, pace


def build(g, T, ops):
    queues = {"v": g.vector, "a": g.scalar, "p": g.tensor, "s": g.sync, "g": g}
    last, readers = {}, {}
    known = {q: {} for q in "vapsgx"}
    clock, waits, used = {}, [], set()
    seq = {q: 0 for q in queues}
    totals = {}
    for n, (q, fn, rd, wr, own) in enumerate(ops):
        if own is None:
            seq[q] += 1
            tok = ("q" + q, seq[q])
        else:
            tok = own
            totals[own[0]] = max(totals.get(own[0], 0), own[1])
        need = []
        for t in rd:
            if t in last:
                need.append(last[t])
            if t in BANKS:
                need.extend(x for x in readers.get(t, []) if x[0] != "q" + q)
        for t in wr:
            if t in last:
                need.append(last[t])
            need.extend(readers.get(t, []))
        mine = []
        if fn is not None:
            kn = known[q]
            for (s, c) in sorted(set(need), key=lambda x: -x[1]):
                if (q == "p" and s == "qp") or kn.get(s, 0) >= c:
                    continue
                mine.append((s, c))
                used.add((s, c))
                kn[s] = c
                for s2, c2 in clock.get((s, c), {}).items():
                    if kn.get(s2, 0) < c2:
                        kn[s2] = c2
            clock[tok] = dict(kn)
        waits.append((tok, mine))
        for t in rd:
            readers.setdefault(t, []).append(tok)
        for t in wr:
            last[t] = tok
            readers[t] = []
    count = {}
    for s in ("qv", "qa", "qp", "qg"):
        for k, x in enumerate(sorted(c for (s2, c) in used if s2 == s)):
            count[(s, x)] = k + 1
    for n, (q, fn, rd, wr, own) in enumerate(ops):
        if fn is None:
            continue
        tok, mine = waits[n]
        for w in mine:
            queues[q].wait_ge(T.sem[w[0]], count.get(w, w[1]))
        for f in fn:
            ins = f()
            if own is not None and own[0][0] == "d":
                ins.then_inc(T.sem[own[0]], 16)
        if own is None and tok in count:
            ins.then_inc(T.sem[tok[0]], 1)
    for s, c in totals.items():
        g.sync.wait_ge(T.sem[s], c)


def rank_program(g, core, T, topo):
    me = T.rank_of(core)
    if me is None:
        return
    kinds = {f16: "f2", f32: "f4", i32: "i4", bf: "i2", u16: "u2"}
    shapes = [(n, ("f8" if d == f32 else "c8") if w == "psum" else kinds[d], tuple(sh)) for n, (w, sh, d) in SCRATCH.items()]
    shapes += [(n, "i2", tuple(T[n].shape)) for n in ("cen", "pl", "jmp", "wk", "yc", "yx", "yz", "yn")]
    shapes += [(n, "i4", tuple(T[n].shape)) for n in ("ent", "nb", "ye")]
    order, pick, pace = arrange(calls(g, core, me, np.recarray((1,), shapes)[0], T, topo, None))
    ops = calls(g, core, me, T, T, topo, pick)
    for i, j in pace.items():
        ops[i][2].append("pace%d" % i)
        ops[j][3].append("pace%d" % i)
    build(g, T, [(o[0], o[1], [pick.get(t, t) for t in o[2]], [pick.get(t, t) for t in o[3]], o[4])
                 for o in [ops[i] for i in order]])


def calls(g, core, me, T, G, topo, pick):
    ops = []
    nd, nb_ = [0], [0]
    v, a, p = g.vector, g.scalar, g.tensor
    C = CFG
    real = pick is not None
    step, seen = [None], {}

    def op(q, fn, rd, wr, own=None, cost=None, name=None):
        if name is None:
            name = (list(wr) + [own[0][:2] if own and own[0][0] == "l" else "out" + "".join(rd)[:2]])[0]
            if name[:2] == "M#":
                name = "m" + name.split("#")[2]
            elif step[0] is not None:
                name = "AP" + name[4:] if name[:2] == "AP" else \
                    name if name[:2] in ("AN", "MN", "MP", "EU", "L1", "A3", "A8") else name.rstrip("0123456789")
        k = seen[q, name, step[0]] = seen.get((q, name, step[0]), -1) + 1
        name = q + ":" + name + (".%d" % k if k else "") + ("_" if step[0] is None else "'" * (step[0] % 2))
        ops.append((q, fn, list(rd), list(wr), own, cost or (0.0, 0.0, 0.0), name, step[0]))

    def join(n, w=250.0):
        some = ops[-n:]
        del ops[-n:]
        ops.append(some[0][:1] + ([f for o in some for f in o[1]],) + some[0][2:5] +
                   ((C["fix"] * 2 + w * 0.83 * C["f"], 0.0, 0.0),) + some[0][6:])

    def lend(what):
        nb_[0] += 1
        tag = "M#%d#%s" % (nb_[0], what)
        return T[pick[tag] if real else "M1"], tag

    def ind(win, off):
        return win.indirect(off) if real else (win, off)

    def work(out, ins, two=False):
        if real:
            return None
        if isinstance(out, tuple):
            c = C["s"] * 16 * out[1].shape[1]
        elif isinstance(ins[0], tuple):
            c = C["g"] * out.shape[1]
        else:
            c = ins[0].shape[1]
            if all(x.itemsize == 2 or x.dtype.kind == "c" for x in [out] + ins):
                c = c * (C["half"] if two and any(x.itemsize == 8 for x in ins) else 0.5)
            if two and all(x.itemsize < 8 for x in ins):
                c = 2 * c
        return (C["fix"] + max(64.0, c) * 0.83 * C["f"], 0.0, 0.0)

    def moved(rows, nbytes, engines):
        return (rows * C["row"] + nbytes / C["bw"]) / engines

    def dma(q, pairs, rd, wr, add=False):
        s = "d%d" % nd[0]
        nd[0] += 1
        e = {"s": g.sync, "a": g.scalar, "g": g}[q]
        cost = None if real else ((900.0 if q == "g" else 60.0) * len(pairs), C["dma"] + (500.0 if q == "g" else 0.0),
                                  sum(moved(max(o.shape[0], i.shape[0], 16), o.nbytes * (2 if add else 1), 16) for o, i in pairs))
        if add:
            op(q, [lambda o=o, i=i: g.dma_start(o, i, accum_op=ALU.add, max_dma_last_dim=4096) for o, i in pairs], rd, wr,
               (s, 16 * len(pairs)), cost)
        else:
            op(q, [lambda o=o, i=i: e.dma_start(o, i) for o, i in pairs], rd, wr, (s, 16 * len(pairs)), cost)

    def ts(out, in0, s1, s2, o0, o1, rd, wr):
        if s2 is None:
            op("v", [lambda: v.tensor_scalar(out, in0, s1, None, o0)], rd, wr, None, work(out, [in0]))
        else:
            op("v", [lambda: v.tensor_scalar(out, in0, s1, s2, o0, o1)], rd, wr, None, work(out, [in0]))

    def tt(out, in0, in1, o, rd, wr):
        op("v", [lambda: v.tensor_tensor(out, in0, in1, o)], rd, wr, None, work(out, [in0, in1], True))

    def cp(out, in_, rd, wr):
        op("v", [lambda: v.tensor_copy(out, in_)], rd, wr, None, work(out, [in_]))

    def fill(ap, x, wr):
        op("v", [lambda: v.memset(ap, x)], [], wr, None, work(ap, [ap]))

    def scan(out, d0, d1, o0, o1, rd, wr):
        op("v", [lambda: v.tensor_tensor_scan(out, d0, d1, 0.0, o0, o1)], rd, wr, None, work(out, [d0, d1]))

    def act(out, in_, func, rd, wr, bias=0.0, scale=1.0):
        cost = None if real else work(out, [in_, T.COL])
        if func == ACT.Copy:
            op("a", [lambda: a.activation(out, in_, func)], rd, wr, None, cost)
        else:
            op("a", [lambda: a.activation(out, in_, func, bias=bias, scale=scale)], rd, wr, None, cost)

    def move(e, out, src, rd, wr):
        if e == "v":
            cp(out, src, rd, wr)
        else:
            act(out, src, ACT.Copy, rd, wr)

    def mm(terms, bank, first=True, final=True, after=(), name=None):
        fns, rd = [], []
        for n, (o, l, r, x) in enumerate(terms):
            st, sp = first and n == 0, final and n == len(terms) - 1
            fns.append(lambda o=o, l=l, r=r, st=st, sp=sp: p.matmul(o, l, r, st, sp))
            rd += x
        cost = None if real else (sum(max(64, o.shape[1]) * (4 if l.itemsize == 4 else 1) for o, l, r, x in terms)
                                  * C["pe"] * C["f"], 0.0, 0.0)
        op("p", fns, sorted(set(rd)), [bank] + list(after), None, cost, name)

    def turn(pairs, rd, bank):
        op("p", [lambda o=o, i=i: p.transpose(o, i, T.ID[:, :]) for o, i in pairs], rd + ["ID"], [bank], None,
           (128 * len(pairs) * C["pe"] * C["f"], 0.0, 0.0))

    def pool(fn, w, rd, wr):
        op("g", [fn], rd, wr, None, ((150.0 + 2 * w * 0.83) * C["f"], 0.0, 0.0))

    def iota(name, lo, hi, pat, base=0, cm=0, integer=False, tag=None):
        if integer:
            pool(lambda: g.iota(T[name][:, lo:hi], pat, base, cm), hi - lo, [], [tag or name])
        else:
            pool(lambda: g.iota(T[name][:, lo:hi], pat, base, cm, allow_small_or_imprecise_dtypes=True), hi - lo, [], [tag or name])

    def sel(name, r):
        return T[name][:, 15 - r:143 - r]

    peers = [(me + d) % N for d in (1, 2, 3)]
    ids = {q: DstId(rid=topo.addr(G.cores[q])[0], pnc=topo.addr(G.cores[q])[1]) for q in peers}
    eng = [e for e in topo.engines(core, G.cores[peers[0]])
           if all(e in topo.engines(core, G.cores[q]) for q in peers)]
    full = sum(1 << e for e in eng)
    part = len(eng) // 4
    own0 = me * V
    n1 = CAP * (N - 1 - me)
    CTALL = ["CTo0", "CTo1", "CTo2", "CTo3", "CTr"]
    WALL = ["W0", "W1", "W2", "W3"]

    def send_c(lo, w, t, rd):
        ap = T.CT[:, own0 + lo:own0 + lo + w]
        op("g", [lambda: g.remote_dma_fused([RemoteDMATransfer(
            dst_ids=[ids[q] for q in peers], dma_engine_mask=full, remote_sem=G.sem["ac%d" % t], srcs=[ap], dsts=[ap, ap, ap])],
            local_sem=G.sem["lc%d" % t])], rd, [], ("lc%d" % t, len(eng)),
           (500.0, C["rem"] * (2 if w == V else 1), moved(384, 768 * w, len(eng))))
        op("x", None, [], ["CTr"], ("ac%d" % t, 3 * len(eng)))

    def send_x(t):
        xb = T["XB%d" % t]

        def trs():
            return [RemoteDMATransfer(dst_ids=[ids[q]], dma_engine_mask=sum(1 << e for e in eng[d * part:(d + 1) * part]),
                                      remote_sem=G.sem["ax%d" % t], src=xb[:, NC + CAP * d:NC + CAP * (d + 1)],
                                      dst=xb[:, CAP * (2 - d):CAP * (3 - d)]) for d, q in enumerate(peers)]
        if C["x2"]:
            def tr(d, es):
                return RemoteDMATransfer(dst_ids=[ids[peers[d]]], dma_engine_mask=sum(1 << e for e in es),
                                         remote_sem=G.sem["ax%d" % t], src=xb[:, NC + CAP * d:NC + CAP * (d + 1)],
                                         dst=xb[:, CAP * (2 - d):CAP * (3 - d)])
            far = sorted(range(3), key=lambda d: topo.die(G.cores[peers[d]]) == topo.die(core))
            op("g", [lambda: g.remote_dma_fused([tr(far[0], eng[:2 * part]), tr(far[1], eng[2 * part:])], local_sem=G.sem["lx%d" % t]),
                     lambda: g.remote_dma_fused([tr(far[2], eng)], local_sem=G.sem["lx%d" % t])],
               ["XB%d" % t], [], ("lx%d" % t, 8 * part), (1000.0, C["rem"], moved(384, 384 * 192, len(eng))))
            op("x", None, [], ["XL%d" % t], ("ax%d" % t, 8 * part))
            return
        op("g", [lambda: g.remote_dma_fused(trs(), local_sem=G.sem["lx%d" % t])], ["XB%d" % t], [], ("lx%d" % t, 3 * part),
           (500.0, C["rem"], moved(128, 128 * 192, part)))
        op("x", None, [], ["XL%d" % t], ("ax%d" % t, 3 * part))

    def send_free(t):
        op("g", [lambda: g.remote_dma_fused([RemoteDMATransfer(dst_ids=[ids[q]], dma_engine_mask=1 << eng[3 * part + d],
                                                               remote_sem=G.sem["af%d" % t]) for d, q in enumerate(peers)],
                                            local_sem=G.sem["lf%d" % t])],
           ["AN%d" % j for j in range(8)], [], ("lf%d" % t, 3), (500.0, C["rem"], 0.0))
        op("x", None, [], ["FR"], ("af%d" % t, 3))

    def col(j):
        return T.COL[:, j:j + 1]

    def on(r):
        return T.DIAG[:, r:r + 1]

    def blk(name, b):
        return T[name][:, b * B:(b + 1) * B]

    def cown(t):
        b = t % 4
        return T.CT[:, own0 + b * B:own0 + (b + 1) * B]

    def dmat(name, w, rd=()):
        ts(T[name][:, :], T.X143[:, :], col(2), w, ALU.is_equal, ALU.mult, ["X143", "c2"] + list(rd), [name])

    def scaled(name, src, w):
        act(T[name][:, :], T[src][:, :], ACT.Identity, [src], [name], scale=w)

    def y_make(xlo, t0, t1, rd):
        n = (t1 - t0) * B
        c, tags = n // 16, ["Y%d" % t for t in range(t0, t1)]
        ps, bank = lend("HI")
        if C["hi"][t0] == "v":
            mm([(ps[:, 0:c], sel("DW", r), T.XS[:, xlo + r:xlo + n:16], ["DW"] + rd) for r in range(16)], bank, after=["HI"])
            cp(T.HI[:, 0:c], ps[:, 0:c], [bank], ["HI"])
            ts(T.HI[:, 0:c], T.HI[:, 0:c], M - 1, None, ALU.bitwise_and, None, ["HI"], ["HI"])
            cp(T.HU[:, 0:c], T.HI[:, 0:c], ["HI"], ["HU"])
        else:
            mm([(ps[:, 0:c], sel("DW", r), T.XS[:, xlo + r:xlo + n:16], ["DW"] + rd) for r in range(16)], bank, after=["HI", "HU"])
            act(T.SG[:, 0:c], ps[:, 0:c], ACT.Identity, [bank], ["HI", "SG"], bias=1024.0 - 255.5 / 64, scale=1.0 / 64)
            mm([(ps[:, 0:c], T.ID64[:, :], T.SG[:, 0:c], ["ID64", "SG"])], bank, False, True, name="mod")
            ts(T.HU[:, 0:c], ps[:, 0:c], 65536.0, None, ALU.add, None, [bank], ["HU"])
        for t in range(t0, t1):
            lo = (t - t0) * B
            df, tg, x = T.DF[:, lo:lo + B], "DF%d" % (t - t0), T.XS[:, xlo + lo:xlo + lo + B]
            jump = ind(T.JM[:, :], T.HU[:, lo // 16:lo // 16 + 16])
            if C["y"][t] == "v":
                tt(df, jump, x, ALU.subtract, ["JM", "HU"] + rd, [tg])
                act(blk("Y", t), df, ACT.Abs, [tg], ["Y%d" % t])
            else:
                act(df, jump, ACT.Copy, ["JM", "HU"], [tg])
                ps, bank = lend("Y")
                mm([(ps[:, 0:B], T.ID[:, :], df, ["ID", tg]), (ps[:, 0:B], T.IDM[:, :], x, ["IDM"] + rd)], bank)
                act(blk("Y", t), ps[:, 0:B], ACT.Abs, [bank], ["Y%d" % t])
        dma("g", [(T.YF[:, t0 * B:t1 * B], T.Y[:, t0 * B:t1 * B])], tags, ["YF%d" % t for t in range(t0, t1)])

    def nb_lists(b):
        nbi, tg = blk("NBI", b), "NBI%d" % b
        cp(blk("NBU", b), nbi, [tg], ["NBU%d" % b])
        cp(T.NBF[:, :], nbi, [tg], ["NBF"])
        for e, out, w, x, tag in [(C["nb"][b][0], blk("KO2", b), 1.0 / 1024, 193.0 - 511.5 / 1024, "KO2%d" % b),
                                  (C["nb"][b][1], T.A8[:, :], 1.0 / 256, 192.0 - 127.5 / 256, "A8")]:
            if e == "v":
                ts(out, nbi, w, x, ALU.mult, ALU.add, [tg], [tag])
            else:
                act(out, T.NBF[:, :], ACT.Identity, ["NBF"], [tag], bias=x, scale=w)
        ps, bank = lend("TC")
        o = ps[:, 0:B]
        mm([(o, T.IDF[:, :], T.NBF[:, :], ["IDF", "NBF"]), (o, T.ID8[:, :], T.A8[:, :], ["ID8", "A8"]),
            (o, T.ID10[:, :], blk("KO2", b), ["ID10", "KO2%d" % b]), (o, T.ID[:, :], T.K1[:, :], ["ID", "K1"])], bank)
        act(blk("TC", b), o, ACT.Identity, [bank], ["TC%d" % b], bias=512.0 * (16384 * 193 - 3840 * 192), scale=512.0)

    def ent_split(b):
        if C["split"][b] == "v":
            cp(blk("EH", b), blk("EI", b), ["EI%d" % b], ["EH%d" % b])
            tt(blk("EL", b), blk("EI", b), blk("EH", b), ALU.subtract, ["EI%d" % b, "EH%d" % b], ["EL%d" % b])
        else:
            cp(blk("EF", b), blk("EI", b), ["EI%d" % b], ["EF%d" % b])
            act(blk("EH", b), blk("EF", b), ACT.Copy, ["EF%d" % b], ["EH%d" % b])
            ps, bank = lend("EL")
            o = ps[:, 0:B]
            mm([(o, T.IDF[:, :], blk("EF", b), ["IDF", "EF%d" % b]), (o, T.IDM[:, :], blk("EH", b), ["IDM", "EH%d" % b])], bank)
            act(blk("EL", b), o, ACT.Copy, [bank], ["EL%d" % b])
        w = slice(b * K * B, (b + 1) * K * B)
        dma("s", [(T.W[0::16, w], blk("EH", b)), (T.W[1::16, w], blk("EL", b))], ["EH%d" % b, "EL%d" % b],
            ["W%d" % b] + ["Wf%d" % x for x in range(4 * b, 4 * b + 4)])

    def w_fill(x0, x1):
        for x in range(x0, x1):
            lo, e = V * x, C["fill"][x]
            if e == "g":
                iota("W", lo, lo + V, [[0, V]], 1, tag="Wf%d" % x)
            elif e == "v":
                fill(T.W[:, lo:lo + V], 1.0, ["Wf%d" % x])
            elif e == "a":
                act(T.W[:, lo:lo + V], T.ONES[:, :], ACT.Copy, ["ONES"], ["Wf%d" % x])
            else:
                dma("s", [(T.W[:, lo:lo + V], T.ONES[:, :])], ["ONES"], ["Wf%d" % x])

    def e_lists(t):
        b = t % 4
        for lo, hi in zip(C["cut"][:-1], C["cut"][1:]):
            ps, bank = lend("EU")
            tags = ["EU%d" % j for j in range(lo // 32, hi // 32)]
            mm([(ps[:, 0:hi - lo], sel("DE", r), T.W[:, b * K * B + 16 * lo + r:b * K * B + 16 * hi:16], ["DE", "W%d" % b])
                for r in range(16)], bank, after=tags)
            cp(T.EU[:, lo:hi], ps[:, 0:hi - lo], [bank], tags)

    def n_tile(t):
        b = t % 4
        dma("s", [(T.NN[:, :], T.W[2::16, b * K * B:(b + 1) * K * B])], ["W%d" % b], ["NN"])

    def ucalc(t):
        ps, bank = lend("UF")
        mm([(ps[:, 0:B], T.BO[:, :], blk("Y", t), ["BO", "Y%d" % t])], bank, after=["UF"])
        act(T.UF[:, :], ps[:, 0:B], ACT.Identity, [bank], ["UF"], bias=192.0 - 31.5 / 64, scale=1.0 / 64)
        ps, bank = lend("U")
        o, u = ps[:, 0:B], "U%d" % (t % 2)
        mm([(o, T.BO[:, :], blk("Y", t), ["BO", "Y%d" % t]), (o, T.ID64[:, :], T.UF[:, :], ["ID64", "UF"])], bank, after=[u])
        act(blk("U", t % 2), o, ACT.Identity, [bank], [u], bias=64.0 * 192)

    def twice(e, src, c, rd, stage, bank, lo=0, n=2):
        turn([(T[bank][:, lo + h:lo + h + 128], T[src][:, c + h:c + h + 128]) for h in (0, 128)], rd, bank)
        move(e, T[stage][:, :], T[bank][:, lo:lo + B], [bank], [stage])
        turn([(T[bank][:, lo + h:lo + h + 128], T[stage][:, h % B:h % B + 128]) for h in range(0, n * B, 128)], [stage], bank)

    def yrep(t):
        twice(C["yt"][t], "Y", B * t, ["Y%d" % t], "YT", "YB", 0, 4 if C["wide"] else 2)

    def crep(t):
        twice(C["ct"][t], "CT", own0 + B * (t % 4), ["CTo%d" % (t % 4)], "CTT", "CB", 2 * B * (t % 2))
        if C["dv"][t] == "m":
            act(blk("CM", t % 2), cown(t), ACT.Identity, ["CTo%d" % (t % 4)], ["CM%d" % (t % 2)], bias=-1.0)
            act(blk("CM", 2), T.CTT[:, :], ACT.Identity, ["CTT"], ["CP"], bias=1.0)
            turn([(T.YB[:, B * (2 + t % 2) + h:B * (2 + t % 2) + h + 128], T.CM[:, 2 * B + h:2 * B + h + 128]) for h in (0, 128)],
                 ["CP"], "YB")

    def tiles_n(t):
        dma("s", [(T.AN[:, 0:B], cown(t))], ["CTo%d" % (t % 4)], ["ANo"])

    def tiles_p(t):
        ap = "AP%d" % (t % 2)
        dma("s", [(blk(ap, 16), cown(t)), (blk(ap, 17), blk("Y", t))], ["CTo%d" % (t % 4), "Y%d" % t], [ap + "x"])

    def payload(t):
        if C["pw"] and t < 5:
            return
        if t < 4:
            act(T.PW[:, 0:NC], T.PB[:, :], ACT.Identity, ["PB", "BC", "DIAG"], ["PW"], bias=T.BC[:, t:t + 1], scale=on(1))
        elif t == 4:
            act(T.PW[:, 0:NC], T.PB[:, :], ACT.Identity, ["PB", "DIAG"], ["PW"], scale=on(1))
        else:
            act(T.NBF[:, 0:NC], T.PB[:, :], ACT.Identity, ["PB", "DIAG"], ["PF", "NBF"], scale=on(0))

    def template(t):
        dma("s", [(T["XB%d" % t][:, 144:336], T.TPL[:, :])], ["TPL"], ["XB%d" % t])

    def acount():
        ps, bank = lend("A")
        o = ps[:, 0:1]
        mm([(o, T.ONES[:, 0:128], T.S[:, 79:80], ["ONES", "S"]), (o, T.ONES[:, 0:128], T.MONE[:, 16:17], ["C96"])], bank)
        act(T.AG[:, 0:1], o, ACT.Identity, [bank], ["AG"], bias=-2048.0 * 31.5, scale=-2048.0)
        act(T.AM[:, :], o, ACT.Identity, [bank, "AG"], ["AM"], bias=T.AG[:, 0:1], scale=2048.0)

    def arrive(t):
        xb, tg = T["XB%d" % t], ["XB%d" % t, "XL%d" % t]
        if C["hx"][t] == "v":
            ts(T.HX[:, :], xb[:, 0:NC], MAGIC, MAGIC, ALU.add, ALU.subtract, tg, ["HX"])
        else:
            act(T.HX[:, :], xb[:, 0:NC], ACT.Identity, tg, ["HX"], bias=MAGIC)
            act(T.HX[:, :], T.HX[:, :], ACT.Identity, ["HX"], ["HX"], bias=-MAGIC)
        ps, bank = lend("MS")
        o = ps[:, 0:NC]
        mm([(o, T.ID[:, :], T.MASK[:, :], ["ID", "MASK"]), (o, T.BOS[:, :], T.HX[:, :], ["BOS", "HX"])], bank)
        scan(T.MS[:, :], T.SEG[:, :], o, ALU.mult, ALU.max, ["SEG", bank], ["MS"])
        cp(T.MU[:, :], T.MS[:, 15:NC:16], ["MS"], ["MU"])
        cuts = [(NC - n1, 0, n1)] * (n1 > 0) + [(0, n1, NC - n1)]
        if C["pl"][t] == "v":
            for to, at, w in cuts:
                tt(T.PL[:, NC * t + to:NC * t + to + w], xb[:, at:at + w], T.HX[:, at:at + w], ALU.subtract, tg + ["HX"], ["PL"])
            join(len(cuts), 450.0)
            return
        ps, bank = lend("PL")
        o = ps[:, 0:NC]
        mm([(o, T.IDF[:, :], xb[:, 0:NC], ["IDF"] + tg), (o, T.IDFM[:, :], T.HX[:, :], ["IDFM", "HX"])], bank, after=["PL"])
        for to, at, w in cuts:
            act(T.PL[:, NC * t + to:NC * t + to + w], ps[:, at:at + w], ACT.Copy, [bank], ["PL"])
        join(len(cuts))

    def arrive_w(t):
        if t < 4:
            cp(ind(T.W[:, :], T.MU[:, :]), T.PW[:, NC * t * C["pw"]:NC * (t * C["pw"] + 1)], ["MU", "PW"], WALL)
            return
        tw = "TW" if t == 4 else "MS"
        ts(T[tw][:, :], ind(T.W[:, :], T.MU[:, :]), col(5), T.BC[:, t:t + 1], ALU.mult, ALU.add, ["MU", "c5", "BC"] + WALL, [tw])
        if t == 4:
            tt(ind(T.W[:, :], T.MU[:, :]), T.TW[:, :], T.PW[:, NC * t * C["pw"]:NC * (t * C["pw"] + 1)], ALU.add, ["MU", "PW", "TW"], WALL)
        else:
            tt(ind(T.WF[:, :], T.MU[:, :]), T.MS[:, :], T.NBF[:, 0:NC], ALU.add, ["MU", "PF", "MS"], ["WFe", "WFn"])

    def entry_piece(t, j):
        ap, ct, c0 = "AP%d" % (t % 2), "CTo%d" % (t % 4), own0 + B * (t % 4)
        tg, ks, sl = "%s_%d" % (ap, j), (2 * j, 2 * j + 1), slice(2 * B * j, 2 * B * (j + 1))
        move(C["pv"][t][j], T[ap][:, sl], ind(T.PL[:, :], T.EU[:, 32 * j:32 * j + 32]), ["PL", "EU%d" % j], [tg])

        def sums(name, w, x):
            return [(T.HB[:, h + k:h + 128:16], T[name][:, B * k + h:B * k + h + 128], w, x) for k in ks for h in (0, 128)]
        if j == 0:
            mm([(T.HB[:, 0:B], T.ID[:, :], T.ZERO[:, :], ["ID", "ZERO"])] +
               [(T.HB[:, h:h + 128], T.CT[:, c0 + h:c0 + h + 128], T.BOM[:, :], ["BOM", ct]) for h in (0, 128)],
               "HB", True, False, name="hc")
        tt(T.MP[:, sl], T[ap][:, sl], T.CB[:, 2 * B * (t % 2):2 * B * (t % 2 + 1)], ALU.max, [tg, "CB"], ["MP%d" % j])
        mm(sums(ap, T.BOM[:, 0::16], ["BOM", tg]) + sums("MP", T.BO2[:, :], ["BO2", "MP%d" % j]), "HB", False, j == 7,
           name="h%d" % j)

    dma("s", [(T.CT[:, own0:own0 + V], T.cen[:, :])], [], CTALL[:4])
    send_c(0, V, 5, CTALL[:4])
    dma("s", [(T.JM[:, :], T.jmp[:, :])], [], ["JM"])
    dma("s", [(T.PL[:, :], T.pl[:, :])], [], ["PL"])
    for b0, b1 in ((0, 1), (1, 4)):
        dma("s", [(blk("EI", b), T.ent[:, b * K * B:(b + 1) * K * B]) for b in range(b0, b1)], [], ["EI%d" % b for b in range(b0, b1)])
        dma("s", [(T.XS[:, b0 * B:b1 * B], T.wk[:, b0 * B:b1 * B])], [], ["XS%d" % b for b in range(b0, b1)])
        dma("s", [(T.NBI[:, b0 * B:b1 * B], T.nb[:, b0 * B:b1 * B])], [], ["NBI%d" % b for b in range(b0, b1)])
    iota("PI", 0, 4, [[0, 4]], 0, 1, True)
    iota("X143", 0, 144, [[1, 144]])
    iota("XG", 0, 128, [[1, 8], [0, 16]])
    fill(T.ONES[:, :], 1.0, ["ONES"])
    w_fill(0, 4)
    iota("KO1", 0, B, [[8, B]], -192)
    iota("K1", 0, B, [[512, 8], [-256, 2], [0, 16]], 256)
    iota("J16", 0, B, [[0, 16], [1, 16]])
    iota("C16", 0, 16, [[16, 16]])
    iota("OC", 0, 16 * (N - me), [[1, N - me], [0, 16]], me + 1)
    if me:
        iota("OC", 16 * (N - me), 64, [[1, me], [0, 16]], 1)
    iota("OC", 64, 80, [[0, 16]], 0)
    join(3 if me else 2)
    iota("NDC", 0, 64, [[CAP, 4], [-16, 16]], 64)
    iota("THR", 0, 64, [[CAP, 4], [-16, 16]], 48)
    iota("HX", 0, NC, [[0, 4], [512, CAP]], 512 * (K * V + CAP * me))
    if n1:
        iota("PB", 0, n1, [[1, n1]], NC - n1)
    iota("PB", n1, NC, [[1, NC - n1]], 0)
    join(2 if n1 else 1)
    iota("BC", 8, 16, [[NC, 8]], tag="BI")
    ts(T.PI[:, 4:8], T.PI[:, 0:4], 15, None, ALU.bitwise_and, None, ["PI"], ["PJ"])
    cp(col(1), T.PI[:, 0:1], ["PI"], ["c1"])
    cp(col(0), T.PI[:, 4:5], ["PJ"], ["c0"])
    ts(col(2), col(1), col(0), 15.0, ALU.subtract, ALU.add, ["c0", "c1"], ["c2"])
    act(col(3), col(0), ACT.Identity, ["c0"], ["c3"], bias=1.0, scale=2.0)
    ts(col(4), col(0), 2.0, None, ALU.is_lt, None, ["c0"], ["c4"])
    ts(T.IDF[:, :], T.X143[:, 0:128], col(1), None, ALU.is_equal, None, ["X143", "c1"], ["IDF"])
    ts(T.D1[:, :], T.X143[:, :], col(2), None, ALU.is_equal, None, ["X143", "c2"], ["D1"])
    act(T.DW[:, :], T.D1[:, :], ACT.Identity, ["D1", "c3"], ["DW"], scale=col(3))
    act(T.DE[:, :], T.D1[:, :], ACT.Identity, ["D1", "c4"], ["DE"], scale=col(4))
    ts(col(6), col(2), -15.0, 0.0625, ALU.add, ALU.mult, ["c2"], ["c6"])
    ts(T.BOF[:, :], T.XG[:, :], col(6), None, ALU.is_equal, None, ["XG", "c6"], ["BOF"])
    for nm, src, w in [("ID", "IDF", 1.0), ("IDM", "IDF", -1.0), ("DA", "D1", -2048.0), ("DM", "D1", 4096.0),
                       ("BOM", "BOF", -1.0), ("B64", "BOF", 64.0), ("ID8", "IDF", 3840.0), ("ID10", "IDF", -16384.0),
                       ("IDB", "IDF", 65536.0), ("BO", "BOF", 1.0), ("DC", "D1", 256.0),
                       ("ID64", "IDF", -64.0), ("IDFM", "IDF", -1.0), ("BOS", "BOF", 1.0 / 512)]:
        scaled(nm, src, w)
    act(T.BO2[:, :], T.BOF[:, 0::16], ACT.Identity, ["BOF"], ["BO2"], scale=2.0)
    fill(T.ZERO[:, :], 0.0, ["ZERO"])
    pool(lambda: g.affine_select(T.LB[:, :], T.BOM[:, :], [[-1, 128]], ALU.is_ge, 0.0, 0, 1), 128, ["BOM"], ["LB"])
    pool(lambda: g.affine_select(T.LM[:, :], T.LB[:, :], [[-1, 128]], ALU.not_equal, -65.0, 0, 1), 128, ["LB"], ["LM"])
    pool(lambda: g.affine_select(T.TRI[:, :], T.B64[:, :], [[1, 128]], ALU.is_ge, 0.0, 0, -1), 128, ["B64"], ["TRI"])
    for ap, w, x, tag in [(T.AM[:, :], 1, 0.0, "AM"), (T.INI[:, :], 64, BIG, "INI"), (T.MONE[:, 16:32], 16, -96.0, "C96"),
                          (T.MONE[:, 0:16], 16, -1.0, "MONE")]:
        act(ap, T.X143[:, 0:w], ACT.Identity, ["X143"], [tag], bias=x, scale=0.0)
    ts(T.REP[:, :], T.X143[:, 0:8], 0.0, col(0), ALU.mult, ALU.add, ["X143", "c0"], ["REP"])
    ts(T.DIAG[:, :], T.J16[:, :], col(0), None, ALU.is_equal, None, ["J16", "c0"], ["DIAG"])
    act(T.MASK[:, :], T.DIAG[:, 0:NC], ACT.Identity, ["DIAG"], ["MASK"], bias=-32768.0, scale=32768.0)
    cp(T.TRH[:, :], T.TRI[:, :], ["TRI"], ["TRH"])
    cp(T.BOH[:, :], T.BO[:, :], ["BO"], ["BOH"])
    if "v" in C["rt"]:
        cp(T.IDH[:, :], T.IDM[:, :], ["IDM"], ["IDH"])
    act(T.SEG[:, :], T.J16[:, 0:NC], ACT.Sign, ["J16"], ["SEG"])
    act(T.IB[:, :], T.C16[:, :], ACT.Identity, ["C16", "c0"], ["IB"], bias=col(0))
    act(T.I17[:, :], T.IB[:, :], ACT.Identity, ["IB"], ["I17"], bias=17.0 * B)
    act(col(8), col(0), ACT.Identity, ["c0"], ["c8"], bias=-float(NC), scale=-1.0)
    act(T.DG[:, :], T.IDF[:, :], ACT.Identity, ["IDF", "c8"], ["DG"], scale=col(8))
    act(col(5), col(4), ACT.Identity, ["c4"], ["c5"], bias=1.0, scale=-1.0)
    act(col(15), col(4), ACT.Identity, ["c4"], ["c15"], bias=2.0, scale=-2.0)
    act(T.BC[:, 0:4], T.BC[:, 8:12], ACT.Identity, ["BI", "DIAG", "c15"], ["BC"], bias=col(15), scale=on(0))
    act(T.BC[:, 4:8], T.BC[:, 12:16], ACT.Identity, ["BI", "DIAG", "c5"], ["BC"], bias=col(5), scale=on(0))
    act(T.TPL[:, :], T.HX[:, :], ACT.Identity, ["HX", "DIAG"], ["TPL"], scale=on(0))
    if C["pw"]:
        iota("PW", 0, 4 * NC, [[NC, 4], [0, NC]], tag="PWa")
        iota("PW", 4 * NC, 6 * NC, [[2, 2], [0, NC]], tag="PWb")
        dma("s", [(T.PW[1::16, NC * t:NC * (t + 1)], T.PB[1::16, :]) for t in range(5)] +
            [(T.PW[2::16, NC * t:NC * (t + 1)], T.PW[3::16, 5 * NC:6 * NC]) for t in range(4)], ["PB", "PWa", "PWb"], ["PW"])
    ent_split(0)
    e_lists(0)
    crep(0)
    y_make(0, 0, 1, ["XS0"])
    tiles_n(0)
    yrep(0)
    tiles_p(0)
    nb_lists(0)
    template(0)
    ucalc(0)
    payload(0)
    y_make(B, 1, 4, ["XS1", "XS2", "XS3"])
    fill(T.W[:, K * V:WW], 1.0, ["Wf15"])
    w_fill(4, 16)
    if C["bulk"]:
        cp(T.EF[:, B:V], T.EI[:, B:V], ["EI1", "EI2", "EI3"], ["EF1"])
        act(T.EH[:, B:V], T.EF[:, B:V], ACT.Copy, ["EF1"], ["EH1"])
        for b0, b1 in ((1, 3), (3, 4)):
            ps, bank = lend("EL")
            o, w = ps[:, 0:B * (b1 - b0)], slice(b0 * B, b1 * B)
            mm([(o, T.IDF[:, :], T.EF[:, w], ["IDF", "EF1"]), (o, T.IDM[:, :], T.EH[:, w], ["IDM", "EH1"])], bank)
            act(T.EL[:, w], o, ACT.Copy, [bank], ["EL%d" % b0])
            dma("s", [(T.W[x::16, b * K * B:(b + 1) * K * B], blk(("EH", "EL")[x], b)) for b in range(b0, b1) for x in (0, 1)],
                ["EH1", "EL%d" % b0], ["W%d" % b for b in range(b0, b1)] + ["Wf%d" % x for x in range(4 * b0, 4 * b1)])
    for b in (1, 2, 3)[3 * C["bulk"]:]:
        ent_split(b)

    for t in range(R):
        b = t % 4
        ap = "AP%d" % (t % 2)
        APALL = ["%s_%d" % (ap, j) for j in range(8)] + [ap + "x"]
        nx = t + 1 < R
        step[0] = t
        tt(T.MN[:, 0:B], T.AN[:, 0:B], T.YB[:, 0:B], ALU.max, ["ANo", "YB"], ["MNo"])
        for j in range(8):
            lo = B + 2 * B * j
            move(C["nv"][t][j], T.AN[:, lo:lo + 2 * B], ind(T.CT[:, :], T.NBU[:, b * B + 32 * j:b * B + 32 * j + 32]),
                 CTALL + ["NBU%d" % b], ["AN%d" % j])
            if j >= C["wide"]:
                tt(T.MN[:, lo:lo + 2 * B], T.AN[:, lo:lo + 2 * B], T.YB[:, 0:2 * B], ALU.max, ["AN%d" % j, "YB"], ["MN%d" % j])
            elif j % 2:
                tt(T.MN[:, lo - 2 * B:lo + 2 * B], T.AN[:, lo - 2 * B:lo + 2 * B], T.YB[:, :], ALU.max,
                   ["AN%d" % (j - 1), "AN%d" % j, "YB"], ["MN%d" % j, "MN%d" % (j - 1)])
            if j % 2 == 1:
                q = j // 2
                bank = BANKS[q % 2]
                c0, c1 = (0 if q == 0 else B + 4 * B * q), B + 4 * B * (q + 1)
                w = (c1 - c0) // 16
                out, o = T[bank][:, 0:w], T[bank][:, w - 64:w]
                mm([(out, sel("DA", r), T.AN[:, c0 + r:c1:16], ["DA", "AN%d" % (j - 1), "AN%d" % j] + ["ANo"] * (q == 0))
                    for r in range(16)] +
                   [(o, T.ID[:, :], T.KO1[:, 64 * q:64 * q + 64], ["ID", "KO1"]),
                    (o, T.ID[:, :], T.KO2[:, b * B + 64 * q:b * B + 64 * q + 64], ["KO2%d" % b])], bank, True, False, name="a%d" % q)
                mm([(out, sel("DM", r), T.MN[:, c0 + r:c1:16], ["DM", "MN%d" % (j - 1), "MN%d" % j] + ["MNo"] * (q == 0))
                    for r in range(16)], bank, False, True, name="m%d" % q)
                if q == 0:
                    if C["th"][t] == "v":
                        ts(T.INI[:, 0:16], T.K0[:, 0:16], T.AM[:, :], None, ALU.add, None, ["K0", "AM"], ["INI"])
                    else:
                        act(T.INI[:, 0:16], T.K0[:, 0:16], ACT.Identity, ["K0", "AM"], ["INI"], bias=T.AM[:, :])
                    tt(T.ACC[:, :], T.K0[:, 16:80], T.INI[:, :], ALU.min, ["K0", "INI"], ["ACC"])
                else:
                    tt(T.ACC[:, :], T[bank][:, 0:64], T.ACC[:, :], ALU.min, [bank, "ACC"], ["ACC"])
        if nx:
            send_free(t)
        tt(T.A32[:, :], T.ACC[:, 0:32], T.ACC[:, 32:64], ALU.min, ["ACC"], ["A32"])
        tt(T.KG[:, :], T.A32[:, 0:16], T.A32[:, 16:32], ALU.min, ["A32"], ["KG"])
        if C["key"][t] == "k":
            tt(T.MONE[:, 32:48], T.KG[:, :], T.INI[:, 0:16], ALU.is_ge, ["KG", "INI"], ["KEY"])
        ts(T.CODE[:, :], T.KG[:, :], 7, None, ALU.bitwise_and, None, ["KG"], ["CODE"])
        tt(T.H[:, :], ind(T.CODE[:, :], T.REP[:, 0:5]), T.OC[:, :], ALU.is_equal, ["CODE", "REP", "OC"], ["H"])
        scan(T.S[:, :], T.SEG[:, 0:80], T.H[:, :], ALU.mult, ALU.add, ["SEG", "H"], ["S"])
        o = T.K0[:, 0:64]
        mm([(o, T.ID[:, :], T.NDC[:, :], ["ID", "NDC"]), (o, T.LM[:, :], T.H[:, 0:64], ["LM", "H"]),
            (o, T.BO[:, :], T.S[:, 0:64], ["BO", "S"])], "K0", name="rank")
        ts(T.L1[:, :], T.KG[:, :], 3, 255, ALU.logical_shift_right, ALU.bitwise_and, ["KG"], ["L1"])
        cp(T.L1U[:, :], T.L1[:, :], ["L1"], ["L1U"])
        tt(T.VV[:, :], o, T.THR[:, :], ALU.is_lt, ["K0", "THR"], ["VV"])
        tt(T.Q[:, :], o, T.VV[:, :], ALU.mult, ["K0", "VV"], ["Q"])
        o = T.KB1[:, 0:16]
        mm([(o, T.ID[:, :], T.C16[:, :], ["ID", "C16"]), (o, T.DG[:, :], T.MONE[:, 0:16], ["DG", "MONE"])] +
           [(o, T.DG[:, :], T.VV[:, 16 * d:16 * d + 16], ["VV"]) for d in range(4)], "KB1", True, False, name="pv")
        mm([(o, T.ID[:, :], T.Q[:, 16 * d:16 * d + 16], ["Q"]) for d in range(4)], "KB1", False, True, name="pq")
        tt(T.X[:, :], ind(blk("TC", b), T.L1U[:, :]), T.DIAG[:, :], ALU.mult, ["TC%d" % b, "L1U", "DIAG"], ["X"])
        cp(T.PY[:, :], o, ["KB1"], ["PY"])
        tt(ind(T["XB%d" % t][:, 144:XW_], T.PY[:, :]), T.X[:, :], blk("YF", t), ALU.add, ["PY", "X", "YF%d" % t], ["XB%d" % t])
        send_x(t)
        if nx:
            acount()
            if t in (1, 2):
                y_make((t - 1) * B, t + 3, t + 4, ["XS%d" % (t - 1)])
            yrep(t + 1)
            tiles_n(t + 1)
            template(t + 1)
            if t < 3:
                nb_lists(t + 1)
            ucalc(t + 1)
        for j in range(8):
            entry_piece(t, j)
        if nx:
            crep(t + 1)
        if C["rt"][t] == "a":
            act(T.RT[:, :], T.HB[:, 0:B], ACT.Relu, ["HB"], ["RT"], bias=2047.0, scale=-1.0)
            for h in (0, 128):
                mm([(T.HB[:, B + h:B + h + 128], T.RT[:, h:h + 128], T.IDF[:, :], ["RT", "IDF"])], "HB", name="back")
        else:
            ts(T.RH[:, :], T.HB[:, 0:B], 2047.0, 2047.0, ALU.min, ALU.subtract, ["HB"], ["RT"])
            mm([(T.HB[:, B:B + 128], T.RH[:, 0:128], T.IDH[:, :], ["RT", "IDH"])], "HB", name="back")
            mm([(T.HB[:, B + 128:2 * B], T.RH[:, 128:B], T.IDH[:, :], ["RT", "IDH"])], "HB", name="back")
        gg, bo, tri = ("GH", "BOH", "TRH") if nx else ("G", "BOF", "TRI")
        if t == 0:
            cp(T[gg][:, :], blk("HB", 1), ["HB"], ["G"])
        else:
            tt(T[gg][:, :], blk("HB", 1), T.NN[:, :], ALU.mult, ["HB", "NN"], ["G"])
        mm([(blk("TB", 0), T[bo][:, :], T[gg][:, :], [bo, "G"])], "TB", name="all")
        mm([(blk("HB", 0), T[tri][:, :], T[gg][:, :], [tri, "G"])], "HB", name="run")
        tt(T.UT[:, :], blk("TB", 0), blk("U", t % 2), ALU.mult, ["TB", "U%d" % (t % 2)], ["UT"])
        tt(T.NO[:, :], blk("HB", 0), T.UT[:, :], ALU.is_le, ["HB", "UT"], ["NO"])
        o = T.TB[:, B:B + 16]
        mm([(o, T.ID[:, :], T.IB[:, :], ["ID", "IB"])] + [(o, sel("DC", r), T.NO[:, r:B:16], ["DC", "NO"]) for r in range(16)],
           "TB", True, False, name="cnt")
        if C["key"][t] == "k":
            mm([(o, T.IDB[:, :], T.MONE[:, 32:48], ["IDB", "KEY"])], "TB", False, True, name="stay")
        else:
            mm([(o, T.IDB[:, :], T.H[:, 64:80], ["IDB", "H"])], "TB", False, True, name="stay")
        tt(T.IX[:, :], o, T.I17[:, :], ALU.min, ["TB", "I17"], ["IX"])
        cp(T.IXU[:, :], T.IX[:, :], ["IX"], ["IXU"])
        new = ind(T[ap][:, :], T.IXU[:, :])
        dv, dt_ = (blk("XS", b), ["DV", "XS%d" % b]) if C["dv"][t] == "d" else (T.DV[:, :], ["DV"])
        if C["dv"][t] == "m":
            tt(T.DV[:, :], new, blk("CM", t % 2), ALU.max, APALL + ["IXU", "CM%d" % (t % 2)], ["DV"])
            tt(cown(t), T.DV[:, :], blk("YB", 2 + t % 2), ALU.min, ["DV", "YB"], ["CTo%d" % b])
        else:
            if C["dv"][t] != "a":
                tt(dv, new, cown(t), ALU.subtract, APALL + ["IXU", "CTo%d" % b], dt_)
            else:
                act(blk("XS", b), new, ACT.Copy, APALL + ["IXU"], ["XS%d" % b])
                tt(T.DV[:, :], blk("XS", b), blk("CB", 2 * (t % 2)), ALU.subtract, ["XS%d" % b, "CB"], ["DV"])
            ts(T.SG[:, :], dv, -1.0, 1.0, ALU.max, ALU.min, dt_, ["SG"])
            tt(cown(t), T.SG[:, :], blk("CB", 2 * (t % 2)), ALU.add, ["SG", "CB"], ["CTo%d" % b])
        if nx:
            send_c(b * B, B, t, ["CTo%d" % b, "FR"])
        if C["dv"][t] in "vm":
            act(blk("XS", b), new, ACT.Copy, APALL + ["IXU"], ["XS%d" % b])
        if C["dv"][t] == "d":
            dma("g", [(blk("XS", b), blk(ap, 16))], [ap + "x"], ["XS%d" % b], True)
        if not nx:
            dma("a", [(T.yx[:, b * B:(b + 1) * B], blk("XS", b))], ["XS%d" % b], [])
            dma("s", [(T.yc[:, b * B:(b + 1) * B], cown(t))], ["CTo%d" % b], [])
        arrive(t)
        arrive_w(t)
        if not nx:
            dma("s", [(T.ye[:, :], T.WF[0::16, 0:K * V])], ["WFe"], [])
            dma("g", [(T.yn[:, :], T.WF[2::16, 0:K * V])], ["WFn"], [])
            dma("s", [(T.yz[:, 5 * NC:6 * NC], T.PL[:, 5 * NC:6 * NC])], ["PL"], [])
            break
        e_lists(t + 1)
        n_tile(t + 1)
        payload(t + 1)
        tiles_p(t + 1)
        if t == 4:
            w = slice(0, K * V)
            dma("g", [(T.WF[0::16, w], T.W[0::16, w])], WALL, ["WFe"])
            dma("g", [(T.WF[2::16, w], T.W[2::16, w])], WALL, ["WFn"])
            dma("g", [(T.WF[0::16, w], T.W[1::16, w])], WALL, ["WFe"], True)
            dma("s", [(T.yz[:, 0:5 * NC], T.PL[:, 0:5 * NC]), (T.yz[:, 6 * NC:ZP], T.PL[:, 6 * NC:ZP])], ["PL"], [])
        if t >= 2:
            dma("s", [(T.yc[:, b * B:(b + 1) * B], cown(t)), (T.yx[:, b * B:(b + 1) * B], blk("XS", b))],
                ["CTo%d" % b, "XS%d" % b], [])
    return ops
